import numpy as np
import ml_dtypes


def mxq(x, axis, fmt="e4m3"):
    dtype, down = {"e4m3": (ml_dtypes.float8_e4m3fn, 7), "e5m2": (ml_dtypes.float8_e5m2, 14)}[fmt]
    v = np.moveaxis(np.asarray(x, np.float32).astype(ml_dtypes.bfloat16).astype(np.float64), axis, -1)
    blocks = v.reshape(v.shape[:-1] + (-1, 32))
    amax = np.abs(blocks).max(-1, keepdims=True)
    byte = np.maximum(np.where(amax > 0, np.frexp(amax)[1] - 1 + 127, 0) - down, 1)
    scale = np.exp2(byte - 127.0)
    codes = (blocks / scale).astype(np.float32).astype(dtype).astype(np.float64)
    return np.moveaxis((codes * scale).reshape(v.shape), -1, axis)


WIDE = False


def mx_kscale(k):
    if not WIDE:
        return np.ones(k)
    levels = np.array([10, -10, 5, -5, 0])
    if k % 512:
        return np.exp2(np.random.permutation(np.resize(levels, k // 32))).repeat(32)
    a = np.empty((k // 512, 16))
    for p in range(k // 512):
        a[p, :8] = np.random.permutation(np.resize(levels, 8))
        for g in range(8):
            far = levels[np.abs(levels - a[p, g]) >= 10]
            a[p, g + 8] = far[np.random.randint(len(far))]
    return np.exp2(a.ravel()).repeat(32)


def f64(x):
    return np.asarray(x).astype(np.float64)


def striped(idx):
    return np.tile(idx.reshape(-1, 16).T, (8, 1)).astype(np.uint16)


def unstriped(offs):
    return offs[:16].T.reshape(-1).astype(np.int64)


E2M1 = np.array([0.0, 0.5, 1.0, 1.5, 2.0, 3.0, 4.0, 6.0, -0.0, -0.5, -1.0, -1.5, -2.0, -3.0, -4.0, -6.0])


def pack_weight(w, fmt):
    k, n = w.shape
    w = f64(np.asarray(w, np.float32).astype(ml_dtypes.bfloat16)).reshape(k // 32, 32, n)
    amax = np.abs(w).max(1)
    if fmt == "e4m3":
        byte = np.frexp(amax)[1] - 1 + 127 - 7
    else:
        mant, ex = np.frexp(amax / 6.0)
        byte = np.where(mant > 0.5, ex, ex - 1) + 127
    byte = np.clip(np.where(amax > 0, byte, 1), 1, 254)
    scaled = (w * np.exp2(127.0 - byte)[:, None, :]).reshape(k, n).astype(np.float32)
    by_word = np.ascontiguousarray(scaled.reshape(k // 512, 128, 4, n).transpose(0, 1, 3, 2))
    if fmt == "e4m3":
        words = by_word.astype(ml_dtypes.float8_e4m3fn).view(np.uint8)
    else:
        c = by_word.astype(ml_dtypes.float4_e2m1fn).view(np.uint8) & 0xF
        words = (c[..., 0::2] | (c[..., 1::2] << 4)).reshape(k // 512, 128, 2 * n)
    return np.ascontiguousarray(words), np.ascontiguousarray(byte.astype(np.uint8).reshape(k // 512, 16, n))


def unpack_weight(words, scales, fmt):
    g, _, n = scales.shape
    words = np.ascontiguousarray(words).reshape(g, 128, n, -1)
    if fmt == "e4m3":
        vals = words.view(ml_dtypes.float8_e4m3fn).astype(np.float64)
    else:
        nib = np.empty((g, 128, n, 4), np.uint8)
        nib[..., 0::2] = words & 0xF
        nib[..., 1::2] = words >> 4
        vals = E2M1[nib]
    vals = vals * np.repeat(np.exp2(scales.astype(np.float64) - 127.0), 8, axis=1)[..., None]
    return vals.transpose(0, 1, 3, 2).reshape(g * 512, n)


def gelu(v):
    return 0.5 * v * (1.0 + np.tanh(np.sqrt(2.0 / np.pi) * (v + 0.044715 * v**3)))


K, H, N, T, T2, S = 1024, 512, 512, 4096, 4096, 1024

def setup_inputs():
    n = np.random.standard_normal
    s = mx_kscale(K)[:, None]
    u = mx_kscale(H)[:, None]
    tab_words, tab_scales = pack_weight(n((K, T)) * s, "e4m3")
    wg_words, wg_scales = pack_weight(n((K, H)) / np.sqrt(K) / s, "e2m1")
    wr_words, wr_scales = pack_weight(0.7 * n((K, N)) / np.sqrt(K) / s, "e4m3")
    return {
        "tab_words": tab_words, "tab_scales": tab_scales,
        "offs": striped(np.random.permutation(T)[:S]),
        "wf": (n((K, H)) / np.sqrt(K) / s).astype(np.float32),
        "wg_words": wg_words, "wg_scales": wg_scales,
        "gain": (np.exp(0.2 * n(H)) * u[:, 0]).astype(np.float32),
        "wo": (2.0 * n((H, N)) / np.sqrt(H) / u).astype(np.float32),
        "wr_words": wr_words, "wr_scales": wr_scales,
        "wgo": np.exp(0.3 * n((128, S))).astype(np.float32),
        "offs2": striped(np.random.permutation(T2)[:S]),
    }

def reference(tab_words, tab_scales, offs, wf, wg_words, wg_scales, gain, wo, wr_words, wr_scales, wgo, offs2):
    v = unpack_weight(tab_words, tab_scales, "e4m3")[:, unstriped(offs)]
    wg = unpack_weight(wg_words, wg_scales, "e2m1")
    wr = unpack_weight(wr_words, wr_scales, "e4m3")
    a = mxq(f64(wf), 0, "e4m3").T @ v
    b = wg.T @ v
    h = f64(gain)[:, None] * np.tanh(a) * (1.0 / (1.0 + np.exp(-b)))
    hq = mxq(h, 0, "e4m3")
    y = mxq(f64(wo), 0, "e4m3").T @ hq + wr.T @ v
    out = np.zeros((N, T2))
    out[:, unstriped(offs2)] = np.tile(f64(wgo), (N // 128, 1)) * y
    return out

@@ -1,0 +1,185 @@
+from contextlib import ExitStack
+
+import concourse.mybir as mybir
+
+K, H, N, T, S = 1024, 512, 512, 4096, 1024
+FLOPS = 2 * S * (2 * K * H + H * N + K * N)
+
+F32 = mybir.dt.float32
+BF16 = mybir.dt.bfloat16
+I32 = mybir.dt.int32
+U32 = mybir.dt.uint32
+U16 = mybir.dt.uint16
+U8 = mybir.dt.uint8
+FP8X4 = mybir.dt.float8_e4m3fn_x4
+FP4X4 = mybir.dt.float4_e2m1fn_x4
+ACT = mybir.ActivationFunctionType
+MULT = mybir.AluOpType.mult
+
+P = 128
+PASSES = K // 512
+HALF = S // 2
+CHUNK = 128
+
+
+def tile_list_wavenet_gate_store_kernel(tc, tab_words, tab_scales, offs, wf, wg_words, wg_scales, gain, wo,
+                                                 wr_words, wr_scales, wgo, offs2, out):
+    nc = tc.nc
+    with ExitStack() as ctx:
+        lists = ctx.enter_context(tc.tile_pool(name="lists", bufs=1))
+        keep = ctx.enter_context(tc.tile_pool(name="keep", bufs=1))
+        stage = ctx.enter_context(tc.tile_pool(name="stage", bufs=1))
+        psum = ctx.enter_context(tc.psum_pool(name="psum", bufs=1))
+        bank = [psum.tile([P, 512], F32, name="bank%d" % b) for b in range(8)]
+
+        idx = lists.tile([P, S // 16], U16, name="idx")
+        nc.sync.dma_start(idx[:], offs)
+        tsc = keep.tile([P, T // 4], I32, name="tsc")
+        nc.sync.dma_start(tsc[0:32, :], tab_scales.rearrange("a q t -> (a q) t").bitcast(I32))
+        wgs_raw = keep.tile([P, H], U8, name="wgs_raw")
+        nc.sync.dma_start(wgs_raw[0:32, :].bitcast(I32), wg_scales.rearrange("a q c -> (a q) c").bitcast(I32))
+        rows16 = stage.tile([P, PASSES, S + H + N], U8, name="rows16", tag="slot_a")
+        nc.sync.dma_start(rows16[0:32, 0, S + H:].bitcast(I32), wr_scales.rearrange("a q c -> (a q) c").bitcast(I32))
+        wg_raw = keep.tile([P, PASSES, H // 2], I32, name="wg_raw")
+        nc.sync.dma_start(wg_raw[:], wg_words.bitcast(I32).rearrange("a p c -> p a c"))
+        tab = [stage.tile([P, T], I32, name="tab%d" % a, tag="tab%d" % a, align_bytes=64) for a in range(PASSES)]
+        nc.sync.dma_start(tab[0][:], tab_words[0].rearrange("p t i -> p (t i)").bitcast(I32))
+        idx2 = lists.tile([P, S // 16], U16, name="idx2")
+        nc.sync.dma_start(idx2[:], offs2)
+        gain_sb = keep.tile([P, 4], F32, name="gain_sb")
+        nc.sync.dma_start(gain_sb[:], gain.rearrange("(p t) -> p t", t=4))
+        nc.sync.dma_start(tab[1][:], tab_words[1].rearrange("p t i -> p (t i)").bitcast(I32))
+        wf_raw = [stage.tile([P, 4, H], F32, name="wf_raw%d" % a, tag="wf%d" % a, align_bytes=64) for a in range(PASSES)]
+        for a in range(PASSES):
+            nc.sync.dma_start(wf_raw[a][:], wf[512 * a: 512 * (a + 1), :].rearrange("(p j) c -> p j c", j=4))
+
+        nc.vector.memset(tsc[32:64, :], 0)
+        nc.vector.memset(tsc[64:128, :], 0)
+        nc.vector.memset(wgs_raw[32:64, :].bitcast(I32), 0)
+        nc.vector.memset(wgs_raw[64:128, :].bitcast(I32), 0)
+        planes = keep.tile([P, PASSES, S + H + N], U8, name="planes", align_bytes=64)
+        nc.vector.memset(planes[:].bitcast(I32), 0)
+        cache = []
+
+        def new_cache(pool, tag):
+            window = pool.tile([P, T], F32, name="cache%d" % len(cache), tag=tag)
+            cache.append(window)
+            for c in range(4):
+                nc.gpsimd.memset(window[:, 1024 * c: 1024 * (c + 1)], 0.0)
+
+        new_cache(keep, "cache0")
+        new_cache(keep, "cache1")
+
+        warm = keep.tile([P, 1], F32, name="warm")
+        nc.scalar.activation(warm[:], gain_sb[:, 0:1], ACT.Sigmoid)
+
+        picked = keep.tile([P, S], U8, name="picked")
+        nc.vector.tensor_copy(picked[:], tsc[:].bitcast(U8).indirect(idx[:]))
+        nc.vector.tensor_copy(rows16[:, 0, S: S + H].rearrange("p (t m) -> p t m", t=4),
+                              wgs_raw[:].rearrange("p (m t) -> p t m", t=4))
+        nc.vector.tensor_copy(rows16[:, 0, 0:S].bitcast(I32), picked[:].bitcast(I32))
+        nc.scalar.dma_start(rows16[0:16, 1, :].bitcast(I32), rows16[16:32, 0, :].bitcast(I32))
+        for q in range(4):
+            nc.scalar.dma_start(planes[32 * q: 32 * q + 4].bitcast(I32), rows16[4 * q: 4 * q + 4].bitcast(I32))
+        wg_codes = keep.tile([P, PASSES, 2 * H], U8, name="wg_codes", align_bytes=64)
+        nc.vector.tensor_copy(wg_codes[:].bitcast(U16).rearrange("p a (t m) -> p a t m", t=4),
+                              wg_raw[:].bitcast(U16).rearrange("p a (m t) -> p a t m", t=4))
+        v_codes = [keep.tile([P, S], U32, name="v_codes%d" % a, align_bytes=64) for a in range(PASSES)]
+        nc.vector.tensor_copy(v_codes[0][:], tab[0][:].bitcast(U32).indirect(idx[:]))
+        for h in range(2):
+            nc.vector.tensor_copy(v_codes[1][:, HALF * h: HALF * (h + 1)],
+                                  tab[1][:].bitcast(U32).indirect(idx[:, 32 * h: 32 * (h + 1)]))
+
+        wo_raw = stage.tile([P, 4, N], F32, name="wo_raw", tag="slot_a")
+        nc.sync.dma_start(wo_raw[:], wo.rearrange("(p j) c -> p j c", j=4))
+
+        wf_codes = keep.tile([P, PASSES, H], U32, name="wf_codes", align_bytes=64)
+        wf_sc = keep.tile([P, PASSES, H], U8, name="wf_sc", align_bytes=64)
+        q_in = stage.tile([P, 8, 512], BF16, name="q_in", tag="tab1", align_bytes=64)
+        wo_codes = keep.tile([P, N], U32, name="wo_codes", align_bytes=64)
+        wo_sc = keep.tile([P, N], U8, name="wo_sc", align_bytes=64)
+        gated = [stage.tile([P, 4, HALF], F32, name="gated%d" % h, tag="gated%d" % h) for h in range(2)]
+        h_codes = keep.tile([P, S], U32, name="h_codes", align_bytes=64)
+        h_sc = keep.tile([P, S], U8, name="h_sc", align_bytes=64)
+        sig = keep.tile([P, 2, HALF], F32, name="sig")
+        th = keep.tile([P, 4, 4 * CHUNK], F32, name="th")
+        y_sb = keep.tile([P, 4, HALF], F32, name="y_sb")
+
+        def gate(h, banks):
+            cols = slice(HALF * h, HALF * (h + 1))
+            for t in range(4):
+                b_ps = bank[banks[t]]
+                for a in range(PASSES):
+                    nc.tensor.matmul_mx(b_ps[:], wg_codes[:, a, 256 * t: 256 * (t + 1)].bitcast(FP4X4),
+                                        planes[:, a, S + P * t: S + P * (t + 1)], v_codes[a][:, cols].bitcast(FP8X4),
+                                        planes[:, a, cols], start=(a == 0), stop=(a == PASSES - 1))
+                nc.scalar.activation(sig[:, t % 2, :], b_ps[:], ACT.Sigmoid)
+                nc.scalar.activation(gated[h][:, t, :], sig[:, t % 2, :], ACT.Copy, scale=gain_sb[:, t: t + 1])
+
+        def quantise_wf(a):
+            dst = q_in[:, 4 * a: 4 * a + 4, :]
+            nc.vector.tensor_copy(dst.rearrange("p t (m j) -> p m t j", j=4),
+                                  wf_raw[a][:].rearrange("p j (m t) -> p m t j", t=4))
+            nc.vector.quantize_mx(wf_codes[:, a, :].bitcast(FP8X4), wf_sc[:, a, :], dst.rearrange("p t c -> p (t c)"))
+
+        def quantise_wo(n, slot, copy):
+            dst = q_in[:, slot, :]
+            src = wo_raw[:, :, P * n: P * (n + 1)]
+            copy(dst.rearrange("p (c i j) -> p c j i", i=4, j=4), src.rearrange("p j (c i) -> p c j i", i=4))
+            nc.vector.quantize_mx(wo_codes[:, P * n: P * (n + 1)].bitcast(FP8X4), wo_sc[:, P * n: P * (n + 1)], dst)
+
+        def hidden(h, banks, slots):
+            for c in range(HALF // CHUNK):
+                j0 = HALF * h + CHUNK * c
+                cols = slice(j0, j0 + CHUNK)
+                a_ps = bank[banks[c]]
+                for t in range(4):
+                    for a in (1, 0):
+                        nc.tensor.matmul_mx(a_ps[:, CHUNK * t: CHUNK * (t + 1)], wf_codes[:, a, P * t: P * (t + 1)].bitcast(FP8X4),
+                                            wf_sc[:, a, P * t: P * (t + 1)], v_codes[a][:, cols].bitcast(FP8X4),
+                                            planes[:, a, cols], start=(a == 1), stop=(a == 0))
+                nc.scalar.activation(th[:, c, :], a_ps[:], ACT.Tanh)
+                h_bf = q_in[:, slots[c], :]
+                nc.vector.tensor_tensor(h_bf.rearrange("p (c i t) -> p c t i", i=4, t=4),
+                                        th[:, c, :].rearrange("p (t c i) -> p c t i", t=4, i=4),
+                                        gated[h][:, :, CHUNK * c: CHUNK * (c + 1)].rearrange("p t (c i) -> p c t i", i=4), MULT)
+                nc.vector.quantize_mx(h_codes[:, cols].bitcast(FP8X4), h_sc[:, cols], h_bf)
+
+        def place(n, h, step):
+            cols = slice(HALF * h, HALF * (h + 1))
+            rows = slice(P * n, P * (n + 1))
+            y_ps = bank[4 + step % 3]
+            for a in range(PASSES):
+                nc.tensor.matmul_mx(y_ps[:], wr_codes[:, a, rows].bitcast(FP8X4), planes[:, a, S + H + P * n: S + H + P * (n + 1)],
+                                    v_codes[a][:, cols].bitcast(FP8X4), planes[:, a, cols], start=(a == 0), stop=False)
+            nc.tensor.matmul_mx(y_ps[:], wo_codes[:, rows].bitcast(FP8X4), wo_sc[:, rows],
+                                h_codes[:, cols].bitcast(FP8X4), h_sc[:, cols], start=False, stop=True)
+            nc.scalar.copy(y_sb[:, step % 4, :], y_ps[:])
+            nc.vector.tensor_tensor(cache[n][:].indirect(idx2[:, 32 * h: 32 * (h + 1)]), y_sb[:, step % 4, :], wgo_sb[:, cols], MULT)
+            if h == 1:
+                nc.sync.dma_start(out[rows, :], cache[n][:])
+
+        gate(0, (0, 1, 2, 3))
+        quantise_wf(0)
+        wr_codes = stage.tile([P, PASSES, N], I32, name="wr_codes", tag="wf0", align_bytes=64)
+        nc.sync.dma_start(wr_codes[:], wr_words.rearrange("a p c i -> a p (c i)").bitcast(I32).rearrange("a p c -> p a c"))
+        quantise_wf(1)
+        wgo_sb = stage.tile([P, S], F32, name="wgo_sb", tag="wf1", align_bytes=64)
+        nc.sync.dma_start(wgo_sb[:], wgo)
+        quantise_wo(0, 4, nc.vector.tensor_copy)
+        hidden(0, (4, 5, 6, 7), (5, 6, 7, 0))
+        new_cache(stage, "gated0")
+        place(0, 0, 0)
+        quantise_wo(1, 7, nc.scalar.copy)
+        place(1, 0, 1)
+        gate(1, (7, 7, 7, 7))
+        hidden(1, (0, 1, 2, 3), (1, 2, 3, 4))
+        new_cache(stage, "gated1")
+        place(0, 1, 2)
+        quantise_wo(2, 0, nc.scalar.copy)
+        quantise_wo(3, 7, nc.scalar.copy)
+        place(2, 0, 3)
+        place(1, 1, 4)
+        place(2, 1, 5)
+        place(3, 0, 6)
+        place(3, 1, 7)

@@ -34,7 +34,7 @@ def tile_list_wavenet_gate_store_kernel(tc, tab_words, tab_scales, offs, wf, wg_
 
         idx = lists.tile([P, S // 16], U16, name="idx")
         nc.sync.dma_start(idx[:], offs)
-        tsc = keep.tile([P, T // 4], I32, name="tsc")
+        tsc = stage.tile([P, T // 4], I32, name="tsc", tag="tsc", align_bytes=64)
         nc.sync.dma_start(tsc[0:32, :], tab_scales.rearrange("a q t -> (a q) t").bitcast(I32))
         wgs_raw = keep.tile([P, H], U8, name="wgs_raw")
         nc.sync.dma_start(wgs_raw[0:32, :].bitcast(I32), wg_scales.rearrange("a q c -> (a q) c").bitcast(I32))
@@ -62,13 +62,12 @@ def tile_list_wavenet_gate_store_kernel(tc, tab_words, tab_scales, offs, wf, wg_
         cache = []
 
         def new_cache(pool, tag):
-            window = pool.tile([P, T], F32, name="cache%d" % len(cache), tag=tag)
+            window = pool.tile([P, T], F32, name="cache%d" % len(cache), tag=tag, align_bytes=64)
             cache.append(window)
             for c in range(4):
-                nc.gpsimd.memset(window[:, 1024 * c: 1024 * (c + 1)], 0.0)
+                nc.vector.memset(window[:, 1024 * c: 1024 * (c + 1)].bitcast(I32), 0)
 
         new_cache(keep, "cache0")
-        new_cache(keep, "cache1")
 
         warm = keep.tile([P, 1], F32, name="warm")
         nc.scalar.activation(warm[:], gain_sb[:, 0:1], ACT.Sigmoid)
@@ -84,6 +83,7 @@ def tile_list_wavenet_gate_store_kernel(tc, tab_words, tab_scales, offs, wf, wg_
         wg_codes = keep.tile([P, PASSES, 2 * H], U8, name="wg_codes", align_bytes=64)
         nc.vector.tensor_copy(wg_codes[:].bitcast(U16).rearrange("p a (t m) -> p a t m", t=4),
                               wg_raw[:].bitcast(U16).rearrange("p a (m t) -> p a t m", t=4))
+        new_cache(stage, "tsc")
         v_codes = [keep.tile([P, S], U32, name="v_codes%d" % a, align_bytes=64) for a in range(PASSES)]
         nc.vector.tensor_copy(v_codes[0][:], tab[0][:].bitcast(U32).indirect(idx[:]))
         for h in range(2):
@@ -98,7 +98,7 @@ def tile_list_wavenet_gate_store_kernel(tc, tab_words, tab_scales, offs, wf, wg_
         q_in = stage.tile([P, 8, 512], BF16, name="q_in", tag="tab1", align_bytes=64)
         wo_codes = keep.tile([P, N], U32, name="wo_codes", align_bytes=64)
         wo_sc = keep.tile([P, N], U8, name="wo_sc", align_bytes=64)
-        gated = [stage.tile([P, 4, HALF], F32, name="gated%d" % h, tag="gated%d" % h) for h in range(2)]
+        gated = [keep.tile([P, 4, HALF], F32, name="gated%d" % h) for h in range(2)]
         h_codes = keep.tile([P, S], U32, name="h_codes", align_bytes=64)
         h_sc = keep.tile([P, S], U8, name="h_sc", align_bytes=64)
         sig = keep.tile([P, 2, HALF], F32, name="sig")
@@ -155,9 +155,9 @@ def tile_list_wavenet_gate_store_kernel(tc, tab_words, tab_scales, offs, wf, wg_
             nc.tensor.matmul_mx(y_ps[:], wo_codes[:, rows].bitcast(FP8X4), wo_sc[:, rows],
                                 h_codes[:, cols].bitcast(FP8X4), h_sc[:, cols], start=False, stop=True)
             nc.scalar.copy(y_sb[:, step % 4, :], y_ps[:])
-            nc.vector.tensor_tensor(cache[n][:].indirect(idx2[:, 32 * h: 32 * (h + 1)]), y_sb[:, step % 4, :], wgo_sb[:, cols], MULT)
+            nc.vector.tensor_tensor(cache[n % 3][:].indirect(idx2[:, 32 * h: 32 * (h + 1)]), y_sb[:, step % 4, :], wgo_sb[:, cols], MULT)
             if h == 1:
-                nc.sync.dma_start(out[rows, :], cache[n][:])
+                nc.sync.dma_start(out[rows, :], cache[n % 3][:])
 
         gate(0, (0, 1, 2, 3))
         quantise_wf(0)
@@ -168,18 +168,17 @@ def tile_list_wavenet_gate_store_kernel(tc, tab_words, tab_scales, offs, wf, wg_
         nc.sync.dma_start(wgo_sb[:], wgo)
         quantise_wo(0, 4, nc.vector.tensor_copy)
         hidden(0, (4, 5, 6, 7), (5, 6, 7, 0))
-        new_cache(stage, "gated0")
         place(0, 0, 0)
+        new_cache(stage, "tab0")
         quantise_wo(1, 7, nc.scalar.copy)
         place(1, 0, 1)
         gate(1, (7, 7, 7, 7))
         hidden(1, (0, 1, 2, 3), (1, 2, 3, 4))
-        new_cache(stage, "gated1")
         place(0, 1, 2)
         quantise_wo(2, 0, nc.scalar.copy)
         quantise_wo(3, 7, nc.scalar.copy)
-        place(2, 0, 3)
-        place(1, 1, 4)
+        place(1, 1, 3)
+        place(2, 0, 4)
         place(2, 1, 5)
         place(3, 0, 6)
         place(3, 1, 7)

@@ -20,6 +20,9 @@ P = 128
 PASSES = K // 512
 HALF = S // 2
 CHUNK = 128
+CHUNKS = HALF // CHUNK
+ROW0 = 96
+Y_BANK = 4
 
 
 def tile_list_wavenet_gate_store_kernel(tc, tab_words, tab_scales, offs, wf, wg_words, wg_scales, gain, wo,
@@ -29,156 +32,157 @@ def tile_list_wavenet_gate_store_kernel(tc, tab_words, tab_scales, offs, wf, wg_
         lists = ctx.enter_context(tc.tile_pool(name="lists", bufs=1))
         keep = ctx.enter_context(tc.tile_pool(name="keep", bufs=1))
         stage = ctx.enter_context(tc.tile_pool(name="stage", bufs=1))
+        late = ctx.enter_context(tc.tile_pool(name="late", bufs=1))
         psum = ctx.enter_context(tc.psum_pool(name="psum", bufs=1))
         bank = [psum.tile([P, 512], F32, name="bank%d" % b) for b in range(8)]
 
         idx = lists.tile([P, S // 16], U16, name="idx")
         nc.sync.dma_start(idx[:], offs)
-        tsc = stage.tile([P, T // 4], I32, name="tsc", tag="tsc", align_bytes=64)
-        nc.sync.dma_start(tsc[0:32, :], tab_scales.rearrange("a q t -> (a q) t").bitcast(I32))
+        tsc = stage.tile([P, T // 4], I32, name="tsc", tag="first", align_bytes=64)
+        nc.sync.dma_start(tsc[ROW0:P, :], tab_scales.rearrange("a q t -> (a q) t").bitcast(I32))
         wgs_raw = keep.tile([P, H], U8, name="wgs_raw")
-        nc.sync.dma_start(wgs_raw[0:32, :].bitcast(I32), wg_scales.rearrange("a q c -> (a q) c").bitcast(I32))
-        rows16 = stage.tile([P, PASSES, S + H + N], U8, name="rows16", tag="slot_a")
-        nc.sync.dma_start(rows16[0:32, 0, S + H:].bitcast(I32), wr_scales.rearrange("a q c -> (a q) c").bitcast(I32))
-        wg_raw = keep.tile([P, PASSES, H // 2], I32, name="wg_raw")
+        nc.sync.dma_start(wgs_raw[ROW0:P, :].bitcast(I32), wg_scales.rearrange("a q c -> (a q) c").bitcast(I32))
+        rows = late.tile([P, PASSES, S + H + N], U8, name="rows", offset=6144)
+        nc.sync.dma_start(rows[ROW0:P, 0, S + H:].bitcast(I32), wr_scales.rearrange("a q c -> (a q) c").bitcast(I32))
+        wg_raw = stage.tile([P, PASSES, H // 2], I32, name="wg_raw", tag="second", align_bytes=64)
         nc.sync.dma_start(wg_raw[:], wg_words.bitcast(I32).rearrange("a p c -> p a c"))
-        tab = [stage.tile([P, T], I32, name="tab%d" % a, tag="tab%d" % a, align_bytes=64) for a in range(PASSES)]
+        tab = [keep.tile([P, T], I32, name="tab%d" % a, align_bytes=64) for a in range(PASSES)]
         nc.sync.dma_start(tab[0][:], tab_words[0].rearrange("p t i -> p (t i)").bitcast(I32))
-        idx2 = lists.tile([P, S // 16], U16, name="idx2")
-        nc.sync.dma_start(idx2[:], offs2)
         gain_sb = keep.tile([P, 4], F32, name="gain_sb")
         nc.sync.dma_start(gain_sb[:], gain.rearrange("(p t) -> p t", t=4))
+        idx2 = lists.tile([P, S // 16], U16, name="idx2")
+        nc.sync.dma_start(idx2[:], offs2)
         nc.sync.dma_start(tab[1][:], tab_words[1].rearrange("p t i -> p (t i)").bitcast(I32))
-        wf_raw = [stage.tile([P, 4, H], F32, name="wf_raw%d" % a, tag="wf%d" % a, align_bytes=64) for a in range(PASSES)]
-        for a in range(PASSES):
-            nc.sync.dma_start(wf_raw[a][:], wf[512 * a: 512 * (a + 1), :].rearrange("(p j) c -> p j c", j=4))
 
-        nc.vector.memset(tsc[32:64, :], 0)
-        nc.vector.memset(tsc[64:128, :], 0)
-        nc.vector.memset(wgs_raw[32:64, :].bitcast(I32), 0)
-        nc.vector.memset(wgs_raw[64:128, :].bitcast(I32), 0)
+        nc.vector.memset(tsc[0:ROW0, :], 0)
+        nc.vector.memset(wgs_raw[0:ROW0, :].bitcast(I32), 0)
         planes = keep.tile([P, PASSES, S + H + N], U8, name="planes", align_bytes=64)
         nc.vector.memset(planes[:].bitcast(I32), 0)
-        cache = []
-
-        def new_cache(pool, tag):
-            window = pool.tile([P, T], F32, name="cache%d" % len(cache), tag=tag, align_bytes=64)
-            cache.append(window)
-            for c in range(4):
-                nc.vector.memset(window[:, 1024 * c: 1024 * (c + 1)].bitcast(I32), 0)
-
-        new_cache(keep, "cache0")
 
         warm = keep.tile([P, 1], F32, name="warm")
         nc.scalar.activation(warm[:], gain_sb[:, 0:1], ACT.Sigmoid)
 
         picked = keep.tile([P, S], U8, name="picked")
         nc.vector.tensor_copy(picked[:], tsc[:].bitcast(U8).indirect(idx[:]))
-        nc.vector.tensor_copy(rows16[:, 0, S: S + H].rearrange("p (t m) -> p t m", t=4),
+        nc.vector.tensor_copy(rows[:, 0, S: S + H].rearrange("p (t m) -> p t m", t=4),
                               wgs_raw[:].rearrange("p (m t) -> p t m", t=4))
-        nc.vector.tensor_copy(rows16[:, 0, 0:S].bitcast(I32), picked[:].bitcast(I32))
-        nc.scalar.dma_start(rows16[0:16, 1, :].bitcast(I32), rows16[16:32, 0, :].bitcast(I32))
+        nc.vector.tensor_copy(rows[:, 0, 0:S].bitcast(I32), picked[:].bitcast(I32))
+        nc.scalar.dma_start(rows[ROW0: ROW0 + 16, 1, :].bitcast(I32), rows[ROW0 + 16: P, 0, :].bitcast(I32))
         for q in range(4):
-            nc.scalar.dma_start(planes[32 * q: 32 * q + 4].bitcast(I32), rows16[4 * q: 4 * q + 4].bitcast(I32))
+            nc.scalar.dma_start(planes[32 * q: 32 * q + 4].bitcast(I32), rows[ROW0 + 4 * q: ROW0 + 4 * q + 4].bitcast(I32))
         wg_codes = keep.tile([P, PASSES, 2 * H], U8, name="wg_codes", align_bytes=64)
         nc.vector.tensor_copy(wg_codes[:].bitcast(U16).rearrange("p a (t m) -> p a t m", t=4),
                               wg_raw[:].bitcast(U16).rearrange("p a (m t) -> p a t m", t=4))
-        new_cache(stage, "tsc")
-        v_codes = [keep.tile([P, S], U32, name="v_codes%d" % a, align_bytes=64) for a in range(PASSES)]
-        nc.vector.tensor_copy(v_codes[0][:], tab[0][:].bitcast(U32).indirect(idx[:]))
-        for h in range(2):
-            nc.vector.tensor_copy(v_codes[1][:, HALF * h: HALF * (h + 1)],
-                                  tab[1][:].bitcast(U32).indirect(idx[:, 32 * h: 32 * (h + 1)]))
 
-        wo_raw = stage.tile([P, 4, N], F32, name="wo_raw", tag="slot_a")
+        wf_raw = [stage.tile([P, 4, H], F32, name="wf_raw%d" % a, tag=("first", "second")[a], align_bytes=64)
+                  for a in range(PASSES)]
+        for a in range(PASSES):
+            nc.sync.dma_start(wf_raw[a][:], wf[512 * a: 512 * (a + 1), :].rearrange("(p j) c -> p j c", j=4))
+        wr_codes = late.tile([P, PASSES, N], I32, name="wr_codes", offset=8192, align_bytes=64)
+        nc.sync.dma_start(wr_codes[:], wr_words.rearrange("a p c i -> a p (c i)").bitcast(I32).rearrange("a p c -> p a c"))
+        wo_raw = late.tile([P, 4, N], F32, name="wo_raw", offset=0)
         nc.sync.dma_start(wo_raw[:], wo.rearrange("(p j) c -> p j c", j=4))
+
+        v0 = keep.tile([P, S], U32, name="v0", align_bytes=64)
+        nc.vector.tensor_copy(v0[:], tab[0][:].bitcast(U32).indirect(idx[:]))
+
+        cache = [keep.tile([P, T], F32, name="cache%d" % w, align_bytes=64) for w in range(2)]
+        for w in range(2):
+            for c in range(4):
+                nc.vector.memset(cache[w][:, 1024 * c: 1024 * (c + 1)].bitcast(I32), 0)
+
+        v1 = []
+
+        def gather_second_pass(pool, tag):
+            h = len(v1)
+            v1.append(pool.tile([P, HALF], U32, name="v1_%d" % h, tag=tag, align_bytes=64))
+            nc.vector.tensor_copy(v1[h][:], tab[1][:].bitcast(U32).indirect(idx[:, 32 * h: 32 * (h + 1)]))
+
+        def frames(a, j0, width):
+            if a == 0:
+                return v0[:, j0: j0 + width].bitcast(FP8X4)
+            return v1[j0 // HALF][:, j0 % HALF: j0 % HALF + width].bitcast(FP8X4)
 
         wf_codes = keep.tile([P, PASSES, H], U32, name="wf_codes", align_bytes=64)
         wf_sc = keep.tile([P, PASSES, H], U8, name="wf_sc", align_bytes=64)
-        q_in = stage.tile([P, 8, 512], BF16, name="q_in", tag="tab1", align_bytes=64)
+        wf_bf = [keep.tile([P, 4 * H], BF16, name="wf_bf%d" % a, align_bytes=64) for a in range(PASSES)]
         wo_codes = keep.tile([P, N], U32, name="wo_codes", align_bytes=64)
         wo_sc = keep.tile([P, N], U8, name="wo_sc", align_bytes=64)
         gated = [keep.tile([P, 4, HALF], F32, name="gated%d" % h) for h in range(2)]
+        h_bf = keep.tile([P, CHUNKS, 4 * CHUNK], BF16, name="h_bf", align_bytes=64)
         h_codes = keep.tile([P, S], U32, name="h_codes", align_bytes=64)
         h_sc = keep.tile([P, S], U8, name="h_sc", align_bytes=64)
         sig = keep.tile([P, 2, HALF], F32, name="sig")
-        th = keep.tile([P, 4, 4 * CHUNK], F32, name="th")
-        y_sb = keep.tile([P, 4, HALF], F32, name="y_sb")
+        y_sb = keep.tile([P, 2, HALF], F32, name="y_sb")
 
-        def gate(h, banks):
-            cols = slice(HALF * h, HALF * (h + 1))
+        def gate(h):
             for t in range(4):
-                b_ps = bank[banks[t]]
+                b_ps = bank[t]
                 for a in range(PASSES):
                     nc.tensor.matmul_mx(b_ps[:], wg_codes[:, a, 256 * t: 256 * (t + 1)].bitcast(FP4X4),
-                                        planes[:, a, S + P * t: S + P * (t + 1)], v_codes[a][:, cols].bitcast(FP8X4),
-                                        planes[:, a, cols], start=(a == 0), stop=(a == PASSES - 1))
+                                        planes[:, a, S + P * t: S + P * (t + 1)], frames(a, HALF * h, HALF),
+                                        planes[:, a, HALF * h: HALF * (h + 1)], start=(a == 0), stop=(a == PASSES - 1))
                 nc.scalar.activation(sig[:, t % 2, :], b_ps[:], ACT.Sigmoid)
                 nc.scalar.activation(gated[h][:, t, :], sig[:, t % 2, :], ACT.Copy, scale=gain_sb[:, t: t + 1])
 
         def quantise_wf(a):
-            dst = q_in[:, 4 * a: 4 * a + 4, :]
-            nc.vector.tensor_copy(dst.rearrange("p t (m j) -> p m t j", j=4),
+            nc.vector.tensor_copy(wf_bf[a][:].rearrange("p (t m j) -> p m t j", t=4, j=4),
                                   wf_raw[a][:].rearrange("p j (m t) -> p m t j", t=4))
-            nc.vector.quantize_mx(wf_codes[:, a, :].bitcast(FP8X4), wf_sc[:, a, :], dst.rearrange("p t c -> p (t c)"))
+            nc.vector.quantize_mx(wf_codes[:, a, :].bitcast(FP8X4), wf_sc[:, a, :], wf_bf[a][:])
 
-        def quantise_wo(n, slot, copy):
-            dst = q_in[:, slot, :]
+        def quantise_wo(n, tag):
+            dst = stage.tile([P, 4 * P], BF16, name="wo_bf%d" % n, tag=tag, align_bytes=64)
             src = wo_raw[:, :, P * n: P * (n + 1)]
-            copy(dst.rearrange("p (c i j) -> p c j i", i=4, j=4), src.rearrange("p j (c i) -> p c j i", i=4))
-            nc.vector.quantize_mx(wo_codes[:, P * n: P * (n + 1)].bitcast(FP8X4), wo_sc[:, P * n: P * (n + 1)], dst)
+            nc.scalar.copy(dst[:].rearrange("p (c i j) -> p c j i", i=4, j=4), src.rearrange("p j (c i) -> p c j i", i=4))
+            nc.vector.quantize_mx(wo_codes[:, P * n: P * (n + 1)].bitcast(FP8X4), wo_sc[:, P * n: P * (n + 1)], dst[:])
 
-        def hidden(h, banks, slots):
-            for c in range(HALF // CHUNK):
+        def hidden(h, banks):
+            for c in range(CHUNKS):
                 j0 = HALF * h + CHUNK * c
                 cols = slice(j0, j0 + CHUNK)
                 a_ps = bank[banks[c]]
                 for t in range(4):
                     for a in (1, 0):
                         nc.tensor.matmul_mx(a_ps[:, CHUNK * t: CHUNK * (t + 1)], wf_codes[:, a, P * t: P * (t + 1)].bitcast(FP8X4),
-                                            wf_sc[:, a, P * t: P * (t + 1)], v_codes[a][:, cols].bitcast(FP8X4),
+                                            wf_sc[:, a, P * t: P * (t + 1)], frames(a, j0, CHUNK),
                                             planes[:, a, cols], start=(a == 1), stop=(a == 0))
-                nc.scalar.activation(th[:, c, :], a_ps[:], ACT.Tanh)
-                h_bf = q_in[:, slots[c], :]
-                nc.vector.tensor_tensor(h_bf.rearrange("p (c i t) -> p c t i", i=4, t=4),
-                                        th[:, c, :].rearrange("p (t c i) -> p c t i", t=4, i=4),
+                th = stage.tile([P, 4 * CHUNK], F32, name="th%d_%d" % (h, c), tag="th%d_%d" % (h, c), align_bytes=64)
+                nc.scalar.activation(th[:], a_ps[:], ACT.Tanh)
+                nc.vector.tensor_tensor(h_bf[:, c, :].rearrange("p (c i t) -> p c t i", i=4, t=4),
+                                        th[:].rearrange("p (t c i) -> p c t i", t=4, i=4),
                                         gated[h][:, :, CHUNK * c: CHUNK * (c + 1)].rearrange("p t (c i) -> p c t i", i=4), MULT)
-                nc.vector.quantize_mx(h_codes[:, cols].bitcast(FP8X4), h_sc[:, cols], h_bf)
+                nc.vector.quantize_mx(h_codes[:, cols].bitcast(FP8X4), h_sc[:, cols], h_bf[:, c, :])
 
-        def place(n, h, step):
+        def place(n, h):
             cols = slice(HALF * h, HALF * (h + 1))
-            rows = slice(P * n, P * (n + 1))
-            y_ps = bank[4 + step % 3]
+            out_rows = slice(P * n, P * (n + 1))
+            y_ps = bank[Y_BANK]
             for a in range(PASSES):
-                nc.tensor.matmul_mx(y_ps[:], wr_codes[:, a, rows].bitcast(FP8X4), planes[:, a, S + H + P * n: S + H + P * (n + 1)],
-                                    v_codes[a][:, cols].bitcast(FP8X4), planes[:, a, cols], start=(a == 0), stop=False)
-            nc.tensor.matmul_mx(y_ps[:], wo_codes[:, rows].bitcast(FP8X4), wo_sc[:, rows],
-                                h_codes[:, cols].bitcast(FP8X4), h_sc[:, cols], start=False, stop=True)
-            nc.scalar.copy(y_sb[:, step % 4, :], y_ps[:])
-            nc.vector.tensor_tensor(cache[n % 3][:].indirect(idx2[:, 32 * h: 32 * (h + 1)]), y_sb[:, step % 4, :], wgo_sb[:, cols], MULT)
+                nc.tensor.matmul_mx(y_ps[:], wr_codes[:, a, out_rows].bitcast(FP8X4), planes[:, a, S + H + P * n: S + H + P * (n + 1)],
+                                    frames(a, HALF * h, HALF), planes[:, a, cols], start=(a == 0), stop=False)
+            for c in range(CHUNKS):
+                part = slice(HALF * h + CHUNK * c, HALF * h + CHUNK * (c + 1))
+                nc.tensor.matmul_mx(y_ps[:, CHUNK * c: CHUNK * (c + 1)], wo_codes[:, out_rows].bitcast(FP8X4), wo_sc[:, out_rows],
+                                    h_codes[:, part].bitcast(FP8X4), h_sc[:, part], start=False, stop=(c == CHUNKS - 1))
+            nc.scalar.copy(y_sb[:, h, :], y_ps[:])
+            nc.vector.tensor_tensor(cache[n % 2][:].indirect(idx2[:, 32 * h: 32 * (h + 1)]), y_sb[:, h, :], wgo_sb[:, cols], MULT)
             if h == 1:
-                nc.sync.dma_start(out[rows, :], cache[n % 3][:])
+                nc.sync.dma_start(out[out_rows, :], cache[n % 2][:])
 
-        gate(0, (0, 1, 2, 3))
+        gather_second_pass(keep, "v1_0")
+        gate(0)
         quantise_wf(0)
-        wr_codes = stage.tile([P, PASSES, N], I32, name="wr_codes", tag="wf0", align_bytes=64)
-        nc.sync.dma_start(wr_codes[:], wr_words.rearrange("a p c i -> a p (c i)").bitcast(I32).rearrange("a p c -> p a c"))
-        quantise_wf(1)
-        wgo_sb = stage.tile([P, S], F32, name="wgo_sb", tag="wf1", align_bytes=64)
+        wgo_sb = stage.tile([P, S], F32, name="wgo_sb", tag="first", align_bytes=64)
         nc.sync.dma_start(wgo_sb[:], wgo)
-        quantise_wo(0, 4, nc.vector.tensor_copy)
-        hidden(0, (4, 5, 6, 7), (5, 6, 7, 0))
-        place(0, 0, 0)
-        new_cache(stage, "tab0")
-        quantise_wo(1, 7, nc.scalar.copy)
-        place(1, 0, 1)
-        gate(1, (7, 7, 7, 7))
-        hidden(1, (0, 1, 2, 3), (1, 2, 3, 4))
-        place(0, 1, 2)
-        quantise_wo(2, 0, nc.scalar.copy)
-        quantise_wo(3, 7, nc.scalar.copy)
-        place(1, 1, 3)
-        place(2, 0, 4)
-        place(2, 1, 5)
-        place(3, 0, 6)
-        place(3, 1, 7)
+        quantise_wf(1)
+        gather_second_pass(stage, "second")
+        hidden(0, (Y_BANK, 5, 6, 7))
+        quantise_wo(0, "th0_0")
+        place(0, 0)
+        gate(1)
+        hidden(1, (5, 6, 7, 0))
+        place(0, 1)
+        for n in range(1, 4):
+            quantise_wo(n, "th1_%d" % (n - 1))
+            place(n, 0)
+            place(n, 1)

@@ -59,9 +59,6 @@ def tile_list_wavenet_gate_store_kernel(tc, tab_words, tab_scales, offs, wf, wg_
         planes = keep.tile([P, PASSES, S + H + N], U8, name="planes", align_bytes=64)
         nc.vector.memset(planes[:].bitcast(I32), 0)
 
-        warm = keep.tile([P, 1], F32, name="warm")
-        nc.scalar.activation(warm[:], gain_sb[:, 0:1], ACT.Sigmoid)
-
         picked = keep.tile([P, S], U8, name="picked")
         nc.vector.tensor_copy(picked[:], tsc[:].bitcast(U8).indirect(idx[:]))
         nc.vector.tensor_copy(rows[:, 0, S: S + H].rearrange("p (t m) -> p t m", t=4),
@@ -86,10 +83,16 @@ def tile_list_wavenet_gate_store_kernel(tc, tab_words, tab_scales, offs, wf, wg_
         v0 = keep.tile([P, S], U32, name="v0", align_bytes=64)
         nc.vector.tensor_copy(v0[:], tab[0][:].bitcast(U32).indirect(idx[:]))
 
-        cache = [keep.tile([P, T], F32, name="cache%d" % w, align_bytes=64) for w in range(2)]
-        for w in range(2):
+        cache = [keep.tile([P, T], F32, name="cache%d" % w, align_bytes=64) for w in range(3)]
+
+        def clear(w):
             for c in range(4):
                 nc.vector.memset(cache[w][:, 1024 * c: 1024 * (c + 1)].bitcast(I32), 0)
+
+        clear(0)
+        clear(1)
+        warm = keep.tile([P, 1], F32, name="warm")
+        nc.scalar.activation(warm[:], cache[0][:, 0:1], ACT.Sigmoid)
 
         v1 = []
 
@@ -165,9 +168,9 @@ def tile_list_wavenet_gate_store_kernel(tc, tab_words, tab_scales, offs, wf, wg_
                 nc.tensor.matmul_mx(y_ps[:, CHUNK * c: CHUNK * (c + 1)], wo_codes[:, out_rows].bitcast(FP8X4), wo_sc[:, out_rows],
                                     h_codes[:, part].bitcast(FP8X4), h_sc[:, part], start=False, stop=(c == CHUNKS - 1))
             nc.scalar.copy(y_sb[:, h, :], y_ps[:])
-            nc.vector.tensor_tensor(cache[n % 2][:].indirect(idx2[:, 32 * h: 32 * (h + 1)]), y_sb[:, h, :], wgo_sb[:, cols], MULT)
+            nc.vector.tensor_tensor(cache[n % 3][:].indirect(idx2[:, 32 * h: 32 * (h + 1)]), y_sb[:, h, :], wgo_sb[:, cols], MULT)
             if h == 1:
-                nc.sync.dma_start(out[out_rows, :], cache[n % 2][:])
+                nc.sync.dma_start(out[out_rows, :], cache[n % 3][:])
 
         gather_second_pass(keep, "v1_0")
         gate(0)
@@ -184,5 +187,7 @@ def tile_list_wavenet_gate_store_kernel(tc, tab_words, tab_scales, offs, wf, wg_
         place(0, 1)
         for n in range(1, 4):
             quantise_wo(n, "th1_%d" % (n - 1))
+            if n == 2:
+                clear(2)
             place(n, 0)
             place(n, 1)

@@ -22,7 +22,6 @@ HALF = S // 2
 CHUNK = 128
 CHUNKS = HALF // CHUNK
 ROW0 = 96
-Y_BANK = 4
 
 
 def tile_list_wavenet_gate_store_kernel(tc, tab_words, tab_scales, offs, wf, wg_words, wg_scales, gain, wo,
@@ -116,7 +115,7 @@ def tile_list_wavenet_gate_store_kernel(tc, tab_words, tab_scales, offs, wf, wg_
         h_codes = keep.tile([P, S], U32, name="h_codes", align_bytes=64)
         h_sc = keep.tile([P, S], U8, name="h_sc", align_bytes=64)
         sig = keep.tile([P, 2, HALF], F32, name="sig")
-        y_sb = keep.tile([P, 2, HALF], F32, name="y_sb")
+        y_sb = keep.tile([P, 3, HALF], F32, name="y_sb")
 
         def gate(h):
             for t in range(4):
@@ -156,10 +155,10 @@ def tile_list_wavenet_gate_store_kernel(tc, tab_words, tab_scales, offs, wf, wg_
                                         gated[h][:, :, CHUNK * c: CHUNK * (c + 1)].rearrange("p t (c i) -> p c t i", i=4), MULT)
                 nc.vector.quantize_mx(h_codes[:, cols].bitcast(FP8X4), h_sc[:, cols], h_bf[:, c, :])
 
-        def place(n, h):
+        def place(n, h, step, y_bank):
             cols = slice(HALF * h, HALF * (h + 1))
             out_rows = slice(P * n, P * (n + 1))
-            y_ps = bank[Y_BANK]
+            y_ps = bank[y_bank]
             for a in range(PASSES):
                 nc.tensor.matmul_mx(y_ps[:], wr_codes[:, a, out_rows].bitcast(FP8X4), planes[:, a, S + H + P * n: S + H + P * (n + 1)],
                                     frames(a, HALF * h, HALF), planes[:, a, cols], start=(a == 0), stop=False)
@@ -167,8 +166,8 @@ def tile_list_wavenet_gate_store_kernel(tc, tab_words, tab_scales, offs, wf, wg_
                 part = slice(HALF * h + CHUNK * c, HALF * h + CHUNK * (c + 1))
                 nc.tensor.matmul_mx(y_ps[:, CHUNK * c: CHUNK * (c + 1)], wo_codes[:, out_rows].bitcast(FP8X4), wo_sc[:, out_rows],
                                     h_codes[:, part].bitcast(FP8X4), h_sc[:, part], start=False, stop=(c == CHUNKS - 1))
-            nc.scalar.copy(y_sb[:, h, :], y_ps[:])
-            nc.vector.tensor_tensor(cache[n % 3][:].indirect(idx2[:, 32 * h: 32 * (h + 1)]), y_sb[:, h, :], wgo_sb[:, cols], MULT)
+            nc.scalar.copy(y_sb[:, step % 3, :], y_ps[:])
+            nc.vector.tensor_tensor(cache[n % 3][:].indirect(idx2[:, 32 * h: 32 * (h + 1)]), y_sb[:, step % 3, :], wgo_sb[:, cols], MULT)
             if h == 1:
                 nc.sync.dma_start(out[out_rows, :], cache[n % 3][:])
 
@@ -179,15 +178,19 @@ def tile_list_wavenet_gate_store_kernel(tc, tab_words, tab_scales, offs, wf, wg_
         nc.sync.dma_start(wgo_sb[:], wgo)
         quantise_wf(1)
         gather_second_pass(stage, "second")
-        hidden(0, (Y_BANK, 5, 6, 7))
+        hidden(0, (4, 5, 6, 7))
         quantise_wo(0, "th0_0")
-        place(0, 0)
+        place(0, 0, 0, 4)
         gate(1)
         hidden(1, (5, 6, 7, 0))
-        place(0, 1)
-        for n in range(1, 4):
-            quantise_wo(n, "th1_%d" % (n - 1))
-            if n == 2:
-                clear(2)
-            place(n, 0)
-            place(n, 1)
+        quantise_wo(1, "th1_0")
+        place(1, 0, 1, 0)
+        place(0, 1, 2, 4)
+        place(1, 1, 3, 5)
+        quantise_wo(2, "th1_1")
+        clear(2)
+        place(2, 0, 4, 6)
+        place(2, 1, 5, 7)
+        quantise_wo(3, "th1_2")
+        place(3, 0, 6, 0)
+        place(3, 1, 7, 4)

@@ -22,6 +22,7 @@ HALF = S // 2
 CHUNK = 128
 CHUNKS = HALF // CHUNK
 ROW0 = 96
+ROW1 = 112
 
 
 def tile_list_wavenet_gate_store_kernel(tc, tab_words, tab_scales, offs, wf, wg_words, wg_scales, gain, wo,
@@ -31,6 +32,7 @@ def tile_list_wavenet_gate_store_kernel(tc, tab_words, tab_scales, offs, wf, wg_
         lists = ctx.enter_context(tc.tile_pool(name="lists", bufs=1))
         keep = ctx.enter_context(tc.tile_pool(name="keep", bufs=1))
         stage = ctx.enter_context(tc.tile_pool(name="stage", bufs=1))
+        mid = ctx.enter_context(tc.tile_pool(name="mid", bufs=1))
         late = ctx.enter_context(tc.tile_pool(name="late", bufs=1))
         psum = ctx.enter_context(tc.psum_pool(name="psum", bufs=1))
         bank = [psum.tile([P, 512], F32, name="bank%d" % b) for b in range(8)]
@@ -39,39 +41,41 @@ def tile_list_wavenet_gate_store_kernel(tc, tab_words, tab_scales, offs, wf, wg_
         nc.sync.dma_start(idx[:], offs)
         tsc = stage.tile([P, T // 4], I32, name="tsc", tag="first", align_bytes=64)
         nc.sync.dma_start(tsc[ROW0:P, :], tab_scales.rearrange("a q t -> (a q) t").bitcast(I32))
-        wgs_raw = keep.tile([P, H], U8, name="wgs_raw")
-        nc.sync.dma_start(wgs_raw[ROW0:P, :].bitcast(I32), wg_scales.rearrange("a q c -> (a q) c").bitcast(I32))
+        wgs_raw = keep.tile([P, PASSES, H], U8, name="wgs_raw")
+        nc.sync.dma_start(wgs_raw[ROW1:P].bitcast(I32), wg_scales.bitcast(I32).rearrange("a q c -> q a c"))
         rows = late.tile([P, PASSES, S + H + N], U8, name="rows", offset=6144)
-        nc.sync.dma_start(rows[ROW0:P, 0, S + H:].bitcast(I32), wr_scales.rearrange("a q c -> (a q) c").bitcast(I32))
-        wg_raw = stage.tile([P, PASSES, H // 2], I32, name="wg_raw", tag="second", align_bytes=64)
+        nc.sync.dma_start(rows[ROW1:P, :, S + H:].bitcast(I32), wr_scales.bitcast(I32).rearrange("a q c -> q a c"))
+        wg_raw = keep.tile([P, PASSES, H // 2], I32, name="wg_raw")
         nc.sync.dma_start(wg_raw[:], wg_words.bitcast(I32).rearrange("a p c -> p a c"))
-        tab = [keep.tile([P, T], I32, name="tab%d" % a, align_bytes=64) for a in range(PASSES)]
-        nc.sync.dma_start(tab[0][:], tab_words[0].rearrange("p t i -> p (t i)").bitcast(I32))
+        tab0 = stage.tile([P, T], I32, name="tab0", tag="tab0", align_bytes=64)
+        nc.sync.dma_start(tab0[:], tab_words[0].rearrange("p t i -> p (t i)").bitcast(I32))
         gain_sb = keep.tile([P, 4], F32, name="gain_sb")
         nc.sync.dma_start(gain_sb[:], gain.rearrange("(p t) -> p t", t=4))
         idx2 = lists.tile([P, S // 16], U16, name="idx2")
         nc.sync.dma_start(idx2[:], offs2)
-        nc.sync.dma_start(tab[1][:], tab_words[1].rearrange("p t i -> p (t i)").bitcast(I32))
 
         nc.vector.memset(tsc[0:ROW0, :], 0)
-        nc.vector.memset(wgs_raw[0:ROW0, :].bitcast(I32), 0)
+        nc.vector.memset(wgs_raw[0:ROW0].bitcast(I32), 0)
+        nc.vector.memset(wgs_raw[ROW0:ROW1].bitcast(I32), 0)
         planes = keep.tile([P, PASSES, S + H + N], U8, name="planes", align_bytes=64)
         nc.vector.memset(planes[:].bitcast(I32), 0)
 
-        picked = keep.tile([P, S], U8, name="picked")
+        picked = mid.tile([P, S], U8, name="picked", offset=8192 - 512)
         nc.vector.tensor_copy(picked[:], tsc[:].bitcast(U8).indirect(idx[:]))
-        nc.vector.tensor_copy(rows[:, 0, S: S + H].rearrange("p (t m) -> p t m", t=4),
-                              wgs_raw[:].rearrange("p (m t) -> p t m", t=4))
-        nc.vector.tensor_copy(rows[:, 0, 0:S].bitcast(I32), picked[:].bitcast(I32))
-        nc.scalar.dma_start(rows[ROW0: ROW0 + 16, 1, :].bitcast(I32), rows[ROW0 + 16: P, 0, :].bitcast(I32))
+        nc.sync.dma_start(rows[ROW1:P, 0, 0:S].bitcast(I32), picked[ROW0:ROW1, :].bitcast(I32))
+        tab1 = stage.tile([P, T], I32, name="tab1", tag="first", align_bytes=64)
+        nc.sync.dma_start(tab1[:], tab_words[1].rearrange("p t i -> p (t i)").bitcast(I32))
+        tab = [tab0, tab1]
+        nc.vector.tensor_copy(rows[:, 1, 0:S].bitcast(I32), picked[:].bitcast(I32))
+        nc.vector.tensor_copy(rows[:, :, S: S + H].rearrange("p a (t m) -> p a t m", t=4),
+                              wgs_raw[:].rearrange("p a (m t) -> p a t m", t=4))
         for q in range(4):
-            nc.scalar.dma_start(planes[32 * q: 32 * q + 4].bitcast(I32), rows[ROW0 + 4 * q: ROW0 + 4 * q + 4].bitcast(I32))
+            nc.sync.dma_start(planes[32 * q: 32 * q + 4].bitcast(I32), rows[ROW1 + 4 * q: ROW1 + 4 * q + 4].bitcast(I32))
         wg_codes = keep.tile([P, PASSES, 2 * H], U8, name="wg_codes", align_bytes=64)
         nc.vector.tensor_copy(wg_codes[:].bitcast(U16).rearrange("p a (t m) -> p a t m", t=4),
                               wg_raw[:].bitcast(U16).rearrange("p a (m t) -> p a t m", t=4))
 
-        wf_raw = [stage.tile([P, 4, H], F32, name="wf_raw%d" % a, tag=("first", "second")[a], align_bytes=64)
-                  for a in range(PASSES)]
+        wf_raw = [mid.tile([P, 4, H], F32, name="wf_raw%d" % a, offset=8192 * a) for a in range(PASSES)]
         for a in range(PASSES):
             nc.sync.dma_start(wf_raw[a][:], wf[512 * a: 512 * (a + 1), :].rearrange("(p j) c -> p j c", j=4))
         wr_codes = late.tile([P, PASSES, N], I32, name="wr_codes", offset=8192, align_bytes=64)
@@ -82,22 +86,24 @@ def tile_list_wavenet_gate_store_kernel(tc, tab_words, tab_scales, offs, wf, wg_
         v0 = keep.tile([P, S], U32, name="v0", align_bytes=64)
         nc.vector.tensor_copy(v0[:], tab[0][:].bitcast(U32).indirect(idx[:]))
 
-        cache = [keep.tile([P, T], F32, name="cache%d" % w, align_bytes=64) for w in range(3)]
+        cache = []
 
-        def clear(w):
+        def clear(window, engine):
+            w = len(cache)
+            cache.append(window)
             for c in range(4):
-                nc.vector.memset(cache[w][:, 1024 * c: 1024 * (c + 1)].bitcast(I32), 0)
+                engine.memset(cache[w][:, 1024 * c: 1024 * (c + 1)].bitcast(I32), 0)
 
-        clear(0)
-        clear(1)
+        clear(keep.tile([P, T], F32, name="cache0", align_bytes=64), nc.vector)
+        clear(stage.tile([P, T], F32, name="cache1", tag="tab0", align_bytes=64), nc.vector)
         warm = keep.tile([P, 1], F32, name="warm")
         nc.scalar.activation(warm[:], cache[0][:, 0:1], ACT.Sigmoid)
 
         v1 = []
 
-        def gather_second_pass(pool, tag):
+        def gather_second_pass(tile):
             h = len(v1)
-            v1.append(pool.tile([P, HALF], U32, name="v1_%d" % h, tag=tag, align_bytes=64))
+            v1.append(tile)
             nc.vector.tensor_copy(v1[h][:], tab[1][:].bitcast(U32).indirect(idx[:, 32 * h: 32 * (h + 1)]))
 
         def frames(a, j0, width):
@@ -117,9 +123,9 @@ def tile_list_wavenet_gate_store_kernel(tc, tab_words, tab_scales, offs, wf, wg_
         sig = keep.tile([P, 2, HALF], F32, name="sig")
         y_sb = keep.tile([P, 3, HALF], F32, name="y_sb")
 
-        def gate(h):
+        def gate(h, banks):
             for t in range(4):
-                b_ps = bank[t]
+                b_ps = bank[banks[t]]
                 for a in range(PASSES):
                     nc.tensor.matmul_mx(b_ps[:], wg_codes[:, a, 256 * t: 256 * (t + 1)].bitcast(FP4X4),
                                         planes[:, a, S + P * t: S + P * (t + 1)], frames(a, HALF * h, HALF),
@@ -171,26 +177,26 @@ def tile_list_wavenet_gate_store_kernel(tc, tab_words, tab_scales, offs, wf, wg_
             if h == 1:
                 nc.sync.dma_start(out[out_rows, :], cache[n % 3][:])
 
-        gather_second_pass(keep, "v1_0")
-        gate(0)
-        quantise_wf(0)
+        for h in range(2):
+            gather_second_pass(keep.tile([P, HALF], U32, name="v1_%d" % h, align_bytes=64))
         wgo_sb = stage.tile([P, S], F32, name="wgo_sb", tag="first", align_bytes=64)
         nc.sync.dma_start(wgo_sb[:], wgo)
+        gate(0, (0, 1, 2, 3))
+        quantise_wf(0)
         quantise_wf(1)
-        gather_second_pass(stage, "second")
         hidden(0, (4, 5, 6, 7))
         quantise_wo(0, "th0_0")
         place(0, 0, 0, 4)
-        gate(1)
-        hidden(1, (5, 6, 7, 0))
+        gate(1, (0, 5, 6, 7))
+        hidden(1, (1, 2, 3, 0))
         quantise_wo(1, "th1_0")
         place(1, 0, 1, 0)
         place(0, 1, 2, 4)
         place(1, 1, 3, 5)
         quantise_wo(2, "th1_1")
-        clear(2)
+        clear(stage.tile([P, T], F32, name="cache2", tag="th1_3", align_bytes=64), nc.gpsimd)
         place(2, 0, 4, 6)
         place(2, 1, 5, 7)
         quantise_wo(3, "th1_2")
-        place(3, 0, 6, 0)
-        place(3, 1, 7, 4)
+        place(3, 0, 6, 1)
+        place(3, 1, 7, 2)

@@ -47,7 +47,7 @@ def tile_list_wavenet_gate_store_kernel(tc, tab_words, tab_scales, offs, wf, wg_
         nc.sync.dma_start(rows[ROW1:P, :, S + H:].bitcast(I32), wr_scales.bitcast(I32).rearrange("a q c -> q a c"))
         wg_raw = keep.tile([P, PASSES, H // 2], I32, name="wg_raw")
         nc.sync.dma_start(wg_raw[:], wg_words.bitcast(I32).rearrange("a p c -> p a c"))
-        tab0 = stage.tile([P, T], I32, name="tab0", tag="tab0", align_bytes=64)
+        tab0 = keep.tile([P, T], I32, name="tab0", align_bytes=64)
         nc.sync.dma_start(tab0[:], tab_words[0].rearrange("p t i -> p (t i)").bitcast(I32))
         gain_sb = keep.tile([P, 4], F32, name="gain_sb")
         nc.sync.dma_start(gain_sb[:], gain.rearrange("(p t) -> p t", t=4))
@@ -95,7 +95,6 @@ def tile_list_wavenet_gate_store_kernel(tc, tab_words, tab_scales, offs, wf, wg_
                 engine.memset(cache[w][:, 1024 * c: 1024 * (c + 1)].bitcast(I32), 0)
 
         clear(keep.tile([P, T], F32, name="cache0", align_bytes=64), nc.vector)
-        clear(stage.tile([P, T], F32, name="cache1", tag="tab0", align_bytes=64), nc.vector)
         warm = keep.tile([P, 1], F32, name="warm")
         nc.scalar.activation(warm[:], cache[0][:, 0:1], ACT.Sigmoid)
 
@@ -113,15 +112,14 @@ def tile_list_wavenet_gate_store_kernel(tc, tab_words, tab_scales, offs, wf, wg_
 
         wf_codes = keep.tile([P, PASSES, H], U32, name="wf_codes", align_bytes=64)
         wf_sc = keep.tile([P, PASSES, H], U8, name="wf_sc", align_bytes=64)
-        wf_bf = [keep.tile([P, 4 * H], BF16, name="wf_bf%d" % a, align_bytes=64) for a in range(PASSES)]
+        wf_bf = [[keep.tile([P, 2 * H], BF16, name="wf_bf%d_%d" % (a, u), align_bytes=64) for u in range(2)] for a in range(PASSES)]
         wo_codes = keep.tile([P, N], U32, name="wo_codes", align_bytes=64)
         wo_sc = keep.tile([P, N], U8, name="wo_sc", align_bytes=64)
         gated = [keep.tile([P, 4, HALF], F32, name="gated%d" % h) for h in range(2)]
-        h_bf = keep.tile([P, CHUNKS, 4 * CHUNK], BF16, name="h_bf", align_bytes=64)
         h_codes = keep.tile([P, S], U32, name="h_codes", align_bytes=64)
         h_sc = keep.tile([P, S], U8, name="h_sc", align_bytes=64)
         sig = keep.tile([P, 2, HALF], F32, name="sig")
-        y_sb = keep.tile([P, 3, HALF], F32, name="y_sb")
+        y_sb = keep.tile([P, 4 * HALF], F32, name="y_sb")
 
         def gate(h, banks):
             for t in range(4):
@@ -134,9 +132,12 @@ def tile_list_wavenet_gate_store_kernel(tc, tab_words, tab_scales, offs, wf, wg_
                 nc.scalar.activation(gated[h][:, t, :], sig[:, t % 2, :], ACT.Copy, scale=gain_sb[:, t: t + 1])
 
         def quantise_wf(a):
-            nc.vector.tensor_copy(wf_bf[a][:].rearrange("p (t m j) -> p m t j", t=4, j=4),
-                                  wf_raw[a][:].rearrange("p j (m t) -> p m t j", t=4))
-            nc.vector.quantize_mx(wf_codes[:, a, :].bitcast(FP8X4), wf_sc[:, a, :], wf_bf[a][:])
+            for u in range(2):
+                nc.vector.tensor_copy(wf_bf[a][u][:].rearrange("p (t m j) -> p m t j", t=2, j=4),
+                                      wf_raw[a][:].rearrange("p j (m t) -> p m t j", t=4)[:, :, 2 * u: 2 * u + 2, :])
+            for u in range(2):
+                cols = slice(2 * P * u, 2 * P * (u + 1))
+                nc.vector.quantize_mx(wf_codes[:, a, cols].bitcast(FP8X4), wf_sc[:, a, cols], wf_bf[a][u][:])
 
         def quantise_wo(n, tag):
             dst = stage.tile([P, 4 * P], BF16, name="wo_bf%d" % n, tag=tag, align_bytes=64)
@@ -149,19 +150,20 @@ def tile_list_wavenet_gate_store_kernel(tc, tab_words, tab_scales, offs, wf, wg_
                 j0 = HALF * h + CHUNK * c
                 cols = slice(j0, j0 + CHUNK)
                 a_ps = bank[banks[c]]
-                for t in range(4):
-                    for a in (1, 0):
+                for a in range(PASSES):
+                    for t in range(4):
                         nc.tensor.matmul_mx(a_ps[:, CHUNK * t: CHUNK * (t + 1)], wf_codes[:, a, P * t: P * (t + 1)].bitcast(FP8X4),
                                             wf_sc[:, a, P * t: P * (t + 1)], frames(a, j0, CHUNK),
-                                            planes[:, a, cols], start=(a == 1), stop=(a == 0))
+                                            planes[:, a, cols], start=(a == 0 and t == 0), stop=(a == PASSES - 1 and t == 3))
                 th = stage.tile([P, 4 * CHUNK], F32, name="th%d_%d" % (h, c), tag="th%d_%d" % (h, c), align_bytes=64)
                 nc.scalar.activation(th[:], a_ps[:], ACT.Tanh)
-                nc.vector.tensor_tensor(h_bf[:, c, :].rearrange("p (c i t) -> p c t i", i=4, t=4),
+                h_bf = stage.tile([P, 4 * CHUNK], BF16, name="h_bf%d_%d" % (h, c), tag="h_bf%d_%d" % (h, c), align_bytes=64)
+                nc.vector.tensor_tensor(h_bf[:].rearrange("p (c i t) -> p c t i", i=4, t=4),
                                         th[:].rearrange("p (t c i) -> p c t i", t=4, i=4),
                                         gated[h][:, :, CHUNK * c: CHUNK * (c + 1)].rearrange("p t (c i) -> p c t i", i=4), MULT)
-                nc.vector.quantize_mx(h_codes[:, cols].bitcast(FP8X4), h_sc[:, cols], h_bf[:, c, :])
+                nc.vector.quantize_mx(h_codes[:, cols].bitcast(FP8X4), h_sc[:, cols], h_bf[:])
 
-        def place(n, h, step, y_bank):
+        def project(n, h, slot, y_bank):
             cols = slice(HALF * h, HALF * (h + 1))
             out_rows = slice(P * n, P * (n + 1))
             y_ps = bank[y_bank]
@@ -172,10 +174,13 @@ def tile_list_wavenet_gate_store_kernel(tc, tab_words, tab_scales, offs, wf, wg_
                 part = slice(HALF * h + CHUNK * c, HALF * h + CHUNK * (c + 1))
                 nc.tensor.matmul_mx(y_ps[:, CHUNK * c: CHUNK * (c + 1)], wo_codes[:, out_rows].bitcast(FP8X4), wo_sc[:, out_rows],
                                     h_codes[:, part].bitcast(FP8X4), h_sc[:, part], start=False, stop=(c == CHUNKS - 1))
-            nc.scalar.copy(y_sb[:, step % 3, :], y_ps[:])
-            nc.vector.tensor_tensor(cache[n % 3][:].indirect(idx2[:, 32 * h: 32 * (h + 1)]), y_sb[:, step % 3, :], wgo_sb[:, cols], MULT)
-            if h == 1:
-                nc.sync.dma_start(out[out_rows, :], cache[n % 3][:])
+            nc.scalar.copy(y_sb[:, HALF * slot: HALF * (slot + 1)], y_ps[:])
+
+        def place(n, h, halves, slot):
+            nc.vector.tensor_tensor(cache[n % 3][:].indirect(idx2[:, 32 * h: 32 * (h + halves)]),
+                                    y_sb[:, HALF * slot: HALF * (slot + halves)], wgo_sb[:, HALF * h: HALF * (h + halves)], MULT)
+            if h + halves == 2:
+                nc.sync.dma_start(out[P * n: P * (n + 1), :], cache[n % 3][:])
 
         for h in range(2):
             gather_second_pass(keep.tile([P, HALF], U32, name="v1_%d" % h, align_bytes=64))
@@ -186,17 +191,24 @@ def tile_list_wavenet_gate_store_kernel(tc, tab_words, tab_scales, offs, wf, wg_
         quantise_wf(1)
         hidden(0, (4, 5, 6, 7))
         quantise_wo(0, "th0_0")
-        place(0, 0, 0, 4)
-        gate(1, (0, 5, 6, 7))
+        project(0, 0, 0, 4)
+        place(0, 0, 1, 0)
+        clear(stage.tile([P, T], F32, name="cache1", tag="h_bf0_3", align_bytes=64), nc.gpsimd)
+        gate(1, (5, 6, 7, 5))
         hidden(1, (1, 2, 3, 0))
         quantise_wo(1, "th1_0")
-        place(1, 0, 1, 0)
-        place(0, 1, 2, 4)
-        place(1, 1, 3, 5)
+        project(1, 0, 1, 0)
+        place(1, 0, 1, 1)
+        project(0, 1, 2, 4)
+        place(0, 1, 1, 2)
+        project(1, 1, 3, 5)
+        place(1, 1, 1, 3)
         quantise_wo(2, "th1_1")
-        clear(stage.tile([P, T], F32, name="cache2", tag="th1_3", align_bytes=64), nc.gpsimd)
-        place(2, 0, 4, 6)
-        place(2, 1, 5, 7)
         quantise_wo(3, "th1_2")
-        place(3, 0, 6, 1)
-        place(3, 1, 7, 2)
+        clear(stage.tile([P, T], F32, name="cache2", tag="th1_2", align_bytes=64), nc.gpsimd)
+        project(2, 0, 0, 6)
+        project(2, 1, 1, 7)
+        place(2, 0, 2, 0)
+        project(3, 0, 2, 1)
+        project(3, 1, 3, 2)
+        place(3, 0, 2, 2)

@@ -60,24 +60,27 @@ def tile_list_wavenet_gate_store_kernel(tc, tab_words, tab_scales, offs, wf, wg_
         planes = keep.tile([P, PASSES, S + H + N], U8, name="planes", align_bytes=64)
         nc.vector.memset(planes[:].bitcast(I32), 0)
 
-        picked = mid.tile([P, S], U8, name="picked", offset=8192 - 512)
-        nc.vector.tensor_copy(picked[:], tsc[:].bitcast(U8).indirect(idx[:]))
+        picked_bytes = mid.tile([P, 10240], U8, name="picked", offset=3072)
+        picked = picked_bytes[:, 0:S]
+        nc.vector.tensor_copy(picked, tsc[:].bitcast(U8).indirect(idx[:]))
         nc.sync.dma_start(rows[ROW1:P, 0, 0:S].bitcast(I32), picked[ROW0:ROW1, :].bitcast(I32))
         tab1 = stage.tile([P, T], I32, name="tab1", tag="first", align_bytes=64)
         nc.sync.dma_start(tab1[:], tab_words[1].rearrange("p t i -> p (t i)").bitcast(I32))
         tab = [tab0, tab1]
-        nc.vector.tensor_copy(rows[:, 1, 0:S].bitcast(I32), picked[:].bitcast(I32))
+        nc.vector.tensor_copy(rows[:, 1, 0:S].bitcast(I32), picked.bitcast(I32))
         nc.vector.tensor_copy(rows[:, :, S: S + H].rearrange("p a (t m) -> p a t m", t=4),
                               wgs_raw[:].rearrange("p a (m t) -> p a t m", t=4))
-        for q in range(4):
+        for q in (0, 2, 1, 3):
             nc.sync.dma_start(planes[32 * q: 32 * q + 4].bitcast(I32), rows[ROW1 + 4 * q: ROW1 + 4 * q + 4].bitcast(I32))
         wg_codes = keep.tile([P, PASSES, 2 * H], U8, name="wg_codes", align_bytes=64)
         nc.vector.tensor_copy(wg_codes[:].bitcast(U16).rearrange("p a (t m) -> p a t m", t=4),
                               wg_raw[:].bitcast(U16).rearrange("p a (m t) -> p a t m", t=4))
 
-        wf_raw = [mid.tile([P, 4, H], F32, name="wf_raw%d" % a, offset=8192 * a) for a in range(PASSES)]
-        for a in range(PASSES):
-            nc.sync.dma_start(wf_raw[a][:], wf[512 * a: 512 * (a + 1), :].rearrange("(p j) c -> p j c", j=4))
+        wf_first = mid.tile([P, 4, H], F32, name="wf_first", offset=4096)
+        nc.sync.dma_start(wf_first[:], wf[0:512, :].rearrange("(p j) c -> p j c", j=4))
+        wf_last = [mid.tile([P, 4, H // 2], F32, name="wf_last%d" % u, offset=(0, 12288)[u]) for u in range(2)]
+        for u in range(2):
+            nc.sync.dma_start(wf_last[u][:], wf[512:1024, 256 * u: 256 * (u + 1)].rearrange("(p j) c -> p j c", j=4))
         wr_codes = late.tile([P, PASSES, N], I32, name="wr_codes", offset=8192, align_bytes=64)
         nc.sync.dma_start(wr_codes[:], wr_words.rearrange("a p c i -> a p (c i)").bitcast(I32).rearrange("a p c -> p a c"))
         wo_raw = late.tile([P, 4, N], F32, name="wo_raw", offset=0)
@@ -131,13 +134,21 @@ def tile_list_wavenet_gate_store_kernel(tc, tab_words, tab_scales, offs, wf, wg_
                 nc.scalar.activation(sig[:, t % 2, :], b_ps[:], ACT.Sigmoid)
                 nc.scalar.activation(gated[h][:, t, :], sig[:, t % 2, :], ACT.Copy, scale=gain_sb[:, t: t + 1])
 
-        def quantise_wf(a):
+        def quantise_wf_first():
             for u in range(2):
-                nc.vector.tensor_copy(wf_bf[a][u][:].rearrange("p (t m j) -> p m t j", t=2, j=4),
-                                      wf_raw[a][:].rearrange("p j (m t) -> p m t j", t=4)[:, :, 2 * u: 2 * u + 2, :])
+                nc.vector.tensor_copy(wf_bf[0][u][:].rearrange("p (t m j) -> p m t j", t=2, j=4),
+                                      wf_first[:].rearrange("p j (m t) -> p m t j", t=4)[:, :, 2 * u: 2 * u + 2, :])
             for u in range(2):
                 cols = slice(2 * P * u, 2 * P * (u + 1))
-                nc.vector.quantize_mx(wf_codes[:, a, cols].bitcast(FP8X4), wf_sc[:, a, cols], wf_bf[a][u][:])
+                nc.vector.quantize_mx(wf_codes[:, 0, cols].bitcast(FP8X4), wf_sc[:, 0, cols], wf_bf[0][u][:])
+
+        def quantise_wf_last():
+            for u in range(2):
+                nc.vector.tensor_copy(wf_bf[1][u][:].rearrange("p (t m j) -> p m t j", t=4, j=4),
+                                      wf_last[u][:].rearrange("p j (m t) -> p m t j", t=4))
+                for t in range(4):
+                    cols = slice(P * t + 64 * u, P * t + 64 * (u + 1))
+                    nc.vector.quantize_mx(wf_codes[:, 1, cols].bitcast(FP8X4), wf_sc[:, 1, cols], wf_bf[1][u][:, 256 * t: 256 * (t + 1)])
 
         def quantise_wo(n, tag):
             dst = stage.tile([P, 4 * P], BF16, name="wo_bf%d" % n, tag=tag, align_bytes=64)
@@ -157,13 +168,16 @@ def tile_list_wavenet_gate_store_kernel(tc, tab_words, tab_scales, offs, wf, wg_
                                             planes[:, a, cols], start=(a == 0 and t == 0), stop=(a == PASSES - 1 and t == 3))
                 th = stage.tile([P, 4 * CHUNK], F32, name="th%d_%d" % (h, c), tag="th%d_%d" % (h, c), align_bytes=64)
                 nc.scalar.activation(th[:], a_ps[:], ACT.Tanh)
-                h_bf = stage.tile([P, 4 * CHUNK], BF16, name="h_bf%d_%d" % (h, c), tag="h_bf%d_%d" % (h, c), align_bytes=64)
-                nc.vector.tensor_tensor(h_bf[:].rearrange("p (c i t) -> p c t i", i=4, t=4),
+                if c % 2 == 0:
+                    h_bf = stage.tile([P, 2, 4 * CHUNK], BF16, name="h_bf%d_%d" % (h, c // 2), tag="h_bf%d_%d" % (h, c // 2), align_bytes=64)
+                nc.vector.tensor_tensor(h_bf[:, c % 2, :].rearrange("p (c i t) -> p c t i", i=4, t=4),
                                         th[:].rearrange("p (t c i) -> p c t i", t=4, i=4),
                                         gated[h][:, :, CHUNK * c: CHUNK * (c + 1)].rearrange("p t (c i) -> p c t i", i=4), MULT)
-                nc.vector.quantize_mx(h_codes[:, cols].bitcast(FP8X4), h_sc[:, cols], h_bf[:])
+                if c % 2 == 1:
+                    pair = slice(j0 - CHUNK, j0 + CHUNK)
+                    nc.vector.quantize_mx(h_codes[:, pair].bitcast(FP8X4), h_sc[:, pair], h_bf[:].rearrange("p c w -> p (c w)"))
 
-        def project(n, h, slot, y_bank):
+        def project(n, h, slot, y_bank, copy=nc.scalar.copy):
             cols = slice(HALF * h, HALF * (h + 1))
             out_rows = slice(P * n, P * (n + 1))
             y_ps = bank[y_bank]
@@ -174,7 +188,7 @@ def tile_list_wavenet_gate_store_kernel(tc, tab_words, tab_scales, offs, wf, wg_
                 part = slice(HALF * h + CHUNK * c, HALF * h + CHUNK * (c + 1))
                 nc.tensor.matmul_mx(y_ps[:, CHUNK * c: CHUNK * (c + 1)], wo_codes[:, out_rows].bitcast(FP8X4), wo_sc[:, out_rows],
                                     h_codes[:, part].bitcast(FP8X4), h_sc[:, part], start=False, stop=(c == CHUNKS - 1))
-            nc.scalar.copy(y_sb[:, HALF * slot: HALF * (slot + 1)], y_ps[:])
+            copy(y_sb[:, HALF * slot: HALF * (slot + 1)], y_ps[:])
 
         def place(n, h, halves, slot):
             nc.vector.tensor_tensor(cache[n % 3][:].indirect(idx2[:, 32 * h: 32 * (h + halves)]),
@@ -182,18 +196,18 @@ def tile_list_wavenet_gate_store_kernel(tc, tab_words, tab_scales, offs, wf, wg_
             if h + halves == 2:
                 nc.sync.dma_start(out[P * n: P * (n + 1), :], cache[n % 3][:])
 
-        for h in range(2):
-            gather_second_pass(keep.tile([P, HALF], U32, name="v1_%d" % h, align_bytes=64))
-        wgo_sb = stage.tile([P, S], F32, name="wgo_sb", tag="first", align_bytes=64)
-        nc.sync.dma_start(wgo_sb[:], wgo)
+        gather_second_pass(keep.tile([P, HALF], U32, name="v1_0", align_bytes=64))
         gate(0, (0, 1, 2, 3))
-        quantise_wf(0)
-        quantise_wf(1)
+        quantise_wf_first()
+        wgo_sb = mid.tile([P, S], F32, name="wgo_sb", offset=4096)
+        nc.sync.dma_start(wgo_sb[:], wgo)
+        quantise_wf_last()
+        gather_second_pass(mid.tile([P, HALF], U32, name="v1_1", offset=12288, align_bytes=64))
         hidden(0, (4, 5, 6, 7))
         quantise_wo(0, "th0_0")
-        project(0, 0, 0, 4)
+        project(0, 0, 0, 4, nc.vector.tensor_copy)
         place(0, 0, 1, 0)
-        clear(stage.tile([P, T], F32, name="cache1", tag="h_bf0_3", align_bytes=64), nc.gpsimd)
+        clear(stage.tile([P, T], F32, name="cache1", tag="h_bf0_1", align_bytes=64), nc.gpsimd)
         gate(1, (5, 6, 7, 5))
         hidden(1, (1, 2, 3, 0))
         quantise_wo(1, "th1_0")

@@ -22,7 +22,7 @@ HALF = S // 2
 CHUNK = 128
 CHUNKS = HALF // CHUNK
 ROW0 = 96
-ROW1 = 112
+KB = 1024
 
 
 def tile_list_wavenet_gate_store_kernel(tc, tab_words, tab_scales, offs, wf, wg_words, wg_scales, gain, wo,
@@ -39,12 +39,12 @@ def tile_list_wavenet_gate_store_kernel(tc, tab_words, tab_scales, offs, wf, wg_
 
         idx = lists.tile([P, S // 16], U16, name="idx")
         nc.sync.dma_start(idx[:], offs)
-        tsc = stage.tile([P, T // 4], I32, name="tsc", tag="first", align_bytes=64)
-        nc.sync.dma_start(tsc[ROW0:P, :], tab_scales.rearrange("a q t -> (a q) t").bitcast(I32))
-        wgs_raw = keep.tile([P, PASSES, H], U8, name="wgs_raw")
-        nc.sync.dma_start(wgs_raw[ROW1:P].bitcast(I32), wg_scales.bitcast(I32).rearrange("a q c -> q a c"))
-        rows = late.tile([P, PASSES, S + H + N], U8, name="rows", offset=6144)
-        nc.sync.dma_start(rows[ROW1:P, :, S + H:].bitcast(I32), wr_scales.bitcast(I32).rearrange("a q c -> q a c"))
+        tsc = keep.tile([P, T // 4], I32, name="tsc", align_bytes=64)
+        nc.sync.dma_start(tsc[ROW0:P, :], tab_scales.bitcast(I32).rearrange("a q t -> q a t"))
+        wgs_raw = keep.tile([P, H], U8, name="wgs_raw")
+        nc.sync.dma_start(wgs_raw[ROW0:P].bitcast(I32), wg_scales.bitcast(I32).rearrange("a q c -> q a c"))
+        rows = late.tile([P, S + H + N], U8, name="rows", offset=7 * KB)
+        nc.sync.dma_start(rows[ROW0:P, S + H:].bitcast(I32), wr_scales.bitcast(I32).rearrange("a q c -> q a c"))
         wg_raw = keep.tile([P, PASSES, H // 2], I32, name="wg_raw")
         nc.sync.dma_start(wg_raw[:], wg_words.bitcast(I32).rearrange("a p c -> p a c"))
         tab0 = keep.tile([P, T], I32, name="tab0", align_bytes=64)
@@ -56,56 +56,37 @@ def tile_list_wavenet_gate_store_kernel(tc, tab_words, tab_scales, offs, wf, wg_
 
         nc.vector.memset(tsc[0:ROW0, :], 0)
         nc.vector.memset(wgs_raw[0:ROW0].bitcast(I32), 0)
-        nc.vector.memset(wgs_raw[ROW0:ROW1].bitcast(I32), 0)
         planes = keep.tile([P, PASSES, S + H + N], U8, name="planes", align_bytes=64)
         nc.vector.memset(planes[:].bitcast(I32), 0)
 
-        picked_bytes = mid.tile([P, 10240], U8, name="picked", offset=3072)
+        picked_bytes = mid.tile([P, 14 * KB], U8, name="picked", offset=3 * KB)
         picked = picked_bytes[:, 0:S]
         nc.vector.tensor_copy(picked, tsc[:].bitcast(U8).indirect(idx[:]))
-        nc.sync.dma_start(rows[ROW1:P, 0, 0:S].bitcast(I32), picked[ROW0:ROW1, :].bitcast(I32))
-        tab1 = stage.tile([P, T], I32, name="tab1", tag="first", align_bytes=64)
+        nc.vector.tensor_copy(rows[:, S: S + H].rearrange("p (t m) -> p t m", t=4), wgs_raw[:].rearrange("p (m t) -> p t m", t=4))
+        nc.vector.tensor_copy(rows[:, 0:S].bitcast(I32), picked.bitcast(I32))
+        for q in (0, 2, 1, 3):
+            nc.sync.dma_start(planes[32 * q: 32 * q + 4].bitcast(I32), rows[ROW0 + 8 * q: ROW0 + 8 * q + 8].bitcast(I32))
+        tab1 = mid.tile([P, T], I32, name="tab1", offset=16 * KB, align_bytes=64)
         nc.sync.dma_start(tab1[:], tab_words[1].rearrange("p t i -> p (t i)").bitcast(I32))
         tab = [tab0, tab1]
-        nc.vector.tensor_copy(rows[:, 1, 0:S].bitcast(I32), picked.bitcast(I32))
-        nc.vector.tensor_copy(rows[:, :, S: S + H].rearrange("p a (t m) -> p a t m", t=4),
-                              wgs_raw[:].rearrange("p a (m t) -> p a t m", t=4))
-        for q in (0, 2, 1, 3):
-            nc.sync.dma_start(planes[32 * q: 32 * q + 4].bitcast(I32), rows[ROW1 + 4 * q: ROW1 + 4 * q + 4].bitcast(I32))
         wg_codes = keep.tile([P, PASSES, 2 * H], U8, name="wg_codes", align_bytes=64)
         nc.vector.tensor_copy(wg_codes[:].bitcast(U16).rearrange("p a (t m) -> p a t m", t=4),
                               wg_raw[:].bitcast(U16).rearrange("p a (m t) -> p a t m", t=4))
 
-        wf_first = mid.tile([P, 4, H], F32, name="wf_first", offset=4096)
+        wf_first = mid.tile([P, 4, H], F32, name="wf_first", offset=4 * KB)
         nc.sync.dma_start(wf_first[:], wf[0:512, :].rearrange("(p j) c -> p j c", j=4))
-        wf_last = [mid.tile([P, 4, H // 2], F32, name="wf_last%d" % u, offset=(0, 12288)[u]) for u in range(2)]
+        wf_last = [mid.tile([P, 4, H // 2], F32, name="wf_last%d" % u, offset=(0, 12 * KB)[u]) for u in range(2)]
         for u in range(2):
             nc.sync.dma_start(wf_last[u][:], wf[512:1024, 256 * u: 256 * (u + 1)].rearrange("(p j) c -> p j c", j=4))
-        wr_codes = late.tile([P, PASSES, N], I32, name="wr_codes", offset=8192, align_bytes=64)
+        wr_codes = late.tile([P, PASSES, N], I32, name="wr_codes", offset=8 * KB, align_bytes=64)
         nc.sync.dma_start(wr_codes[:], wr_words.rearrange("a p c i -> a p (c i)").bitcast(I32).rearrange("a p c -> p a c"))
         wo_raw = late.tile([P, 4, N], F32, name="wo_raw", offset=0)
         nc.sync.dma_start(wo_raw[:], wo.rearrange("(p j) c -> p j c", j=4))
 
         v0 = keep.tile([P, S], U32, name="v0", align_bytes=64)
         nc.vector.tensor_copy(v0[:], tab[0][:].bitcast(U32).indirect(idx[:]))
-
-        cache = []
-
-        def clear(window, engine):
-            w = len(cache)
-            cache.append(window)
-            for c in range(4):
-                engine.memset(cache[w][:, 1024 * c: 1024 * (c + 1)].bitcast(I32), 0)
-
-        clear(keep.tile([P, T], F32, name="cache0", align_bytes=64), nc.vector)
-        warm = keep.tile([P, 1], F32, name="warm")
-        nc.scalar.activation(warm[:], cache[0][:, 0:1], ACT.Sigmoid)
-
-        v1 = []
-
-        def gather_second_pass(tile):
-            h = len(v1)
-            v1.append(tile)
+        v1 = [keep.tile([P, HALF], U32, name="v1_%d" % h, align_bytes=64) for h in range(2)]
+        for h in range(2):
             nc.vector.tensor_copy(v1[h][:], tab[1][:].bitcast(U32).indirect(idx[:, 32 * h: 32 * (h + 1)]))
 
         def frames(a, j0, width):
@@ -113,116 +94,132 @@ def tile_list_wavenet_gate_store_kernel(tc, tab_words, tab_scales, offs, wf, wg_
                 return v0[:, j0: j0 + width].bitcast(FP8X4)
             return v1[j0 // HALF][:, j0 % HALF: j0 % HALF + width].bitcast(FP8X4)
 
+        cache = [keep.tile([P, T], F32, name="cache%d" % w, align_bytes=64) for w in range(2)]
+
+        def clear(w):
+            for c in range(4):
+                nc.vector.memset(cache[w][:, 1024 * c: 1024 * (c + 1)].bitcast(I32), 0)
+
         wf_codes = keep.tile([P, PASSES, H], U32, name="wf_codes", align_bytes=64)
         wf_sc = keep.tile([P, PASSES, H], U8, name="wf_sc", align_bytes=64)
-        wf_bf = [[keep.tile([P, 2 * H], BF16, name="wf_bf%d_%d" % (a, u), align_bytes=64) for u in range(2)] for a in range(PASSES)]
-        wo_codes = keep.tile([P, N], U32, name="wo_codes", align_bytes=64)
-        wo_sc = keep.tile([P, N], U8, name="wo_sc", align_bytes=64)
-        gated = [keep.tile([P, 4, HALF], F32, name="gated%d" % h) for h in range(2)]
         h_codes = keep.tile([P, S], U32, name="h_codes", align_bytes=64)
         h_sc = keep.tile([P, S], U8, name="h_sc", align_bytes=64)
-        sig = keep.tile([P, 2, HALF], F32, name="sig")
-        y_sb = keep.tile([P, 4 * HALF], F32, name="y_sb")
+        sig = [keep.tile([P, 4, HALF], F32, name="sig%d" % h) for h in range(2)]
+        wo_sc = keep.tile([P, N], U8, name="wo_sc", align_bytes=64)
+        gated = []
+        wo_codes = []
 
-        def gate(h, banks):
+        def gate(h):
             for t in range(4):
-                b_ps = bank[banks[t]]
+                b_ps = bank[4 * h + t]
                 for a in range(PASSES):
                     nc.tensor.matmul_mx(b_ps[:], wg_codes[:, a, 256 * t: 256 * (t + 1)].bitcast(FP4X4),
                                         planes[:, a, S + P * t: S + P * (t + 1)], frames(a, HALF * h, HALF),
                                         planes[:, a, HALF * h: HALF * (h + 1)], start=(a == 0), stop=(a == PASSES - 1))
-                nc.scalar.activation(sig[:, t % 2, :], b_ps[:], ACT.Sigmoid)
-                nc.scalar.activation(gated[h][:, t, :], sig[:, t % 2, :], ACT.Copy, scale=gain_sb[:, t: t + 1])
+                nc.scalar.activation(sig[h][:, t, :], b_ps[:], ACT.Sigmoid)
 
         def quantise_wf_first():
+            wf_bf = [mid.tile([P, 2 * H], BF16, name="wf_bf0_%d" % u, offset=(20 + 2 * u) * KB, align_bytes=64) for u in range(2)]
             for u in range(2):
-                nc.vector.tensor_copy(wf_bf[0][u][:].rearrange("p (t m j) -> p m t j", t=2, j=4),
+                nc.vector.tensor_copy(wf_bf[u][:].rearrange("p (t m j) -> p m t j", t=2, j=4),
                                       wf_first[:].rearrange("p j (m t) -> p m t j", t=4)[:, :, 2 * u: 2 * u + 2, :])
             for u in range(2):
                 cols = slice(2 * P * u, 2 * P * (u + 1))
-                nc.vector.quantize_mx(wf_codes[:, 0, cols].bitcast(FP8X4), wf_sc[:, 0, cols], wf_bf[0][u][:])
+                nc.vector.quantize_mx(wf_codes[:, 0, cols].bitcast(FP8X4), wf_sc[:, 0, cols], wf_bf[u][:])
 
         def quantise_wf_last():
             for u in range(2):
-                nc.vector.tensor_copy(wf_bf[1][u][:].rearrange("p (t m j) -> p m t j", t=4, j=4),
+                wf_bf = keep.tile([P, 2 * H], BF16, name="wf_bf1_%d" % u, align_bytes=64)
+                nc.vector.tensor_copy(wf_bf[:].rearrange("p (t m j) -> p m t j", t=4, j=4),
                                       wf_last[u][:].rearrange("p j (m t) -> p m t j", t=4))
                 for t in range(4):
                     cols = slice(P * t + 64 * u, P * t + 64 * (u + 1))
-                    nc.vector.quantize_mx(wf_codes[:, 1, cols].bitcast(FP8X4), wf_sc[:, 1, cols], wf_bf[1][u][:, 256 * t: 256 * (t + 1)])
+                    nc.vector.quantize_mx(wf_codes[:, 1, cols].bitcast(FP8X4), wf_sc[:, 1, cols], wf_bf[:, 256 * t: 256 * (t + 1)])
 
-        def quantise_wo(n, tag):
-            dst = stage.tile([P, 4 * P], BF16, name="wo_bf%d" % n, tag=tag, align_bytes=64)
+        def cast_wo(n, dst):
             src = wo_raw[:, :, P * n: P * (n + 1)]
-            nc.scalar.copy(dst[:].rearrange("p (c i j) -> p c j i", i=4, j=4), src.rearrange("p j (c i) -> p c j i", i=4))
-            nc.vector.quantize_mx(wo_codes[:, P * n: P * (n + 1)].bitcast(FP8X4), wo_sc[:, P * n: P * (n + 1)], dst[:])
+            nc.scalar.copy(dst.rearrange("p (c i j) -> p c j i", i=4, j=4), src.rearrange("p j (c i) -> p c j i", i=4))
 
-        def hidden(h, banks):
-            for c in range(CHUNKS):
-                j0 = HALF * h + CHUNK * c
-                cols = slice(j0, j0 + CHUNK)
-                a_ps = bank[banks[c]]
-                for a in range(PASSES):
-                    for t in range(4):
-                        nc.tensor.matmul_mx(a_ps[:, CHUNK * t: CHUNK * (t + 1)], wf_codes[:, a, P * t: P * (t + 1)].bitcast(FP8X4),
-                                            wf_sc[:, a, P * t: P * (t + 1)], frames(a, j0, CHUNK),
-                                            planes[:, a, cols], start=(a == 0 and t == 0), stop=(a == PASSES - 1 and t == 3))
-                th = stage.tile([P, 4 * CHUNK], F32, name="th%d_%d" % (h, c), tag="th%d_%d" % (h, c), align_bytes=64)
-                nc.scalar.activation(th[:], a_ps[:], ACT.Tanh)
-                if c % 2 == 0:
-                    h_bf = stage.tile([P, 2, 4 * CHUNK], BF16, name="h_bf%d_%d" % (h, c // 2), tag="h_bf%d_%d" % (h, c // 2), align_bytes=64)
-                nc.vector.tensor_tensor(h_bf[:, c % 2, :].rearrange("p (c i t) -> p c t i", i=4, t=4),
-                                        th[:].rearrange("p (t c i) -> p c t i", t=4, i=4),
-                                        gated[h][:, :, CHUNK * c: CHUNK * (c + 1)].rearrange("p t (c i) -> p c t i", i=4), MULT)
-                if c % 2 == 1:
-                    pair = slice(j0 - CHUNK, j0 + CHUNK)
-                    nc.vector.quantize_mx(h_codes[:, pair].bitcast(FP8X4), h_sc[:, pair], h_bf[:].rearrange("p c w -> p (c w)"))
+        def hidden(c, order):
+            h = c // CHUNKS
+            j0 = CHUNK * c
+            cols = slice(j0, j0 + CHUNK)
+            a_ps = bank[c]
+            for a in order:
+                for t in range(4):
+                    nc.tensor.matmul_mx(a_ps[:, CHUNK * t: CHUNK * (t + 1)], wf_codes[:, a, P * t: P * (t + 1)].bitcast(FP8X4),
+                                        wf_sc[:, a, P * t: P * (t + 1)], frames(a, j0, CHUNK),
+                                        planes[:, a, cols], start=(a == order[0] and t == 0), stop=(a == order[-1] and t == 3))
+            th = stage.tile([P, 4 * CHUNK], F32, name="th%d" % c, tag="th%d" % c, align_bytes=64)
+            nc.scalar.activation(th[:], a_ps[:], ACT.Tanh)
+            within = j0 % HALF
+            nc.vector.tensor_tensor(h_bf[:, c, :].rearrange("p (c i t) -> p c t i", i=4, t=4),
+                                    th[:].rearrange("p (t c i) -> p c t i", t=4, i=4),
+                                    gated[h][:, :, within: within + CHUNK].rearrange("p t (c i) -> p c t i", i=4), MULT)
+            if c % 2 == 1:
+                pair = slice(j0 - CHUNK, j0 + CHUNK)
+                nc.vector.quantize_mx(h_codes[:, pair].bitcast(FP8X4), h_sc[:, pair], h_bf[:, c - 1: c + 1, :].rearrange("p c w -> p (c w)"))
 
-        def project(n, h, slot, y_bank, copy=nc.scalar.copy):
+        def project(n, h, y):
             cols = slice(HALF * h, HALF * (h + 1))
             out_rows = slice(P * n, P * (n + 1))
-            y_ps = bank[y_bank]
+            y_ps = bank[2 * n + h]
             for a in range(PASSES):
                 nc.tensor.matmul_mx(y_ps[:], wr_codes[:, a, out_rows].bitcast(FP8X4), planes[:, a, S + H + P * n: S + H + P * (n + 1)],
                                     frames(a, HALF * h, HALF), planes[:, a, cols], start=(a == 0), stop=False)
-            for c in range(CHUNKS):
-                part = slice(HALF * h + CHUNK * c, HALF * h + CHUNK * (c + 1))
-                nc.tensor.matmul_mx(y_ps[:, CHUNK * c: CHUNK * (c + 1)], wo_codes[:, out_rows].bitcast(FP8X4), wo_sc[:, out_rows],
-                                    h_codes[:, part].bitcast(FP8X4), h_sc[:, part], start=False, stop=(c == CHUNKS - 1))
-            copy(y_sb[:, HALF * slot: HALF * (slot + 1)], y_ps[:])
+            nc.tensor.matmul_mx(y_ps[:], wo_codes[n].bitcast(FP8X4), wo_sc[:, out_rows],
+                                h_codes[:, cols].bitcast(FP8X4), h_sc[:, cols], start=False, stop=True)
+            nc.scalar.copy(y, y_ps[:])
 
-        def place(n, h, halves, slot):
-            nc.vector.tensor_tensor(cache[n % 3][:].indirect(idx2[:, 32 * h: 32 * (h + halves)]),
-                                    y_sb[:, HALF * slot: HALF * (slot + halves)], wgo_sb[:, HALF * h: HALF * (h + halves)], MULT)
+        def place(n, h, halves, y):
+            nc.vector.tensor_tensor(cache[n % 2][:].indirect(idx2[:, 32 * h: 32 * (h + halves)]),
+                                    y, wgo_sb[:, HALF * h: HALF * (h + halves)], MULT)
             if h + halves == 2:
-                nc.sync.dma_start(out[P * n: P * (n + 1), :], cache[n % 3][:])
+                nc.sync.dma_start(out[P * n: P * (n + 1), :], cache[n % 2][:])
 
-        gather_second_pass(keep.tile([P, HALF], U32, name="v1_0", align_bytes=64))
-        gate(0, (0, 1, 2, 3))
+        h_bf = keep.tile([P, 2 * CHUNKS, 4 * CHUNK], BF16, name="h_bf", align_bytes=64)
+        clear(0)
+        warm = keep.tile([P, 1], F32, name="warm")
+        nc.scalar.activation(warm[:], cache[0][:, 0:1], ACT.Sigmoid)
+        gate(0)
+        gate(1)
         quantise_wf_first()
-        wgo_sb = mid.tile([P, S], F32, name="wgo_sb", offset=4096)
+        wgo_sb = mid.tile([P, S], F32, name="wgo_sb", offset=4 * KB)
         nc.sync.dma_start(wgo_sb[:], wgo)
         quantise_wf_last()
-        gather_second_pass(mid.tile([P, HALF], U32, name="v1_1", offset=12288, align_bytes=64))
-        hidden(0, (4, 5, 6, 7))
-        quantise_wo(0, "th0_0")
-        project(0, 0, 0, 4, nc.vector.tensor_copy)
-        place(0, 0, 1, 0)
-        clear(stage.tile([P, T], F32, name="cache1", tag="h_bf0_1", align_bytes=64), nc.gpsimd)
-        gate(1, (5, 6, 7, 5))
-        hidden(1, (1, 2, 3, 0))
-        quantise_wo(1, "th1_0")
-        project(1, 0, 1, 0)
-        place(1, 0, 1, 1)
-        project(0, 1, 2, 4)
-        place(0, 1, 1, 2)
-        project(1, 1, 3, 5)
-        place(1, 1, 1, 3)
-        quantise_wo(2, "th1_1")
-        quantise_wo(3, "th1_2")
-        clear(stage.tile([P, T], F32, name="cache2", tag="th1_2", align_bytes=64), nc.gpsimd)
-        project(2, 0, 0, 6)
-        project(2, 1, 1, 7)
-        place(2, 0, 2, 0)
-        project(3, 0, 2, 1)
-        project(3, 1, 3, 2)
-        place(3, 0, 2, 2)
+        gated.append(mid.tile([P, 4, HALF], F32, name="gated0", offset=8 * KB))
+        for t in range(4):
+            nc.vector.tensor_scalar(gated[0][:, t, :], sig[0][:, t, :], gain_sb[:, t: t + 1], None, MULT)
+        for c in range(CHUNKS):
+            hidden(c, (0, 1))
+        gated.append(keep.tile([P, 4, HALF], F32, name="gated1"))
+        for t in range(4):
+            nc.scalar.activation(gated[1][:, t, :], sig[1][:, t, :], ACT.Copy, scale=gain_sb[:, t: t + 1])
+        hidden(4, (1, 0))
+        hidden(5, (1, 0))
+        wo_bf0 = stage.tile([P, 4 * P], BF16, name="wo_bf0", tag="th1", align_bytes=64)
+        cast_wo(0, wo_bf0[:])
+        wo_first = keep.tile([P, P], U32, name="wo_first", align_bytes=64)
+        wo_codes.append(wo_first[:])
+        nc.vector.quantize_mx(wo_codes[0].bitcast(FP8X4), wo_sc[:, 0:P], wo_bf0[:])
+        hidden(6, (1, 0))
+        hidden(7, (1, 0))
+        y00 = stage.tile([P, HALF], F32, name="y00", tag="y00", align_bytes=64)
+        project(0, 0, y00[:])
+        place(0, 0, 1, y00[:])
+        y01 = keep.tile([P, HALF], F32, name="y01")
+        project(0, 1, y01[:])
+        wo_bf = stage.tile([P, 3 * 4 * P], BF16, name="wo_bf", tag="th7", align_bytes=64)
+        wo_rest = stage.tile([P, 3 * P], U32, name="wo_rest", tag="y00", align_bytes=64)
+        for n in range(1, 4):
+            cast_wo(n, wo_bf[:, 4 * P * (n - 1): 4 * P * n])
+            wo_codes.append(wo_rest[:, P * (n - 1): P * n])
+        nc.vector.quantize_mx(wo_rest[:, 0:P].bitcast(FP8X4), wo_sc[:, P: 2 * P], wo_bf[:, 0: 4 * P])
+        nc.vector.quantize_mx(wo_rest[:, P:].bitcast(FP8X4), wo_sc[:, 2 * P:], wo_bf[:, 4 * P:])
+        place(0, 1, 1, y01[:])
+        clear(1)
+        for n in range(1, 4):
+            y = keep.tile([P, S], F32, name="y%d" % n)
+            for h in range(2):
+                project(n, h, y[:, HALF * h: HALF * (h + 1)])
+            place(n, 0, 2, y[:])

@@ -39,7 +39,7 @@ def tile_list_wavenet_gate_store_kernel(tc, tab_words, tab_scales, offs, wf, wg_
 
         idx = lists.tile([P, S // 16], U16, name="idx")
         nc.sync.dma_start(idx[:], offs)
-        tsc = keep.tile([P, T // 4], I32, name="tsc", align_bytes=64)
+        tsc = mid.tile([P, T // 4], I32, name="tsc", offset=32 * KB, align_bytes=64)
         nc.sync.dma_start(tsc[ROW0:P, :], tab_scales.bitcast(I32).rearrange("a q t -> q a t"))
         wgs_raw = keep.tile([P, H], U8, name="wgs_raw")
         nc.sync.dma_start(wgs_raw[ROW0:P].bitcast(I32), wg_scales.bitcast(I32).rearrange("a q c -> q a c"))
@@ -49,6 +49,8 @@ def tile_list_wavenet_gate_store_kernel(tc, tab_words, tab_scales, offs, wf, wg_
         nc.sync.dma_start(wg_raw[:], wg_words.bitcast(I32).rearrange("a p c -> p a c"))
         tab0 = keep.tile([P, T], I32, name="tab0", align_bytes=64)
         nc.sync.dma_start(tab0[:], tab_words[0].rearrange("p t i -> p (t i)").bitcast(I32))
+        tab1 = mid.tile([P, T], I32, name="tab1", offset=16 * KB, align_bytes=64)
+        nc.sync.dma_start(tab1[:], tab_words[1].rearrange("p t i -> p (t i)").bitcast(I32))
         gain_sb = keep.tile([P, 4], F32, name="gain_sb")
         nc.sync.dma_start(gain_sb[:], gain.rearrange("(p t) -> p t", t=4))
         idx2 = lists.tile([P, S // 16], U16, name="idx2")
@@ -56,28 +58,23 @@ def tile_list_wavenet_gate_store_kernel(tc, tab_words, tab_scales, offs, wf, wg_
 
         nc.vector.memset(tsc[0:ROW0, :], 0)
         nc.vector.memset(wgs_raw[0:ROW0].bitcast(I32), 0)
-        planes = keep.tile([P, PASSES, S + H + N], U8, name="planes", align_bytes=64)
-        nc.vector.memset(planes[:].bitcast(I32), 0)
+        planes = mid.tile([P, PASSES, S + H + N], U8, name="planes", offset=32 * KB, align_bytes=64)
 
-        picked_bytes = mid.tile([P, 14 * KB], U8, name="picked", offset=3 * KB)
+        picked_bytes = mid.tile([P, 9 * KB], U8, name="picked", offset=7 * KB)
         picked = picked_bytes[:, 0:S]
         nc.vector.tensor_copy(picked, tsc[:].bitcast(U8).indirect(idx[:]))
         nc.vector.tensor_copy(rows[:, S: S + H].rearrange("p (t m) -> p t m", t=4), wgs_raw[:].rearrange("p (m t) -> p t m", t=4))
         nc.vector.tensor_copy(rows[:, 0:S].bitcast(I32), picked.bitcast(I32))
         for q in (0, 2, 1, 3):
             nc.sync.dma_start(planes[32 * q: 32 * q + 4].bitcast(I32), rows[ROW0 + 8 * q: ROW0 + 8 * q + 8].bitcast(I32))
-        tab1 = mid.tile([P, T], I32, name="tab1", offset=16 * KB, align_bytes=64)
-        nc.sync.dma_start(tab1[:], tab_words[1].rearrange("p t i -> p (t i)").bitcast(I32))
         tab = [tab0, tab1]
         wg_codes = keep.tile([P, PASSES, 2 * H], U8, name="wg_codes", align_bytes=64)
         nc.vector.tensor_copy(wg_codes[:].bitcast(U16).rearrange("p a (t m) -> p a t m", t=4),
                               wg_raw[:].bitcast(U16).rearrange("p a (m t) -> p a t m", t=4))
 
-        wf_first = mid.tile([P, 4, H], F32, name="wf_first", offset=4 * KB)
-        nc.sync.dma_start(wf_first[:], wf[0:512, :].rearrange("(p j) c -> p j c", j=4))
-        wf_last = [mid.tile([P, 4, H // 2], F32, name="wf_last%d" % u, offset=(0, 12 * KB)[u]) for u in range(2)]
-        for u in range(2):
-            nc.sync.dma_start(wf_last[u][:], wf[512:1024, 256 * u: 256 * (u + 1)].rearrange("(p j) c -> p j c", j=4))
+        wf_raw = [mid.tile([P, 4, H], F32, name="wf_raw%d" % a, offset=8 * a * KB) for a in range(PASSES)]
+        for a in range(PASSES):
+            nc.sync.dma_start(wf_raw[a][:], wf[512 * a: 512 * (a + 1), :].rearrange("(p j) c -> p j c", j=4))
         wr_codes = late.tile([P, PASSES, N], I32, name="wr_codes", offset=8 * KB, align_bytes=64)
         nc.sync.dma_start(wr_codes[:], wr_words.rearrange("a p c i -> a p (c i)").bitcast(I32).rearrange("a p c -> p a c"))
         wo_raw = late.tile([P, 4, N], F32, name="wo_raw", offset=0)
@@ -118,23 +115,14 @@ def tile_list_wavenet_gate_store_kernel(tc, tab_words, tab_scales, offs, wf, wg_
                                         planes[:, a, HALF * h: HALF * (h + 1)], start=(a == 0), stop=(a == PASSES - 1))
                 nc.scalar.activation(sig[h][:, t, :], b_ps[:], ACT.Sigmoid)
 
-        def quantise_wf_first():
-            wf_bf = [mid.tile([P, 2 * H], BF16, name="wf_bf0_%d" % u, offset=(20 + 2 * u) * KB, align_bytes=64) for u in range(2)]
+        def quantise_wf(a):
+            wf_bf = [mid.tile([P, 2 * H], BF16, name="wf_bf%d_%d" % (a, u), offset=(20 + 4 * a + 2 * u) * KB, align_bytes=64) for u in range(2)]
             for u in range(2):
                 nc.vector.tensor_copy(wf_bf[u][:].rearrange("p (t m j) -> p m t j", t=2, j=4),
-                                      wf_first[:].rearrange("p j (m t) -> p m t j", t=4)[:, :, 2 * u: 2 * u + 2, :])
+                                      wf_raw[a][:].rearrange("p j (m t) -> p m t j", t=4)[:, :, 2 * u: 2 * u + 2, :])
             for u in range(2):
                 cols = slice(2 * P * u, 2 * P * (u + 1))
-                nc.vector.quantize_mx(wf_codes[:, 0, cols].bitcast(FP8X4), wf_sc[:, 0, cols], wf_bf[u][:])
-
-        def quantise_wf_last():
-            for u in range(2):
-                wf_bf = keep.tile([P, 2 * H], BF16, name="wf_bf1_%d" % u, align_bytes=64)
-                nc.vector.tensor_copy(wf_bf[:].rearrange("p (t m j) -> p m t j", t=4, j=4),
-                                      wf_last[u][:].rearrange("p j (m t) -> p m t j", t=4))
-                for t in range(4):
-                    cols = slice(P * t + 64 * u, P * t + 64 * (u + 1))
-                    nc.vector.quantize_mx(wf_codes[:, 1, cols].bitcast(FP8X4), wf_sc[:, 1, cols], wf_bf[:, 256 * t: 256 * (t + 1)])
+                nc.vector.quantize_mx(wf_codes[:, a, cols].bitcast(FP8X4), wf_sc[:, a, cols], wf_bf[u][:])
 
         def cast_wo(n, dst):
             src = wo_raw[:, :, P * n: P * (n + 1)]
@@ -156,9 +144,10 @@ def tile_list_wavenet_gate_store_kernel(tc, tab_words, tab_scales, offs, wf, wg_
             nc.vector.tensor_tensor(h_bf[:, c, :].rearrange("p (c i t) -> p c t i", i=4, t=4),
                                     th[:].rearrange("p (t c i) -> p c t i", t=4, i=4),
                                     gated[h][:, :, within: within + CHUNK].rearrange("p t (c i) -> p c t i", i=4), MULT)
-            if c % 2 == 1:
-                pair = slice(j0 - CHUNK, j0 + CHUNK)
-                nc.vector.quantize_mx(h_codes[:, pair].bitcast(FP8X4), h_sc[:, pair], h_bf[:, c - 1: c + 1, :].rearrange("p c w -> p (c w)"))
+
+        def quantise_h(c):
+            pair = slice(CHUNK * c, CHUNK * (c + 2))
+            nc.vector.quantize_mx(h_codes[:, pair].bitcast(FP8X4), h_sc[:, pair], h_bf[:, c: c + 2, :].rearrange("p c w -> p (c w)"))
 
         def project(n, h, y):
             cols = slice(HALF * h, HALF * (h + 1))
@@ -183,19 +172,25 @@ def tile_list_wavenet_gate_store_kernel(tc, tab_words, tab_scales, offs, wf, wg_
         nc.scalar.activation(warm[:], cache[0][:, 0:1], ACT.Sigmoid)
         gate(0)
         gate(1)
-        quantise_wf_first()
-        wgo_sb = mid.tile([P, S], F32, name="wgo_sb", offset=4 * KB)
+        quantise_wf(0)
+        wgo_sb = mid.tile([P, S], F32, name="wgo_sb", offset=0)
         nc.sync.dma_start(wgo_sb[:], wgo)
-        quantise_wf_last()
-        gated.append(mid.tile([P, 4, HALF], F32, name="gated0", offset=8 * KB))
+        quantise_wf(1)
+        gated.append(mid.tile([P, 4, HALF], F32, name="gated0", offset=4 * KB))
+        gated.append(mid.tile([P, 4, HALF], F32, name="gated1", offset=12 * KB))
         for t in range(4):
             nc.vector.tensor_scalar(gated[0][:, t, :], sig[0][:, t, :], gain_sb[:, t: t + 1], None, MULT)
-        for c in range(CHUNKS):
-            hidden(c, (0, 1))
-        gated.append(keep.tile([P, 4, HALF], F32, name="gated1"))
-        for t in range(4):
+        for t in range(2):
+            nc.vector.tensor_scalar(gated[1][:, t, :], sig[1][:, t, :], gain_sb[:, t: t + 1], None, MULT)
+        for t in range(2, 4):
             nc.scalar.activation(gated[1][:, t, :], sig[1][:, t, :], ACT.Copy, scale=gain_sb[:, t: t + 1])
+        hidden(0, (0, 1))
+        hidden(1, (0, 1))
+        hidden(2, (0, 1))
+        quantise_h(0)
+        hidden(3, (0, 1))
         hidden(4, (1, 0))
+        quantise_h(2)
         hidden(5, (1, 0))
         wo_bf0 = stage.tile([P, 4 * P], BF16, name="wo_bf0", tag="th1", align_bytes=64)
         cast_wo(0, wo_bf0[:])
@@ -203,7 +198,9 @@ def tile_list_wavenet_gate_store_kernel(tc, tab_words, tab_scales, offs, wf, wg_
         wo_codes.append(wo_first[:])
         nc.vector.quantize_mx(wo_codes[0].bitcast(FP8X4), wo_sc[:, 0:P], wo_bf0[:])
         hidden(6, (1, 0))
+        quantise_h(4)
         hidden(7, (1, 0))
+        quantise_h(6)
         y00 = stage.tile([P, HALF], F32, name="y00", tag="y00", align_bytes=64)
         project(0, 0, y00[:])
         place(0, 0, 1, y00[:])

@@ -43,11 +43,10 @@ def tile_list_wavenet_gate_store_kernel(tc, tab_words, tab_scales, offs, wf, wg_
         nc.sync.dma_start(tsc[ROW0:P, :], tab_scales.bitcast(I32).rearrange("a q t -> q a t"))
         wgs_raw = keep.tile([P, H], U8, name="wgs_raw")
         nc.sync.dma_start(wgs_raw[ROW0:P].bitcast(I32), wg_scales.bitcast(I32).rearrange("a q c -> q a c"))
-        rows = late.tile([P, S + H + N], U8, name="rows", offset=7 * KB)
-        nc.sync.dma_start(rows[ROW0:P, S + H:].bitcast(I32), wr_scales.bitcast(I32).rearrange("a q c -> q a c"))
+        rows = late.tile([P, S + H], U8, name="rows", offset=7 * KB)
         wg_raw = keep.tile([P, PASSES, H // 2], I32, name="wg_raw")
         nc.sync.dma_start(wg_raw[:], wg_words.bitcast(I32).rearrange("a p c -> p a c"))
-        tab0 = keep.tile([P, T], I32, name="tab0", align_bytes=64)
+        tab0 = mid.tile([P, T], I32, name="tab0", offset=36 * KB, align_bytes=64)
         nc.sync.dma_start(tab0[:], tab_words[0].rearrange("p t i -> p (t i)").bitcast(I32))
         tab1 = mid.tile([P, T], I32, name="tab1", offset=16 * KB, align_bytes=64)
         nc.sync.dma_start(tab1[:], tab_words[1].rearrange("p t i -> p (t i)").bitcast(I32))
@@ -58,7 +57,7 @@ def tile_list_wavenet_gate_store_kernel(tc, tab_words, tab_scales, offs, wf, wg_
 
         nc.vector.memset(tsc[0:ROW0, :], 0)
         nc.vector.memset(wgs_raw[0:ROW0].bitcast(I32), 0)
-        planes = mid.tile([P, PASSES, S + H + N], U8, name="planes", offset=32 * KB, align_bytes=64)
+        planes = mid.tile([P, PASSES, S + H], U8, name="planes", offset=32 * KB, align_bytes=64)
 
         picked_bytes = mid.tile([P, 9 * KB], U8, name="picked", offset=7 * KB)
         picked = picked_bytes[:, 0:S]
@@ -72,16 +71,21 @@ def tile_list_wavenet_gate_store_kernel(tc, tab_words, tab_scales, offs, wf, wg_
         nc.vector.tensor_copy(wg_codes[:].bitcast(U16).rearrange("p a (t m) -> p a t m", t=4),
                               wg_raw[:].bitcast(U16).rearrange("p a (m t) -> p a t m", t=4))
 
-        wf_raw = [mid.tile([P, 4, H], F32, name="wf_raw%d" % a, offset=8 * a * KB) for a in range(PASSES)]
-        for a in range(PASSES):
-            nc.sync.dma_start(wf_raw[a][:], wf[512 * a: 512 * (a + 1), :].rearrange("(p j) c -> p j c", j=4))
-        wr_codes = late.tile([P, PASSES, N], I32, name="wr_codes", offset=8 * KB, align_bytes=64)
-        nc.sync.dma_start(wr_codes[:], wr_words.rearrange("a p c i -> a p (c i)").bitcast(I32).rearrange("a p c -> p a c"))
+        wf_first = mid.tile([P, 4, H], F32, name="wf_first", offset=0)
+        nc.sync.dma_start(wf_first[:], wf[0:512, :].rearrange("(p j) c -> p j c", j=4))
+        wf_last = [mid.tile([P, 4, H // 2], F32, name="wf_last%d" % u, offset=(8 + 4 * u) * KB) for u in range(2)]
+        for u in range(2):
+            nc.sync.dma_start(wf_last[u][:], wf[512:1024, 256 * u: 256 * (u + 1)].rearrange("(p j) c -> p j c", j=4))
         wo_raw = late.tile([P, 4, N], F32, name="wo_raw", offset=0)
         nc.sync.dma_start(wo_raw[:], wo.rearrange("(p j) c -> p j c", j=4))
+        wr_codes = late.tile([P, PASSES, N], I32, name="wr_codes", offset=8 * KB, align_bytes=64)
+        nc.sync.dma_start(wr_codes[:], wr_words.rearrange("a p c i -> a p (c i)").bitcast(I32).rearrange("a p c -> p a c"))
 
         v0 = keep.tile([P, S], U32, name="v0", align_bytes=64)
         nc.vector.tensor_copy(v0[:], tab[0][:].bitcast(U32).indirect(idx[:]))
+        wr_sc = mid.tile([P, PASSES, N], U8, name="wr_sc", offset=36 * KB, align_bytes=64)
+        for q in range(4):
+            nc.sync.dma_start(wr_sc[32 * q: 32 * q + 4].bitcast(I32), wr_scales.bitcast(I32)[:, 4 * q: 4 * q + 4, :].rearrange("a r c -> r a c"))
         v1 = [keep.tile([P, HALF], U32, name="v1_%d" % h, align_bytes=64) for h in range(2)]
         for h in range(2):
             nc.vector.tensor_copy(v1[h][:], tab[1][:].bitcast(U32).indirect(idx[:, 32 * h: 32 * (h + 1)]))
@@ -115,14 +119,23 @@ def tile_list_wavenet_gate_store_kernel(tc, tab_words, tab_scales, offs, wf, wg_
                                         planes[:, a, HALF * h: HALF * (h + 1)], start=(a == 0), stop=(a == PASSES - 1))
                 nc.scalar.activation(sig[h][:, t, :], b_ps[:], ACT.Sigmoid)
 
-        def quantise_wf(a):
-            wf_bf = [mid.tile([P, 2 * H], BF16, name="wf_bf%d_%d" % (a, u), offset=(20 + 4 * a + 2 * u) * KB, align_bytes=64) for u in range(2)]
+        def quantise_wf_first():
+            wf_bf = [mid.tile([P, 2 * H], BF16, name="wf_bf0_%d" % u, offset=(20 + 2 * u) * KB, align_bytes=64) for u in range(2)]
             for u in range(2):
                 nc.vector.tensor_copy(wf_bf[u][:].rearrange("p (t m j) -> p m t j", t=2, j=4),
-                                      wf_raw[a][:].rearrange("p j (m t) -> p m t j", t=4)[:, :, 2 * u: 2 * u + 2, :])
+                                      wf_first[:].rearrange("p j (m t) -> p m t j", t=4)[:, :, 2 * u: 2 * u + 2, :])
             for u in range(2):
                 cols = slice(2 * P * u, 2 * P * (u + 1))
-                nc.vector.quantize_mx(wf_codes[:, a, cols].bitcast(FP8X4), wf_sc[:, a, cols], wf_bf[u][:])
+                nc.vector.quantize_mx(wf_codes[:, 0, cols].bitcast(FP8X4), wf_sc[:, 0, cols], wf_bf[u][:])
+
+        def quantise_wf_last():
+            for u in range(2):
+                wf_bf = keep.tile([P, 2 * H], BF16, name="wf_bf1_%d" % u, align_bytes=64)
+                nc.vector.tensor_copy(wf_bf[:].rearrange("p (t m j) -> p m t j", t=4, j=4),
+                                      wf_last[u][:].rearrange("p j (m t) -> p m t j", t=4))
+                for t in range(4):
+                    cols = slice(P * t + 64 * u, P * t + 64 * (u + 1))
+                    nc.vector.quantize_mx(wf_codes[:, 1, cols].bitcast(FP8X4), wf_sc[:, 1, cols], wf_bf[:, 256 * t: 256 * (t + 1)])
 
         def cast_wo(n, dst):
             src = wo_raw[:, :, P * n: P * (n + 1)]
@@ -154,7 +167,7 @@ def tile_list_wavenet_gate_store_kernel(tc, tab_words, tab_scales, offs, wf, wg_
             out_rows = slice(P * n, P * (n + 1))
             y_ps = bank[2 * n + h]
             for a in range(PASSES):
-                nc.tensor.matmul_mx(y_ps[:], wr_codes[:, a, out_rows].bitcast(FP8X4), planes[:, a, S + H + P * n: S + H + P * (n + 1)],
+                nc.tensor.matmul_mx(y_ps[:], wr_codes[:, a, out_rows].bitcast(FP8X4), wr_sc[:, a, out_rows],
                                     frames(a, HALF * h, HALF), planes[:, a, cols], start=(a == 0), stop=False)
             nc.tensor.matmul_mx(y_ps[:], wo_codes[n].bitcast(FP8X4), wo_sc[:, out_rows],
                                 h_codes[:, cols].bitcast(FP8X4), h_sc[:, cols], start=False, stop=True)
@@ -172,12 +185,12 @@ def tile_list_wavenet_gate_store_kernel(tc, tab_words, tab_scales, offs, wf, wg_
         nc.scalar.activation(warm[:], cache[0][:, 0:1], ACT.Sigmoid)
         gate(0)
         gate(1)
-        quantise_wf(0)
+        quantise_wf_first()
         wgo_sb = mid.tile([P, S], F32, name="wgo_sb", offset=0)
         nc.sync.dma_start(wgo_sb[:], wgo)
-        quantise_wf(1)
-        gated.append(mid.tile([P, 4, HALF], F32, name="gated0", offset=4 * KB))
-        gated.append(mid.tile([P, 4, HALF], F32, name="gated1", offset=12 * KB))
+        quantise_wf_last()
+        gated.append(mid.tile([P, 4, HALF], F32, name="gated0", offset=5 * KB))
+        gated.append(mid.tile([P, 4, HALF], F32, name="gated1", offset=13 * KB))
         for t in range(4):
             nc.vector.tensor_scalar(gated[0][:, t, :], sig[0][:, t, :], gain_sb[:, t: t + 1], None, MULT)
         for t in range(2):

@@ -122,8 +122,8 @@ def tile_list_wavenet_gate_store_kernel(tc, tab_words, tab_scales, offs, wf, wg_
         def quantise_wf_first():
             wf_bf = [mid.tile([P, 2 * H], BF16, name="wf_bf0_%d" % u, offset=(20 + 2 * u) * KB, align_bytes=64) for u in range(2)]
             for u in range(2):
-                nc.vector.tensor_copy(wf_bf[u][:].rearrange("p (t m j) -> p m t j", t=2, j=4),
-                                      wf_first[:].rearrange("p j (m t) -> p m t j", t=4)[:, :, 2 * u: 2 * u + 2, :])
+                nc.vector.tensor_copy(wf_bf[u][:].rearrange("p (t m j) -> p m j t", t=2, j=4),
+                                      wf_first[:].rearrange("p j (m t) -> p m j t", t=4)[:, :, :, 2 * u: 2 * u + 2])
             for u in range(2):
                 cols = slice(2 * P * u, 2 * P * (u + 1))
                 nc.vector.quantize_mx(wf_codes[:, 0, cols].bitcast(FP8X4), wf_sc[:, 0, cols], wf_bf[u][:])
@@ -131,8 +131,8 @@ def tile_list_wavenet_gate_store_kernel(tc, tab_words, tab_scales, offs, wf, wg_
         def quantise_wf_last():
             for u in range(2):
                 wf_bf = keep.tile([P, 2 * H], BF16, name="wf_bf1_%d" % u, align_bytes=64)
-                nc.vector.tensor_copy(wf_bf[:].rearrange("p (t m j) -> p m t j", t=4, j=4),
-                                      wf_last[u][:].rearrange("p j (m t) -> p m t j", t=4))
+                nc.vector.tensor_copy(wf_bf[:].rearrange("p (t m j) -> p m j t", t=4, j=4),
+                                      wf_last[u][:].rearrange("p j (m t) -> p m j t", t=4))
                 for t in range(4):
                     cols = slice(P * t + 64 * u, P * t + 64 * (u + 1))
                     nc.vector.quantize_mx(wf_codes[:, 1, cols].bitcast(FP8X4), wf_sc[:, 1, cols], wf_bf[:, 256 * t: 256 * (t + 1)])

@@ -50,8 +50,6 @@ def tile_list_wavenet_gate_store_kernel(tc, tab_words, tab_scales, offs, wf, wg_
         nc.sync.dma_start(tab0[:], tab_words[0].rearrange("p t i -> p (t i)").bitcast(I32))
         tab1 = mid.tile([P, T], I32, name="tab1", offset=16 * KB, align_bytes=64)
         nc.sync.dma_start(tab1[:], tab_words[1].rearrange("p t i -> p (t i)").bitcast(I32))
-        gain_sb = keep.tile([P, 4], F32, name="gain_sb")
-        nc.sync.dma_start(gain_sb[:], gain.rearrange("(p t) -> p t", t=4))
         idx2 = lists.tile([P, S // 16], U16, name="idx2")
         nc.sync.dma_start(idx2[:], offs2)
 
@@ -76,9 +74,11 @@ def tile_list_wavenet_gate_store_kernel(tc, tab_words, tab_scales, offs, wf, wg_
         wf_last = [mid.tile([P, 4, H // 2], F32, name="wf_last%d" % u, offset=(8 + 4 * u) * KB) for u in range(2)]
         for u in range(2):
             nc.sync.dma_start(wf_last[u][:], wf[512:1024, 256 * u: 256 * (u + 1)].rearrange("(p j) c -> p j c", j=4))
+        gain_sb = late.tile([P, 4], F32, name="gain_sb", offset=8 * KB)
+        nc.sync.dma_start(gain_sb[:], gain.rearrange("(p t) -> p t", t=4))
         wo_raw = late.tile([P, 4, N], F32, name="wo_raw", offset=0)
         nc.sync.dma_start(wo_raw[:], wo.rearrange("(p j) c -> p j c", j=4))
-        wr_codes = late.tile([P, PASSES, N], I32, name="wr_codes", offset=8 * KB, align_bytes=64)
+        wr_codes = late.tile([P, PASSES, N], I32, name="wr_codes", offset=8 * KB + 64, align_bytes=64)
         nc.sync.dma_start(wr_codes[:], wr_words.rearrange("a p c i -> a p (c i)").bitcast(I32).rearrange("a p c -> p a c"))
 
         v0 = keep.tile([P, S], U32, name="v0", align_bytes=64)
@@ -105,9 +105,8 @@ def tile_list_wavenet_gate_store_kernel(tc, tab_words, tab_scales, offs, wf, wg_
         wf_sc = keep.tile([P, PASSES, H], U8, name="wf_sc", align_bytes=64)
         h_codes = keep.tile([P, S], U32, name="h_codes", align_bytes=64)
         h_sc = keep.tile([P, S], U8, name="h_sc", align_bytes=64)
-        sig = [keep.tile([P, 4, HALF], F32, name="sig%d" % h) for h in range(2)]
+        sig = keep.tile([P, 4, S], F32, name="sig")
         wo_sc = keep.tile([P, N], U8, name="wo_sc", align_bytes=64)
-        gated = []
         wo_codes = []
 
         def gate(h):
@@ -117,7 +116,7 @@ def tile_list_wavenet_gate_store_kernel(tc, tab_words, tab_scales, offs, wf, wg_
                     nc.tensor.matmul_mx(b_ps[:], wg_codes[:, a, 256 * t: 256 * (t + 1)].bitcast(FP4X4),
                                         planes[:, a, S + P * t: S + P * (t + 1)], frames(a, HALF * h, HALF),
                                         planes[:, a, HALF * h: HALF * (h + 1)], start=(a == 0), stop=(a == PASSES - 1))
-                nc.scalar.activation(sig[h][:, t, :], b_ps[:], ACT.Sigmoid)
+                nc.scalar.activation(sig[:, t, HALF * h: HALF * (h + 1)], b_ps[:], ACT.Sigmoid)
 
         def quantise_wf_first():
             wf_bf = [mid.tile([P, 2 * H], BF16, name="wf_bf0_%d" % u, offset=(20 + 2 * u) * KB, align_bytes=64) for u in range(2)]
@@ -131,8 +130,9 @@ def tile_list_wavenet_gate_store_kernel(tc, tab_words, tab_scales, offs, wf, wg_
         def quantise_wf_last():
             for u in range(2):
                 wf_bf = keep.tile([P, 2 * H], BF16, name="wf_bf1_%d" % u, align_bytes=64)
-                nc.vector.tensor_copy(wf_bf[:].rearrange("p (t m j) -> p m j t", t=4, j=4),
-                                      wf_last[u][:].rearrange("p j (m t) -> p m j t", t=4))
+                for w in range(2):
+                    nc.vector.tensor_copy(wf_bf[:, H * w: H * (w + 1)].rearrange("p (t m j) -> p m j t", t=2, j=4),
+                                          wf_last[u][:].rearrange("p j (m t) -> p m j t", t=4)[:, :, :, 2 * w: 2 * w + 2])
                 for t in range(4):
                     cols = slice(P * t + 64 * u, P * t + 64 * (u + 1))
                     nc.vector.quantize_mx(wf_codes[:, 1, cols].bitcast(FP8X4), wf_sc[:, 1, cols], wf_bf[:, 256 * t: 256 * (t + 1)])
@@ -142,7 +142,6 @@ def tile_list_wavenet_gate_store_kernel(tc, tab_words, tab_scales, offs, wf, wg_
             nc.scalar.copy(dst.rearrange("p (c i j) -> p c j i", i=4, j=4), src.rearrange("p j (c i) -> p c j i", i=4))
 
         def hidden(c, order):
-            h = c // CHUNKS
             j0 = CHUNK * c
             cols = slice(j0, j0 + CHUNK)
             a_ps = bank[c]
@@ -153,10 +152,9 @@ def tile_list_wavenet_gate_store_kernel(tc, tab_words, tab_scales, offs, wf, wg_
                                         planes[:, a, cols], start=(a == order[0] and t == 0), stop=(a == order[-1] and t == 3))
             th = stage.tile([P, 4 * CHUNK], F32, name="th%d" % c, tag="th%d" % c, align_bytes=64)
             nc.scalar.activation(th[:], a_ps[:], ACT.Tanh)
-            within = j0 % HALF
             nc.vector.tensor_tensor(h_bf[:, c, :].rearrange("p (c i t) -> p c t i", i=4, t=4),
                                     th[:].rearrange("p (t c i) -> p c t i", t=4, i=4),
-                                    gated[h][:, :, within: within + CHUNK].rearrange("p t (c i) -> p c t i", i=4), MULT)
+                                    gated[:, :, cols].rearrange("p t (c i) -> p c t i", i=4), MULT)
 
         def quantise_h(c):
             pair = slice(CHUNK * c, CHUNK * (c + 2))
@@ -189,14 +187,12 @@ def tile_list_wavenet_gate_store_kernel(tc, tab_words, tab_scales, offs, wf, wg_
         wgo_sb = mid.tile([P, S], F32, name="wgo_sb", offset=0)
         nc.sync.dma_start(wgo_sb[:], wgo)
         quantise_wf_last()
-        gated.append(mid.tile([P, 4, HALF], F32, name="gated0", offset=5 * KB))
-        gated.append(mid.tile([P, 4, HALF], F32, name="gated1", offset=13 * KB))
+        gated = mid.tile([P, 4, S], F32, name="gated", offset=4 * KB)
         for t in range(4):
-            nc.vector.tensor_scalar(gated[0][:, t, :], sig[0][:, t, :], gain_sb[:, t: t + 1], None, MULT)
-        for t in range(2):
-            nc.vector.tensor_scalar(gated[1][:, t, :], sig[1][:, t, :], gain_sb[:, t: t + 1], None, MULT)
+            width = S if t < 2 else HALF
+            nc.vector.tensor_scalar(gated[:, t, 0:width], sig[:, t, 0:width], gain_sb[:, t: t + 1], None, MULT)
         for t in range(2, 4):
-            nc.scalar.activation(gated[1][:, t, :], sig[1][:, t, :], ACT.Copy, scale=gain_sb[:, t: t + 1])
+            nc.scalar.activation(gated[:, t, HALF:], sig[:, t, HALF:], ACT.Copy, scale=gain_sb[:, t: t + 1])
         hidden(0, (0, 1))
         hidden(1, (0, 1))
         hidden(2, (0, 1))

@@ -43,11 +43,11 @@ def tile_list_wavenet_gate_store_kernel(tc, tab_words, tab_scales, offs, wf, wg_
         nc.sync.dma_start(tsc[ROW0:P, :], tab_scales.bitcast(I32).rearrange("a q t -> q a t"))
         wgs_raw = keep.tile([P, H], U8, name="wgs_raw")
         nc.sync.dma_start(wgs_raw[ROW0:P].bitcast(I32), wg_scales.bitcast(I32).rearrange("a q c -> q a c"))
-        rows = late.tile([P, S + H], U8, name="rows", offset=7 * KB)
-        wg_raw = keep.tile([P, PASSES, H // 2], I32, name="wg_raw")
-        nc.sync.dma_start(wg_raw[:], wg_words.bitcast(I32).rearrange("a p c -> p a c"))
+        rows = late.tile([P, S + H], U8, name="rows", offset=7 * KB, align_bytes=64)
         tab0 = mid.tile([P, T], I32, name="tab0", offset=36 * KB, align_bytes=64)
         nc.sync.dma_start(tab0[:], tab_words[0].rearrange("p t i -> p (t i)").bitcast(I32))
+        wg_raw = keep.tile([P, PASSES, H // 2], I32, name="wg_raw")
+        nc.sync.dma_start(wg_raw[:], wg_words.bitcast(I32).rearrange("a p c -> p a c"))
         tab1 = mid.tile([P, T], I32, name="tab1", offset=16 * KB, align_bytes=64)
         nc.sync.dma_start(tab1[:], tab_words[1].rearrange("p t i -> p (t i)").bitcast(I32))
         idx2 = lists.tile([P, S // 16], U16, name="idx2")
@@ -65,9 +65,6 @@ def tile_list_wavenet_gate_store_kernel(tc, tab_words, tab_scales, offs, wf, wg_
         for q in (0, 2, 1, 3):
             nc.sync.dma_start(planes[32 * q: 32 * q + 4].bitcast(I32), rows[ROW0 + 8 * q: ROW0 + 8 * q + 8].bitcast(I32))
         tab = [tab0, tab1]
-        wg_codes = keep.tile([P, PASSES, 2 * H], U8, name="wg_codes", align_bytes=64)
-        nc.vector.tensor_copy(wg_codes[:].bitcast(U16).rearrange("p a (t m) -> p a t m", t=4),
-                              wg_raw[:].bitcast(U16).rearrange("p a (m t) -> p a t m", t=4))
 
         wf_first = mid.tile([P, 4, H], F32, name="wf_first", offset=0)
         nc.sync.dma_start(wf_first[:], wf[0:512, :].rearrange("(p j) c -> p j c", j=4))
@@ -83,19 +80,23 @@ def tile_list_wavenet_gate_store_kernel(tc, tab_words, tab_scales, offs, wf, wg_
 
         v0 = keep.tile([P, S], U32, name="v0", align_bytes=64)
         nc.vector.tensor_copy(v0[:], tab[0][:].bitcast(U32).indirect(idx[:]))
-        wr_sc = mid.tile([P, PASSES, N], U8, name="wr_sc", offset=36 * KB, align_bytes=64)
-        for q in range(4):
-            nc.sync.dma_start(wr_sc[32 * q: 32 * q + 4].bitcast(I32), wr_scales.bitcast(I32)[:, 4 * q: 4 * q + 4, :].rearrange("a r c -> r a c"))
+        wg_codes = keep.tile([P, PASSES, 2 * H], U8, name="wg_codes", align_bytes=64)
+        nc.vector.tensor_copy(wg_codes[:].bitcast(U16).rearrange("p a (t m) -> p a t m", t=4),
+                              wg_raw[:].bitcast(U16).rearrange("p a (m t) -> p a t m", t=4))
+        cache = [keep.tile([P, T], F32, name="cache0", align_bytes=64),
+                 mid.tile([P, T], F32, name="cache1", offset=36 * KB, align_bytes=64)]
+        nc.vector.memset(cache[1][:].bitcast(I32), 0)
         v1 = [keep.tile([P, HALF], U32, name="v1_%d" % h, align_bytes=64) for h in range(2)]
         for h in range(2):
             nc.vector.tensor_copy(v1[h][:], tab[1][:].bitcast(U32).indirect(idx[:, 32 * h: 32 * (h + 1)]))
+        wr_sc = mid.tile([P, PASSES, N], U8, name="wr_sc", offset=24 * KB, align_bytes=64)
+        for q in range(4):
+            nc.sync.dma_start(wr_sc[32 * q: 32 * q + 4].bitcast(I32), wr_scales.bitcast(I32)[:, 4 * q: 4 * q + 4, :].rearrange("a r c -> r a c"))
 
         def frames(a, j0, width):
             if a == 0:
                 return v0[:, j0: j0 + width].bitcast(FP8X4)
             return v1[j0 // HALF][:, j0 % HALF: j0 % HALF + width].bitcast(FP8X4)
-
-        cache = [keep.tile([P, T], F32, name="cache%d" % w, align_bytes=64) for w in range(2)]
 
         def clear(w):
             for c in range(4):
@@ -181,6 +182,9 @@ def tile_list_wavenet_gate_store_kernel(tc, tab_words, tab_scales, offs, wf, wg_
         clear(0)
         warm = keep.tile([P, 1], F32, name="warm")
         nc.scalar.activation(warm[:], cache[0][:, 0:1], ACT.Sigmoid)
+        for k in range(4):
+            nc.tensor.matmul_mx(bank[7][:], wg_codes[:, 0, 0:256].bitcast(FP4X4), rows[:, S: S + P], frames(0, 0, HALF), rows[:, 0:HALF],
+                                start=True, stop=True)
         gate(0)
         gate(1)
         quantise_wf_first()
@@ -223,7 +227,6 @@ def tile_list_wavenet_gate_store_kernel(tc, tab_words, tab_scales, offs, wf, wg_
         nc.vector.quantize_mx(wo_rest[:, 0:P].bitcast(FP8X4), wo_sc[:, P: 2 * P], wo_bf[:, 0: 4 * P])
         nc.vector.quantize_mx(wo_rest[:, P:].bitcast(FP8X4), wo_sc[:, 2 * P:], wo_bf[:, 4 * P:])
         place(0, 1, 1, y01[:])
-        clear(1)
         for n in range(1, 4):
             y = keep.tile([P, S], F32, name="y%d" % n)
             for h in range(2):

@@ -192,9 +192,12 @@ def tile_list_wavenet_gate_store_kernel(tc, tab_words, tab_scales, offs, wf, wg_
         nc.sync.dma_start(wgo_sb[:], wgo)
         quantise_wf_last()
         gated = mid.tile([P, 4, S], F32, name="gated", offset=4 * KB)
-        for t in range(4):
+        for t in (2, 3, 0):
             width = S if t < 2 else HALF
             nc.vector.tensor_scalar(gated[:, t, 0:width], sig[:, t, 0:width], gain_sb[:, t: t + 1], None, MULT)
+        for h in range(2):
+            cols = slice(HALF * h, HALF * (h + 1))
+            nc.vector.tensor_scalar(gated[:, 1, cols], sig[:, 1, cols], gain_sb[:, 1:2], None, MULT)
         for t in range(2, 4):
             nc.scalar.activation(gated[:, t, HALF:], sig[:, t, HALF:], ACT.Copy, scale=gain_sb[:, t: t + 1])
         hidden(0, (0, 1))
@@ -211,8 +214,8 @@ def tile_list_wavenet_gate_store_kernel(tc, tab_words, tab_scales, offs, wf, wg_
         wo_codes.append(wo_first[:])
         nc.vector.quantize_mx(wo_codes[0].bitcast(FP8X4), wo_sc[:, 0:P], wo_bf0[:])
         hidden(6, (1, 0))
-        quantise_h(4)
         hidden(7, (1, 0))
+        quantise_h(4)
         quantise_h(6)
         y00 = stage.tile([P, HALF], F32, name="y00", tag="y00", align_bytes=64)
         project(0, 0, y00[:])

@@ -129,14 +129,14 @@ def tile_list_wavenet_gate_store_kernel(tc, tab_words, tab_scales, offs, wf, wg_
                 nc.vector.quantize_mx(wf_codes[:, 0, cols].bitcast(FP8X4), wf_sc[:, 0, cols], wf_bf[u][:])
 
         def quantise_wf_last():
+            wf_bf = [keep.tile([P, 2, 2, H // 2], BF16, name="wf_bf1_%d" % w, align_bytes=64) for w in range(2)]
             for u in range(2):
-                wf_bf = keep.tile([P, 2 * H], BF16, name="wf_bf1_%d" % u, align_bytes=64)
                 for w in range(2):
-                    nc.vector.tensor_copy(wf_bf[:, H * w: H * (w + 1)].rearrange("p (t m j) -> p m j t", t=2, j=4),
+                    nc.vector.tensor_copy(wf_bf[w][:, :, u, :].rearrange("p t (m j) -> p m j t", j=4),
                                           wf_last[u][:].rearrange("p j (m t) -> p m j t", t=4)[:, :, :, 2 * w: 2 * w + 2])
-                for t in range(4):
-                    cols = slice(P * t + 64 * u, P * t + 64 * (u + 1))
-                    nc.vector.quantize_mx(wf_codes[:, 1, cols].bitcast(FP8X4), wf_sc[:, 1, cols], wf_bf[:, 256 * t: 256 * (t + 1)])
+            for w in range(2):
+                cols = slice(2 * P * w, 2 * P * (w + 1))
+                nc.vector.quantize_mx(wf_codes[:, 1, cols].bitcast(FP8X4), wf_sc[:, 1, cols], wf_bf[w][:].rearrange("p t u c -> p (t u c)"))
 
         def cast_wo(n, dst):
             src = wo_raw[:, :, P * n: P * (n + 1)]
@@ -155,7 +155,7 @@ def tile_list_wavenet_gate_store_kernel(tc, tab_words, tab_scales, offs, wf, wg_
             nc.scalar.activation(th[:], a_ps[:], ACT.Tanh)
             nc.vector.tensor_tensor(h_bf[:, c, :].rearrange("p (c i t) -> p c t i", i=4, t=4),
                                     th[:].rearrange("p (t c i) -> p c t i", t=4, i=4),
-                                    gated[:, :, cols].rearrange("p t (c i) -> p c t i", i=4), MULT)
+                                    gated[c // CHUNKS][:, :, j0 % HALF: j0 % HALF + CHUNK].rearrange("p t (c i) -> p c t i", i=4), MULT)
 
         def quantise_h(c):
             pair = slice(CHUNK * c, CHUNK * (c + 2))
@@ -191,20 +191,16 @@ def tile_list_wavenet_gate_store_kernel(tc, tab_words, tab_scales, offs, wf, wg_
         wgo_sb = mid.tile([P, S], F32, name="wgo_sb", offset=0)
         nc.sync.dma_start(wgo_sb[:], wgo)
         quantise_wf_last()
-        gated = mid.tile([P, 4, S], F32, name="gated", offset=4 * KB)
-        for t in (2, 3, 0):
-            width = S if t < 2 else HALF
-            nc.vector.tensor_scalar(gated[:, t, 0:width], sig[:, t, 0:width], gain_sb[:, t: t + 1], None, MULT)
-        for h in range(2):
-            cols = slice(HALF * h, HALF * (h + 1))
-            nc.vector.tensor_scalar(gated[:, 1, cols], sig[:, 1, cols], gain_sb[:, 1:2], None, MULT)
+        gated = [mid.tile([P, 4, HALF], F32, name="gated%d" % h, offset=(12 - 8 * h) * KB) for h in range(2)]
+        for h, t in ((0, 0), (0, 1), (0, 2), (0, 3), (1, 0), (1, 1)):
+            nc.vector.tensor_scalar(gated[h][:, t, :], sig[:, t, HALF * h: HALF * (h + 1)], gain_sb[:, t: t + 1], None, MULT)
         for t in range(2, 4):
-            nc.scalar.activation(gated[:, t, HALF:], sig[:, t, HALF:], ACT.Copy, scale=gain_sb[:, t: t + 1])
+            nc.scalar.activation(gated[1][:, t, :], sig[:, t, HALF:], ACT.Copy, scale=gain_sb[:, t: t + 1])
         hidden(0, (0, 1))
         hidden(1, (0, 1))
-        hidden(2, (0, 1))
+        hidden(2, (1, 0))
         quantise_h(0)
-        hidden(3, (0, 1))
+        hidden(3, (1, 0))
         hidden(4, (1, 0))
         quantise_h(2)
         hidden(5, (1, 0))
@@ -223,7 +219,7 @@ def tile_list_wavenet_gate_store_kernel(tc, tab_words, tab_scales, offs, wf, wg_
         y01 = keep.tile([P, HALF], F32, name="y01")
         project(0, 1, y01[:])
         wo_bf = stage.tile([P, 3 * 4 * P], BF16, name="wo_bf", tag="th7", align_bytes=64)
-        wo_rest = stage.tile([P, 3 * P], U32, name="wo_rest", tag="y00", align_bytes=64)
+        wo_rest = keep.tile([P, 3 * P], U32, name="wo_rest", align_bytes=64)
         for n in range(1, 4):
             cast_wo(n, wo_bf[:, 4 * P * (n - 1): 4 * P * n])
             wo_codes.append(wo_rest[:, P * (n - 1): P * n])

@@ -21,7 +21,11 @@ PASSES = K // 512
 HALF = S // 2
 CHUNK = 128
 CHUNKS = HALF // CHUNK
-ROW0 = 96
+DENSE = 96
+CLEAR = 1024
+WARM_PASSES = 4
+VECTOR_GAINS = 6
+EARLY_CHUNKS = 2
 KB = 1024
 
 
@@ -40,9 +44,9 @@ def tile_list_wavenet_gate_store_kernel(tc, tab_words, tab_scales, offs, wf, wg_
         idx = lists.tile([P, S // 16], U16, name="idx")
         nc.sync.dma_start(idx[:], offs)
         tsc = mid.tile([P, T // 4], I32, name="tsc", offset=32 * KB, align_bytes=64)
-        nc.sync.dma_start(tsc[ROW0:P, :], tab_scales.bitcast(I32).rearrange("a q t -> q a t"))
+        nc.sync.dma_start(tsc[DENSE:P, :], tab_scales.bitcast(I32).rearrange("a g t -> g a t"))
         wgs_raw = keep.tile([P, H], U8, name="wgs_raw")
-        nc.sync.dma_start(wgs_raw[ROW0:P].bitcast(I32), wg_scales.bitcast(I32).rearrange("a q c -> q a c"))
+        nc.sync.dma_start(wgs_raw[DENSE:P].bitcast(I32), wg_scales.bitcast(I32).rearrange("a g c -> g a c"))
         rows = late.tile([P, S + H], U8, name="rows", offset=7 * KB, align_bytes=64)
         tab0 = mid.tile([P, T], I32, name="tab0", offset=36 * KB, align_bytes=64)
         nc.sync.dma_start(tab0[:], tab_words[0].rearrange("p t i -> p (t i)").bitcast(I32))
@@ -53,8 +57,8 @@ def tile_list_wavenet_gate_store_kernel(tc, tab_words, tab_scales, offs, wf, wg_
         idx2 = lists.tile([P, S // 16], U16, name="idx2")
         nc.sync.dma_start(idx2[:], offs2)
 
-        nc.vector.memset(tsc[0:ROW0, :], 0)
-        nc.vector.memset(wgs_raw[0:ROW0].bitcast(I32), 0)
+        nc.vector.memset(tsc[0:DENSE, :], 0)
+        nc.vector.memset(wgs_raw[0:DENSE].bitcast(I32), 0)
         planes = mid.tile([P, PASSES, S + H], U8, name="planes", offset=32 * KB, align_bytes=64)
 
         picked_bytes = mid.tile([P, 9 * KB], U8, name="picked", offset=7 * KB)
@@ -63,8 +67,7 @@ def tile_list_wavenet_gate_store_kernel(tc, tab_words, tab_scales, offs, wf, wg_
         nc.vector.tensor_copy(rows[:, S: S + H].rearrange("p (t m) -> p t m", t=4), wgs_raw[:].rearrange("p (m t) -> p t m", t=4))
         nc.vector.tensor_copy(rows[:, 0:S].bitcast(I32), picked.bitcast(I32))
         for q in (0, 2, 1, 3):
-            nc.sync.dma_start(planes[32 * q: 32 * q + 4].bitcast(I32), rows[ROW0 + 8 * q: ROW0 + 8 * q + 8].bitcast(I32))
-        tab = [tab0, tab1]
+            nc.sync.dma_start(planes[32 * q: 32 * q + 4].bitcast(I32), rows[DENSE + 8 * q: DENSE + 8 * q + 8].bitcast(I32))
 
         wf_first = mid.tile([P, 4, H], F32, name="wf_first", offset=0)
         nc.sync.dma_start(wf_first[:], wf[0:512, :].rearrange("(p j) c -> p j c", j=4))
@@ -79,16 +82,16 @@ def tile_list_wavenet_gate_store_kernel(tc, tab_words, tab_scales, offs, wf, wg_
         nc.sync.dma_start(wr_codes[:], wr_words.rearrange("a p c i -> a p (c i)").bitcast(I32).rearrange("a p c -> p a c"))
 
         v0 = keep.tile([P, S], U32, name="v0", align_bytes=64)
-        nc.vector.tensor_copy(v0[:], tab[0][:].bitcast(U32).indirect(idx[:]))
+        nc.vector.tensor_copy(v0[:], tab0[:].bitcast(U32).indirect(idx[:]))
         wg_codes = keep.tile([P, PASSES, 2 * H], U8, name="wg_codes", align_bytes=64)
         nc.vector.tensor_copy(wg_codes[:].bitcast(U16).rearrange("p a (t m) -> p a t m", t=4),
                               wg_raw[:].bitcast(U16).rearrange("p a (m t) -> p a t m", t=4))
-        cache = [keep.tile([P, T], F32, name="cache0", align_bytes=64),
-                 mid.tile([P, T], F32, name="cache1", offset=36 * KB, align_bytes=64)]
-        nc.vector.memset(cache[1][:].bitcast(I32), 0)
-        v1 = [keep.tile([P, HALF], U32, name="v1_%d" % h, align_bytes=64) for h in range(2)]
-        for h in range(2):
-            nc.vector.tensor_copy(v1[h][:], tab[1][:].bitcast(U32).indirect(idx[:, 32 * h: 32 * (h + 1)]))
+        window = [keep.tile([P, T], F32, name="window0", align_bytes=64),
+                  mid.tile([P, T], F32, name="window1", offset=36 * KB, align_bytes=64)]
+        nc.vector.memset(window[1][:].bitcast(I32), 0)
+        v1 = [keep.tile([P, HALF], U32, name="v1_%d" % half, align_bytes=64) for half in range(2)]
+        for half in range(2):
+            nc.vector.tensor_copy(v1[half][:], tab1[:].bitcast(U32).indirect(idx[:, 32 * half: 32 * (half + 1)]))
         wr_sc = mid.tile([P, PASSES, N], U8, name="wr_sc", offset=24 * KB, align_bytes=64)
         for q in range(4):
             nc.sync.dma_start(wr_sc[32 * q: 32 * q + 4].bitcast(I32), wr_scales.bitcast(I32)[:, 4 * q: 4 * q + 4, :].rearrange("a r c -> r a c"))
@@ -98,10 +101,6 @@ def tile_list_wavenet_gate_store_kernel(tc, tab_words, tab_scales, offs, wf, wg_
                 return v0[:, j0: j0 + width].bitcast(FP8X4)
             return v1[j0 // HALF][:, j0 % HALF: j0 % HALF + width].bitcast(FP8X4)
 
-        def clear(w):
-            for c in range(4):
-                nc.vector.memset(cache[w][:, 1024 * c: 1024 * (c + 1)].bitcast(I32), 0)
-
         wf_codes = keep.tile([P, PASSES, H], U32, name="wf_codes", align_bytes=64)
         wf_sc = keep.tile([P, PASSES, H], U8, name="wf_sc", align_bytes=64)
         h_codes = keep.tile([P, S], U32, name="h_codes", align_bytes=64)
@@ -110,23 +109,24 @@ def tile_list_wavenet_gate_store_kernel(tc, tab_words, tab_scales, offs, wf, wg_
         wo_sc = keep.tile([P, N], U8, name="wo_sc", align_bytes=64)
         wo_codes = []
 
-        def gate(h):
+        def gate(half):
+            cols = slice(HALF * half, HALF * (half + 1))
             for t in range(4):
-                b_ps = bank[4 * h + t]
+                b_ps = bank[4 * half + t]
                 for a in range(PASSES):
                     nc.tensor.matmul_mx(b_ps[:], wg_codes[:, a, 256 * t: 256 * (t + 1)].bitcast(FP4X4),
-                                        planes[:, a, S + P * t: S + P * (t + 1)], frames(a, HALF * h, HALF),
-                                        planes[:, a, HALF * h: HALF * (h + 1)], start=(a == 0), stop=(a == PASSES - 1))
-                nc.scalar.activation(sig[:, t, HALF * h: HALF * (h + 1)], b_ps[:], ACT.Sigmoid)
+                                        planes[:, a, S + P * t: S + P * (t + 1)], frames(a, HALF * half, HALF),
+                                        planes[:, a, cols], start=(a == 0), stop=(a == PASSES - 1))
+                nc.scalar.activation(sig[:, t, cols], b_ps[:], ACT.Sigmoid)
 
         def quantise_wf_first():
-            wf_bf = [mid.tile([P, 2 * H], BF16, name="wf_bf0_%d" % u, offset=(20 + 2 * u) * KB, align_bytes=64) for u in range(2)]
-            for u in range(2):
-                nc.vector.tensor_copy(wf_bf[u][:].rearrange("p (t m j) -> p m j t", t=2, j=4),
-                                      wf_first[:].rearrange("p j (m t) -> p m j t", t=4)[:, :, :, 2 * u: 2 * u + 2])
-            for u in range(2):
-                cols = slice(2 * P * u, 2 * P * (u + 1))
-                nc.vector.quantize_mx(wf_codes[:, 0, cols].bitcast(FP8X4), wf_sc[:, 0, cols], wf_bf[u][:])
+            wf_bf = [mid.tile([P, 2 * H], BF16, name="wf_bf0_%d" % w, offset=(20 + 2 * w) * KB, align_bytes=64) for w in range(2)]
+            for w in range(2):
+                nc.vector.tensor_copy(wf_bf[w][:].rearrange("p (t m j) -> p m j t", t=2, j=4),
+                                      wf_first[:].rearrange("p j (m t) -> p m j t", t=4)[:, :, :, 2 * w: 2 * w + 2])
+            for w in range(2):
+                cols = slice(2 * P * w, 2 * P * (w + 1))
+                nc.vector.quantize_mx(wf_codes[:, 0, cols].bitcast(FP8X4), wf_sc[:, 0, cols], wf_bf[w][:])
 
         def quantise_wf_last():
             wf_bf = [keep.tile([P, 2, 2, H // 2], BF16, name="wf_bf1_%d" % w, align_bytes=64) for w in range(2)]
@@ -142,47 +142,47 @@ def tile_list_wavenet_gate_store_kernel(tc, tab_words, tab_scales, offs, wf, wg_
             src = wo_raw[:, :, P * n: P * (n + 1)]
             nc.scalar.copy(dst.rearrange("p (c i j) -> p c j i", i=4, j=4), src.rearrange("p j (c i) -> p c j i", i=4))
 
-        def hidden(c, order):
-            j0 = CHUNK * c
+        def hidden(chunk):
+            j0 = CHUNK * chunk
             cols = slice(j0, j0 + CHUNK)
-            a_ps = bank[c]
+            order = (0, 1) if chunk < EARLY_CHUNKS else (1, 0)
+            a_ps = bank[chunk]
             for a in order:
                 for t in range(4):
                     nc.tensor.matmul_mx(a_ps[:, CHUNK * t: CHUNK * (t + 1)], wf_codes[:, a, P * t: P * (t + 1)].bitcast(FP8X4),
                                         wf_sc[:, a, P * t: P * (t + 1)], frames(a, j0, CHUNK),
                                         planes[:, a, cols], start=(a == order[0] and t == 0), stop=(a == order[-1] and t == 3))
-            th = stage.tile([P, 4 * CHUNK], F32, name="th%d" % c, tag="th%d" % c, align_bytes=64)
+            th = stage.tile([P, 4 * CHUNK], F32, name="th%d" % chunk, tag="th%d" % chunk, align_bytes=64)
             nc.scalar.activation(th[:], a_ps[:], ACT.Tanh)
-            nc.vector.tensor_tensor(h_bf[:, c, :].rearrange("p (c i t) -> p c t i", i=4, t=4),
+            nc.vector.tensor_tensor(h_bf[:, chunk, :].rearrange("p (c i t) -> p c t i", i=4, t=4),
                                     th[:].rearrange("p (t c i) -> p c t i", t=4, i=4),
-                                    gated[c // CHUNKS][:, :, j0 % HALF: j0 % HALF + CHUNK].rearrange("p t (c i) -> p c t i", i=4), MULT)
+                                    gated[chunk // CHUNKS][:, :, j0 % HALF: j0 % HALF + CHUNK].rearrange("p t (c i) -> p c t i", i=4), MULT)
 
-        def quantise_h(c):
-            pair = slice(CHUNK * c, CHUNK * (c + 2))
-            nc.vector.quantize_mx(h_codes[:, pair].bitcast(FP8X4), h_sc[:, pair], h_bf[:, c: c + 2, :].rearrange("p c w -> p (c w)"))
+        def quantise_h(chunk):
+            cols = slice(CHUNK * chunk, CHUNK * (chunk + 2))
+            nc.vector.quantize_mx(h_codes[:, cols].bitcast(FP8X4), h_sc[:, cols], h_bf[:, chunk: chunk + 2, :].rearrange("p c w -> p (c w)"))
 
-        def project(n, h, y):
-            cols = slice(HALF * h, HALF * (h + 1))
+        def project(n, half, y):
+            cols = slice(HALF * half, HALF * (half + 1))
             out_rows = slice(P * n, P * (n + 1))
-            y_ps = bank[2 * n + h]
+            y_ps = bank[2 * n + half]
             for a in range(PASSES):
                 nc.tensor.matmul_mx(y_ps[:], wr_codes[:, a, out_rows].bitcast(FP8X4), wr_sc[:, a, out_rows],
-                                    frames(a, HALF * h, HALF), planes[:, a, cols], start=(a == 0), stop=False)
+                                    frames(a, HALF * half, HALF), planes[:, a, cols], start=(a == 0), stop=False)
             nc.tensor.matmul_mx(y_ps[:], wo_codes[n].bitcast(FP8X4), wo_sc[:, out_rows],
                                 h_codes[:, cols].bitcast(FP8X4), h_sc[:, cols], start=False, stop=True)
             nc.scalar.copy(y, y_ps[:])
 
-        def place(n, h, halves, y):
-            nc.vector.tensor_tensor(cache[n % 2][:].indirect(idx2[:, 32 * h: 32 * (h + halves)]),
-                                    y, wgo_sb[:, HALF * h: HALF * (h + halves)], MULT)
-            if h + halves == 2:
-                nc.sync.dma_start(out[P * n: P * (n + 1), :], cache[n % 2][:])
+        def place(n, half, halves, y):
+            nc.vector.tensor_tensor(window[n % 2][:].indirect(idx2[:, 32 * half: 32 * (half + halves)]),
+                                    y, wgo_sb[:, HALF * half: HALF * (half + halves)], MULT)
+            if half + halves == 2:
+                nc.sync.dma_start(out[P * n: P * (n + 1), :], window[n % 2][:])
 
         h_bf = keep.tile([P, 2 * CHUNKS, 4 * CHUNK], BF16, name="h_bf", align_bytes=64)
-        clear(0)
-        warm = keep.tile([P, 1], F32, name="warm")
-        nc.scalar.activation(warm[:], cache[0][:, 0:1], ACT.Sigmoid)
-        for k in range(4):
+        for c0 in range(0, T, CLEAR):
+            nc.vector.memset(window[0][:, c0: c0 + CLEAR].bitcast(I32), 0)
+        for warm_pass in range(WARM_PASSES):
             nc.tensor.matmul_mx(bank[7][:], wg_codes[:, 0, 0:256].bitcast(FP4X4), rows[:, S: S + P], frames(0, 0, HALF), rows[:, 0:HALF],
                                 start=True, stop=True)
         gate(0)
@@ -191,28 +191,34 @@ def tile_list_wavenet_gate_store_kernel(tc, tab_words, tab_scales, offs, wf, wg_
         wgo_sb = mid.tile([P, S], F32, name="wgo_sb", offset=0)
         nc.sync.dma_start(wgo_sb[:], wgo)
         quantise_wf_last()
-        gated = [mid.tile([P, 4, HALF], F32, name="gated%d" % h, offset=(12 - 8 * h) * KB) for h in range(2)]
-        for h, t in ((0, 0), (0, 1), (0, 2), (0, 3), (1, 0), (1, 1)):
-            nc.vector.tensor_scalar(gated[h][:, t, :], sig[:, t, HALF * h: HALF * (h + 1)], gain_sb[:, t: t + 1], None, MULT)
-        for t in range(2, 4):
-            nc.scalar.activation(gated[1][:, t, :], sig[:, t, HALF:], ACT.Copy, scale=gain_sb[:, t: t + 1])
-        hidden(0, (0, 1))
-        hidden(1, (0, 1))
-        hidden(2, (1, 0))
+
+        gated = [mid.tile([P, 4, HALF], F32, name="gated%d" % half, offset=(12 - 8 * half) * KB) for half in range(2)]
+        for tile_no in range(8):
+            half, t = divmod(tile_no, 4)
+            src = sig[:, t, HALF * half: HALF * (half + 1)]
+            if tile_no < VECTOR_GAINS:
+                nc.vector.tensor_scalar(gated[half][:, t, :], src, gain_sb[:, t: t + 1], None, MULT)
+            else:
+                nc.scalar.activation(gated[half][:, t, :], src, ACT.Copy, scale=gain_sb[:, t: t + 1])
+
+        hidden(0)
+        hidden(1)
+        hidden(2)
         quantise_h(0)
-        hidden(3, (1, 0))
-        hidden(4, (1, 0))
+        hidden(3)
+        hidden(4)
         quantise_h(2)
-        hidden(5, (1, 0))
+        hidden(5)
         wo_bf0 = stage.tile([P, 4 * P], BF16, name="wo_bf0", tag="th1", align_bytes=64)
         cast_wo(0, wo_bf0[:])
         wo_first = keep.tile([P, P], U32, name="wo_first", align_bytes=64)
         wo_codes.append(wo_first[:])
         nc.vector.quantize_mx(wo_codes[0].bitcast(FP8X4), wo_sc[:, 0:P], wo_bf0[:])
-        hidden(6, (1, 0))
-        hidden(7, (1, 0))
+        hidden(6)
+        hidden(7)
         quantise_h(4)
         quantise_h(6)
+
         y00 = stage.tile([P, HALF], F32, name="y00", tag="y00", align_bytes=64)
         project(0, 0, y00[:])
         place(0, 0, 1, y00[:])
@@ -228,6 +234,6 @@ def tile_list_wavenet_gate_store_kernel(tc, tab_words, tab_scales, offs, wf, wg_
         place(0, 1, 1, y01[:])
         for n in range(1, 4):
             y = keep.tile([P, S], F32, name="y%d" % n)
-            for h in range(2):
-                project(n, h, y[:, HALF * h: HALF * (h + 1)])
+            for half in range(2):
+                project(n, half, y[:, HALF * half: HALF * (half + 1)])
             place(n, 0, 2, y[:])

@@ -64,7 +64,8 @@ def tile_list_wavenet_gate_store_kernel(tc, tab_words, tab_scales, offs, wf, wg_
         picked_bytes = mid.tile([P, 9 * KB], U8, name="picked", offset=7 * KB)
         picked = picked_bytes[:, 0:S]
         nc.vector.tensor_copy(picked, tsc[:].bitcast(U8).indirect(idx[:]))
-        nc.vector.tensor_copy(rows[:, S: S + H].rearrange("p (t m) -> p t m", t=4), wgs_raw[:].rearrange("p (m t) -> p t m", t=4))
+        nc.vector.tensor_copy(rows[:, S: S + H].bitcast(U16).rearrange("p (t g) -> p t g", t=4),
+                              wgs_raw[:].bitcast(U16).rearrange("p (g t) -> p t g", t=4))
         nc.vector.tensor_copy(rows[:, 0:S].bitcast(I32), picked.bitcast(I32))
         for q in (0, 2, 1, 3):
             nc.sync.dma_start(planes[32 * q: 32 * q + 4].bitcast(I32), rows[DENSE + 8 * q: DENSE + 8 * q + 8].bitcast(I32))
@@ -75,17 +76,20 @@ def tile_list_wavenet_gate_store_kernel(tc, tab_words, tab_scales, offs, wf, wg_
         for u in range(2):
             nc.sync.dma_start(wf_last[u][:], wf[512:1024, 256 * u: 256 * (u + 1)].rearrange("(p j) c -> p j c", j=4))
         gain_sb = late.tile([P, 4], F32, name="gain_sb", offset=8 * KB)
-        nc.sync.dma_start(gain_sb[:], gain.rearrange("(p t) -> p t", t=4))
+        for i in range(2):
+            with nc.allow_non_contiguous_dma(reason="one gain for each partition and channel tile"):
+                nc.sync.dma_start(gain_sb[i:P:2, :], gain.rearrange("(g t i) -> i g t", t=4, i=2)[i])
         wo_raw = late.tile([P, 4, N], F32, name="wo_raw", offset=0)
-        nc.sync.dma_start(wo_raw[:], wo.rearrange("(p j) c -> p j c", j=4))
+        for t in range(4):
+            nc.sync.dma_start(wo_raw[:, t, :], wo.rearrange("(g t i) c -> t g i c", t=4, i=2)[t])
         wr_codes = late.tile([P, PASSES, N], I32, name="wr_codes", offset=8 * KB + 64, align_bytes=64)
         nc.sync.dma_start(wr_codes[:], wr_words.rearrange("a p c i -> a p (c i)").bitcast(I32).rearrange("a p c -> p a c"))
 
         v0 = keep.tile([P, S], U32, name="v0", align_bytes=64)
         nc.vector.tensor_copy(v0[:], tab0[:].bitcast(U32).indirect(idx[:]))
         wg_codes = keep.tile([P, PASSES, 2 * H], U8, name="wg_codes", align_bytes=64)
-        nc.vector.tensor_copy(wg_codes[:].bitcast(U16).rearrange("p a (t m) -> p a t m", t=4),
-                              wg_raw[:].bitcast(U16).rearrange("p a (m t) -> p a t m", t=4))
+        nc.vector.tensor_copy(wg_codes[:].bitcast(I32).rearrange("p a (t g) -> p a t g", t=4),
+                              wg_raw[:].rearrange("p a (g t) -> p a t g", t=4))
         window = [keep.tile([P, T], F32, name="window0", align_bytes=64),
                   mid.tile([P, T], F32, name="window1", offset=36 * KB, align_bytes=64)]
         nc.vector.memset(window[1][:].bitcast(I32), 0)
@@ -122,8 +126,8 @@ def tile_list_wavenet_gate_store_kernel(tc, tab_words, tab_scales, offs, wf, wg_
         def quantise_wf_first():
             wf_bf = [mid.tile([P, 2 * H], BF16, name="wf_bf0_%d" % w, offset=(20 + 2 * w) * KB, align_bytes=64) for w in range(2)]
             for w in range(2):
-                nc.vector.tensor_copy(wf_bf[w][:].rearrange("p (t m j) -> p m j t", t=2, j=4),
-                                      wf_first[:].rearrange("p j (m t) -> p m j t", t=4)[:, :, :, 2 * w: 2 * w + 2])
+                nc.vector.tensor_copy(wf_bf[w][:].rearrange("p (t g i j) -> p g j t i", t=2, i=2, j=4),
+                                      wf_first[:].rearrange("p j (g t i) -> p g j t i", t=4, i=2)[:, :, :, 2 * w: 2 * w + 2])
             for w in range(2):
                 cols = slice(2 * P * w, 2 * P * (w + 1))
                 nc.vector.quantize_mx(wf_codes[:, 0, cols].bitcast(FP8X4), wf_sc[:, 0, cols], wf_bf[w][:])
@@ -132,8 +136,8 @@ def tile_list_wavenet_gate_store_kernel(tc, tab_words, tab_scales, offs, wf, wg_
             wf_bf = [keep.tile([P, 2, 2, H // 2], BF16, name="wf_bf1_%d" % w, align_bytes=64) for w in range(2)]
             for u in range(2):
                 for w in range(2):
-                    nc.vector.tensor_copy(wf_bf[w][:, :, u, :].rearrange("p t (m j) -> p m j t", j=4),
-                                          wf_last[u][:].rearrange("p j (m t) -> p m j t", t=4)[:, :, :, 2 * w: 2 * w + 2])
+                    nc.vector.tensor_copy(wf_bf[w][:, :, u, :].rearrange("p t (g i j) -> p g j t i", i=2, j=4),
+                                          wf_last[u][:].rearrange("p j (g t i) -> p g j t i", t=4, i=2)[:, :, :, 2 * w: 2 * w + 2])
             for w in range(2):
                 cols = slice(2 * P * w, 2 * P * (w + 1))
                 nc.vector.quantize_mx(wf_codes[:, 1, cols].bitcast(FP8X4), wf_sc[:, 1, cols], wf_bf[w][:].rearrange("p t u c -> p (t u c)"))

@@ -54,8 +54,6 @@ def tile_list_wavenet_gate_store_kernel(tc, tab_words, tab_scales, offs, wf, wg_
         nc.sync.dma_start(wg_raw[:], wg_words.bitcast(I32).rearrange("a p c -> p a c"))
         tab1 = mid.tile([P, T], I32, name="tab1", offset=16 * KB, align_bytes=64)
         nc.sync.dma_start(tab1[:], tab_words[1].rearrange("p t i -> p (t i)").bitcast(I32))
-        idx2 = lists.tile([P, S // 16], U16, name="idx2")
-        nc.sync.dma_start(idx2[:], offs2)
 
         nc.vector.memset(tsc[0:DENSE, :], 0)
         nc.vector.memset(wgs_raw[0:DENSE].bitcast(I32), 0)
@@ -194,6 +192,8 @@ def tile_list_wavenet_gate_store_kernel(tc, tab_words, tab_scales, offs, wf, wg_
         quantise_wf_first()
         wgo_sb = mid.tile([P, S], F32, name="wgo_sb", offset=0)
         nc.sync.dma_start(wgo_sb[:], wgo)
+        idx2 = lists.tile([P, S // 16], U16, name="idx2")
+        nc.sync.dma_start(idx2[:], offs2)
         quantise_wf_last()
 
         gated = [mid.tile([P, 4, HALF], F32, name="gated%d" % half, offset=(12 - 8 * half) * KB) for half in range(2)]

@@ -52,6 +52,9 @@ def tile_list_wavenet_gate_store_kernel(tc, tab_words, tab_scales, offs, wf, wg_
         nc.sync.dma_start(tab0[:], tab_words[0].rearrange("p t i -> p (t i)").bitcast(I32))
         wg_raw = keep.tile([P, PASSES, H // 2], I32, name="wg_raw")
         nc.sync.dma_start(wg_raw[:], wg_words.bitcast(I32).rearrange("a p c -> p a c"))
+        gain_sb = keep.tile([P, 7], F32, name="gain_sb")
+        for i in range(2):
+            nc.sync.dma_start(gain_sb[i:P:2, :], gain.rearrange("(g e) -> g e", e=8)[:, i: i + 7])
         tab1 = mid.tile([P, T], I32, name="tab1", offset=16 * KB, align_bytes=64)
         nc.sync.dma_start(tab1[:], tab_words[1].rearrange("p t i -> p (t i)").bitcast(I32))
 
@@ -73,10 +76,6 @@ def tile_list_wavenet_gate_store_kernel(tc, tab_words, tab_scales, offs, wf, wg_
         wf_last = [mid.tile([P, 4, H // 2], F32, name="wf_last%d" % u, offset=(8 + 4 * u) * KB) for u in range(2)]
         for u in range(2):
             nc.sync.dma_start(wf_last[u][:], wf[512:1024, 256 * u: 256 * (u + 1)].rearrange("(p j) c -> p j c", j=4))
-        gain_sb = late.tile([P, 4], F32, name="gain_sb", offset=8 * KB)
-        for i in range(2):
-            with nc.allow_non_contiguous_dma(reason="one gain for each partition and channel tile"):
-                nc.sync.dma_start(gain_sb[i:P:2, :], gain.rearrange("(g t i) -> i g t", t=4, i=2)[i])
         wo_raw = late.tile([P, 4, N], F32, name="wo_raw", offset=0)
         for t in range(4):
             nc.sync.dma_start(wo_raw[:, t, :], wo.rearrange("(g t i) c -> t g i c", t=4, i=2)[t])
@@ -201,9 +200,9 @@ def tile_list_wavenet_gate_store_kernel(tc, tab_words, tab_scales, offs, wf, wg_
             half, t = divmod(tile_no, 4)
             src = sig[:, t, HALF * half: HALF * (half + 1)]
             if tile_no < VECTOR_GAINS:
-                nc.vector.tensor_scalar(gated[half][:, t, :], src, gain_sb[:, t: t + 1], None, MULT)
+                nc.vector.tensor_scalar(gated[half][:, t, :], src, gain_sb[:, 2 * t: 2 * t + 1], None, MULT)
             else:
-                nc.scalar.activation(gated[half][:, t, :], src, ACT.Copy, scale=gain_sb[:, t: t + 1])
+                nc.scalar.activation(gated[half][:, t, :], src, ACT.Copy, scale=gain_sb[:, 2 * t: 2 * t + 1])
 
         hidden(0)
         hidden(1)

@@ -23,7 +23,8 @@ CHUNK = 128
 CHUNKS = HALF // CHUNK
 DENSE = 96
 CLEAR = 1024
-WARM_PASSES = 4
+WARM_EARLY = 3
+WARM_LATE = 2
 VECTOR_GAINS = 6
 EARLY_CHUNKS = 2
 KB = 1024
@@ -121,7 +122,7 @@ def tile_list_wavenet_gate_store_kernel(tc, tab_words, tab_scales, offs, wf, wg_
                 nc.scalar.activation(sig[:, t, cols], b_ps[:], ACT.Sigmoid)
 
         def quantise_wf_first():
-            wf_bf = [mid.tile([P, 2 * H], BF16, name="wf_bf0_%d" % w, offset=(20 + 2 * w) * KB, align_bytes=64) for w in range(2)]
+            wf_bf = [keep.tile([P, 2 * H], BF16, name="wf_bf0_%d" % w, align_bytes=64) for w in range(2)]
             for w in range(2):
                 nc.vector.tensor_copy(wf_bf[w][:].rearrange("p (t g i j) -> p g j t i", t=2, i=2, j=4),
                                       wf_first[:].rearrange("p j (g t i) -> p g j t i", t=4, i=2)[:, :, :, 2 * w: 2 * w + 2])
@@ -183,8 +184,8 @@ def tile_list_wavenet_gate_store_kernel(tc, tab_words, tab_scales, offs, wf, wg_
         h_bf = keep.tile([P, 2 * CHUNKS, 4 * CHUNK], BF16, name="h_bf", align_bytes=64)
         for c0 in range(0, T, CLEAR):
             nc.vector.memset(window[0][:, c0: c0 + CLEAR].bitcast(I32), 0)
-        for warm_pass in range(WARM_PASSES):
-            nc.tensor.matmul_mx(bank[7][:], wg_codes[:, 0, 0:256].bitcast(FP4X4), rows[:, S: S + P], frames(0, 0, HALF), rows[:, 0:HALF],
+        for moving in [frames(0, 0, HALF)] * WARM_EARLY + [tab1[:, 0:HALF].bitcast(FP8X4)] * WARM_LATE:
+            nc.tensor.matmul_mx(bank[7][:], wg_codes[:, 0, 0:256].bitcast(FP4X4), rows[:, S: S + P], moving, rows[:, 0:HALF],
                                 start=True, stop=True)
         gate(0)
         gate(1)

@@ -28,6 +28,7 @@ WARM_LATE = 2
 VECTOR_GAINS = 6
 EARLY_CHUNKS = 2
 KB = 1024
+ALIGN = 256
 
 
 def tile_list_wavenet_gate_store_kernel(tc, tab_words, tab_scales, offs, wf, wg_words, wg_scales, gain, wo,
@@ -44,19 +45,19 @@ def tile_list_wavenet_gate_store_kernel(tc, tab_words, tab_scales, offs, wf, wg_
 
         idx = lists.tile([P, S // 16], U16, name="idx")
         nc.sync.dma_start(idx[:], offs)
-        tsc = mid.tile([P, T // 4], I32, name="tsc", offset=32 * KB, align_bytes=64)
+        tsc = mid.tile([P, T // 4], I32, name="tsc", offset=32 * KB, align_bytes=ALIGN)
         nc.sync.dma_start(tsc[DENSE:P, :], tab_scales.bitcast(I32).rearrange("a g t -> g a t"))
-        wgs_raw = keep.tile([P, H], U8, name="wgs_raw")
+        wgs_raw = keep.tile([P, H], U8, name="wgs_raw", align_bytes=ALIGN)
         nc.sync.dma_start(wgs_raw[DENSE:P].bitcast(I32), wg_scales.bitcast(I32).rearrange("a g c -> g a c"))
-        rows = late.tile([P, S + H], U8, name="rows", offset=7 * KB, align_bytes=64)
-        tab0 = mid.tile([P, T], I32, name="tab0", offset=36 * KB, align_bytes=64)
+        rows = late.tile([P, S + H], U8, name="rows", offset=7 * KB, align_bytes=ALIGN)
+        tab0 = mid.tile([P, T], I32, name="tab0", offset=36 * KB, align_bytes=ALIGN)
         nc.sync.dma_start(tab0[:], tab_words[0].rearrange("p t i -> p (t i)").bitcast(I32))
-        wg_raw = keep.tile([P, PASSES, H // 2], I32, name="wg_raw")
+        wg_raw = keep.tile([P, PASSES, H // 2], I32, name="wg_raw", align_bytes=ALIGN)
         nc.sync.dma_start(wg_raw[:], wg_words.bitcast(I32).rearrange("a p c -> p a c"))
         gain_sb = keep.tile([P, 7], F32, name="gain_sb")
         for i in range(2):
             nc.sync.dma_start(gain_sb[i:P:2, :], gain.rearrange("(g e) -> g e", e=8)[:, i: i + 7])
-        tab1 = mid.tile([P, T], I32, name="tab1", offset=16 * KB, align_bytes=64)
+        tab1 = mid.tile([P, T], I32, name="tab1", offset=16 * KB, align_bytes=ALIGN)
         nc.sync.dma_start(tab1[:], tab_words[1].rearrange("p t i -> p (t i)").bitcast(I32))
 
         nc.vector.memset(tsc[0:DENSE, :], 0)
@@ -80,7 +81,7 @@ def tile_list_wavenet_gate_store_kernel(tc, tab_words, tab_scales, offs, wf, wg_
         wo_raw = late.tile([P, 4, N], F32, name="wo_raw", offset=0)
         for t in range(4):
             nc.sync.dma_start(wo_raw[:, t, :], wo.rearrange("(g t i) c -> t g i c", t=4, i=2)[t])
-        wr_codes = late.tile([P, PASSES, N], I32, name="wr_codes", offset=8 * KB + 64, align_bytes=64)
+        wr_codes = late.tile([P, PASSES, N], I32, name="wr_codes", offset=8 * KB + ALIGN, align_bytes=ALIGN)
         nc.sync.dma_start(wr_codes[:], wr_words.rearrange("a p c i -> a p (c i)").bitcast(I32).rearrange("a p c -> p a c"))
 
         v0 = keep.tile([P, S], U32, name="v0", align_bytes=64)
@@ -88,8 +89,8 @@ def tile_list_wavenet_gate_store_kernel(tc, tab_words, tab_scales, offs, wf, wg_
         wg_codes = keep.tile([P, PASSES, 2 * H], U8, name="wg_codes", align_bytes=64)
         nc.vector.tensor_copy(wg_codes[:].bitcast(I32).rearrange("p a (t g) -> p a t g", t=4),
                               wg_raw[:].rearrange("p a (g t) -> p a t g", t=4))
-        window = [keep.tile([P, T], F32, name="window0", align_bytes=64),
-                  mid.tile([P, T], F32, name="window1", offset=36 * KB, align_bytes=64)]
+        window = [keep.tile([P, T], F32, name="window0", align_bytes=ALIGN),
+                  mid.tile([P, T], F32, name="window1", offset=36 * KB, align_bytes=ALIGN)]
         nc.vector.memset(window[1][:].bitcast(I32), 0)
         v1 = [keep.tile([P, HALF], U32, name="v1_%d" % half, align_bytes=64) for half in range(2)]
         for half in range(2):

@@ -62,7 +62,7 @@ def tile_list_wavenet_gate_store_kernel(tc, tab_words, tab_scales, offs, wf, wg_
 
         nc.vector.memset(tsc[0:DENSE, :], 0)
         nc.vector.memset(wgs_raw[0:DENSE].bitcast(I32), 0)
-        planes = mid.tile([P, PASSES, S + H], U8, name="planes", offset=32 * KB, align_bytes=64)
+        planes = mid.tile([P, PASSES, S + H], U8, name="planes", offset=32 * KB, align_bytes=ALIGN)
 
         picked_bytes = mid.tile([P, 9 * KB], U8, name="picked", offset=7 * KB)
         picked = picked_bytes[:, 0:S]
@@ -84,18 +84,18 @@ def tile_list_wavenet_gate_store_kernel(tc, tab_words, tab_scales, offs, wf, wg_
         wr_codes = late.tile([P, PASSES, N], I32, name="wr_codes", offset=8 * KB + ALIGN, align_bytes=ALIGN)
         nc.sync.dma_start(wr_codes[:], wr_words.rearrange("a p c i -> a p (c i)").bitcast(I32).rearrange("a p c -> p a c"))
 
-        v0 = keep.tile([P, S], U32, name="v0", align_bytes=64)
+        v0 = keep.tile([P, S], U32, name="v0", align_bytes=ALIGN)
         nc.vector.tensor_copy(v0[:], tab0[:].bitcast(U32).indirect(idx[:]))
-        wg_codes = keep.tile([P, PASSES, 2 * H], U8, name="wg_codes", align_bytes=64)
+        wg_codes = keep.tile([P, PASSES, 2 * H], U8, name="wg_codes", align_bytes=ALIGN)
         nc.vector.tensor_copy(wg_codes[:].bitcast(I32).rearrange("p a (t g) -> p a t g", t=4),
                               wg_raw[:].rearrange("p a (g t) -> p a t g", t=4))
         window = [keep.tile([P, T], F32, name="window0", align_bytes=ALIGN),
                   mid.tile([P, T], F32, name="window1", offset=36 * KB, align_bytes=ALIGN)]
         nc.vector.memset(window[1][:].bitcast(I32), 0)
-        v1 = [keep.tile([P, HALF], U32, name="v1_%d" % half, align_bytes=64) for half in range(2)]
+        v1 = [keep.tile([P, HALF], U32, name="v1_%d" % half, align_bytes=ALIGN) for half in range(2)]
         for half in range(2):
             nc.vector.tensor_copy(v1[half][:], tab1[:].bitcast(U32).indirect(idx[:, 32 * half: 32 * (half + 1)]))
-        wr_sc = mid.tile([P, PASSES, N], U8, name="wr_sc", offset=24 * KB, align_bytes=64)
+        wr_sc = mid.tile([P, PASSES, N], U8, name="wr_sc", offset=24 * KB, align_bytes=ALIGN)
         for q in range(4):
             nc.sync.dma_start(wr_sc[32 * q: 32 * q + 4].bitcast(I32), wr_scales.bitcast(I32)[:, 4 * q: 4 * q + 4, :].rearrange("a r c -> r a c"))
 
@@ -104,12 +104,12 @@ def tile_list_wavenet_gate_store_kernel(tc, tab_words, tab_scales, offs, wf, wg_
                 return v0[:, j0: j0 + width].bitcast(FP8X4)
             return v1[j0 // HALF][:, j0 % HALF: j0 % HALF + width].bitcast(FP8X4)
 
-        wf_codes = keep.tile([P, PASSES, H], U32, name="wf_codes", align_bytes=64)
-        wf_sc = keep.tile([P, PASSES, H], U8, name="wf_sc", align_bytes=64)
-        h_codes = keep.tile([P, S], U32, name="h_codes", align_bytes=64)
-        h_sc = keep.tile([P, S], U8, name="h_sc", align_bytes=64)
+        wf_codes = keep.tile([P, PASSES, H], U32, name="wf_codes", align_bytes=ALIGN)
+        wf_sc = keep.tile([P, PASSES, H], U8, name="wf_sc", align_bytes=ALIGN)
+        h_codes = keep.tile([P, S], U32, name="h_codes", align_bytes=ALIGN)
+        h_sc = keep.tile([P, S], U8, name="h_sc", align_bytes=ALIGN)
         sig = keep.tile([P, 4, S], F32, name="sig")
-        wo_sc = keep.tile([P, N], U8, name="wo_sc", align_bytes=64)
+        wo_sc = keep.tile([P, N], U8, name="wo_sc", align_bytes=ALIGN)
         wo_codes = []
 
         def gate(half):
@@ -123,7 +123,7 @@ def tile_list_wavenet_gate_store_kernel(tc, tab_words, tab_scales, offs, wf, wg_
                 nc.scalar.activation(sig[:, t, cols], b_ps[:], ACT.Sigmoid)
 
         def quantise_wf_first():
-            wf_bf = [keep.tile([P, 2 * H], BF16, name="wf_bf0_%d" % w, align_bytes=64) for w in range(2)]
+            wf_bf = [keep.tile([P, 2 * H], BF16, name="wf_bf0_%d" % w, align_bytes=ALIGN) for w in range(2)]
             for w in range(2):
                 nc.vector.tensor_copy(wf_bf[w][:].rearrange("p (t g i j) -> p g j t i", t=2, i=2, j=4),
                                       wf_first[:].rearrange("p j (g t i) -> p g j t i", t=4, i=2)[:, :, :, 2 * w: 2 * w + 2])
@@ -132,7 +132,7 @@ def tile_list_wavenet_gate_store_kernel(tc, tab_words, tab_scales, offs, wf, wg_
                 nc.vector.quantize_mx(wf_codes[:, 0, cols].bitcast(FP8X4), wf_sc[:, 0, cols], wf_bf[w][:])
 
         def quantise_wf_last():
-            wf_bf = [keep.tile([P, 2, 2, H // 2], BF16, name="wf_bf1_%d" % w, align_bytes=64) for w in range(2)]
+            wf_bf = [keep.tile([P, 2, 2, H // 2], BF16, name="wf_bf1_%d" % w, align_bytes=ALIGN) for w in range(2)]
             for u in range(2):
                 for w in range(2):
                     nc.vector.tensor_copy(wf_bf[w][:, :, u, :].rearrange("p t (g i j) -> p g j t i", i=2, j=4),
@@ -155,7 +155,7 @@ def tile_list_wavenet_gate_store_kernel(tc, tab_words, tab_scales, offs, wf, wg_
                     nc.tensor.matmul_mx(a_ps[:, CHUNK * t: CHUNK * (t + 1)], wf_codes[:, a, P * t: P * (t + 1)].bitcast(FP8X4),
                                         wf_sc[:, a, P * t: P * (t + 1)], frames(a, j0, CHUNK),
                                         planes[:, a, cols], start=(a == order[0] and t == 0), stop=(a == order[-1] and t == 3))
-            th = stage.tile([P, 4 * CHUNK], F32, name="th%d" % chunk, tag="th%d" % chunk, align_bytes=64)
+            th = stage.tile([P, 4 * CHUNK], F32, name="th%d" % chunk, tag="th%d" % chunk, align_bytes=ALIGN)
             nc.scalar.activation(th[:], a_ps[:], ACT.Tanh)
             nc.vector.tensor_tensor(h_bf[:, chunk, :].rearrange("p (c i t) -> p c t i", i=4, t=4),
                                     th[:].rearrange("p (t c i) -> p c t i", t=4, i=4),
@@ -182,7 +182,7 @@ def tile_list_wavenet_gate_store_kernel(tc, tab_words, tab_scales, offs, wf, wg_
             if half + halves == 2:
                 nc.sync.dma_start(out[P * n: P * (n + 1), :], window[n % 2][:])
 
-        h_bf = keep.tile([P, 2 * CHUNKS, 4 * CHUNK], BF16, name="h_bf", align_bytes=64)
+        h_bf = keep.tile([P, 2 * CHUNKS, 4 * CHUNK], BF16, name="h_bf", align_bytes=ALIGN)
         for c0 in range(0, T, CLEAR):
             nc.vector.memset(window[0][:, c0: c0 + CLEAR].bitcast(I32), 0)
         for moving in [frames(0, 0, HALF)] * WARM_EARLY + [tab1[:, 0:HALF].bitcast(FP8X4)] * WARM_LATE:
@@ -214,9 +214,9 @@ def tile_list_wavenet_gate_store_kernel(tc, tab_words, tab_scales, offs, wf, wg_
         hidden(4)
         quantise_h(2)
         hidden(5)
-        wo_bf0 = stage.tile([P, 4 * P], BF16, name="wo_bf0", tag="th1", align_bytes=64)
+        wo_bf0 = stage.tile([P, 4 * P], BF16, name="wo_bf0", tag="th1", align_bytes=ALIGN)
         cast_wo(0, wo_bf0[:])
-        wo_first = keep.tile([P, P], U32, name="wo_first", align_bytes=64)
+        wo_first = keep.tile([P, P], U32, name="wo_first", align_bytes=ALIGN)
         wo_codes.append(wo_first[:])
         nc.vector.quantize_mx(wo_codes[0].bitcast(FP8X4), wo_sc[:, 0:P], wo_bf0[:])
         hidden(6)
@@ -224,13 +224,13 @@ def tile_list_wavenet_gate_store_kernel(tc, tab_words, tab_scales, offs, wf, wg_
         quantise_h(4)
         quantise_h(6)
 
-        y00 = stage.tile([P, HALF], F32, name="y00", tag="y00", align_bytes=64)
+        y00 = stage.tile([P, HALF], F32, name="y00", tag="y00", align_bytes=ALIGN)
         project(0, 0, y00[:])
         place(0, 0, 1, y00[:])
         y01 = keep.tile([P, HALF], F32, name="y01")
         project(0, 1, y01[:])
-        wo_bf = stage.tile([P, 3 * 4 * P], BF16, name="wo_bf", tag="th7", align_bytes=64)
-        wo_rest = keep.tile([P, 3 * P], U32, name="wo_rest", align_bytes=64)
+        wo_bf = stage.tile([P, 3 * 4 * P], BF16, name="wo_bf", tag="th7", align_bytes=ALIGN)
+        wo_rest = keep.tile([P, 3 * P], U32, name="wo_rest", align_bytes=ALIGN)
         for n in range(1, 4):
             cast_wo(n, wo_bf[:, 4 * P * (n - 1): 4 * P * n])
             wo_codes.append(wo_rest[:, P * (n - 1): P * n])

from contextlib import ExitStack

import concourse.mybir as mybir

K, H, N, T, S = 1024, 512, 512, 4096, 1024
FLOPS = 2 * S * (2 * K * H + H * N + K * N)

F32 = mybir.dt.float32
BF16 = mybir.dt.bfloat16
I32 = mybir.dt.int32
U32 = mybir.dt.uint32
U16 = mybir.dt.uint16
U8 = mybir.dt.uint8
FP8X4 = mybir.dt.float8_e4m3fn_x4
FP4X4 = mybir.dt.float4_e2m1fn_x4
ACT = mybir.ActivationFunctionType
MULT = mybir.AluOpType.mult

P = 128
PASSES = K // 512
HALF = S // 2
CHUNK = 128
CHUNKS = HALF // CHUNK
DENSE = 96
CLEAR = 1024
WARM_EARLY = 3
WARM_LATE = 2
VECTOR_GAINS = 6
EARLY_CHUNKS = 2
KB = 1024
ALIGN = 256


def tile_list_wavenet_gate_store_kernel(tc, tab_words, tab_scales, offs, wf, wg_words, wg_scales, gain, wo,
                                                 wr_words, wr_scales, wgo, offs2, out):
    nc = tc.nc
    with ExitStack() as ctx:
        lists = ctx.enter_context(tc.tile_pool(name="lists", bufs=1))
        keep = ctx.enter_context(tc.tile_pool(name="keep", bufs=1))
        stage = ctx.enter_context(tc.tile_pool(name="stage", bufs=1))
        mid = ctx.enter_context(tc.tile_pool(name="mid", bufs=1))
        late = ctx.enter_context(tc.tile_pool(name="late", bufs=1))
        psum = ctx.enter_context(tc.psum_pool(name="psum", bufs=1))
        bank = [psum.tile([P, 512], F32, name="bank%d" % b) for b in range(8)]

        idx = lists.tile([P, S // 16], U16, name="idx")
        nc.sync.dma_start(idx[:], offs)
        tsc = mid.tile([P, T // 4], I32, name="tsc", offset=32 * KB, align_bytes=ALIGN)
        nc.sync.dma_start(tsc[DENSE:P, :], tab_scales.bitcast(I32).rearrange("a g t -> g a t"))
        wgs_raw = keep.tile([P, H], U8, name="wgs_raw", align_bytes=ALIGN)
        nc.sync.dma_start(wgs_raw[DENSE:P].bitcast(I32), wg_scales.bitcast(I32).rearrange("a g c -> g a c"))
        rows = late.tile([P, S + H], U8, name="rows", offset=7 * KB, align_bytes=ALIGN)
        tab0 = mid.tile([P, T], I32, name="tab0", offset=36 * KB, align_bytes=ALIGN)
        nc.sync.dma_start(tab0[:], tab_words[0].rearrange("p t i -> p (t i)").bitcast(I32))
        wg_raw = keep.tile([P, PASSES, H // 2], I32, name="wg_raw", align_bytes=ALIGN)
        nc.sync.dma_start(wg_raw[:], wg_words.bitcast(I32).rearrange("a p c -> p a c"))
        gain_sb = keep.tile([P, 7], F32, name="gain_sb")
        for i in range(2):
            nc.sync.dma_start(gain_sb[i:P:2, :], gain.rearrange("(g e) -> g e", e=8)[:, i: i + 7])
        tab1 = mid.tile([P, T], I32, name="tab1", offset=16 * KB, align_bytes=ALIGN)
        nc.sync.dma_start(tab1[:], tab_words[1].rearrange("p t i -> p (t i)").bitcast(I32))

        nc.vector.memset(tsc[0:DENSE, :], 0)
        nc.vector.memset(wgs_raw[0:DENSE].bitcast(I32), 0)
        planes = mid.tile([P, PASSES, S + H], U8, name="planes", offset=32 * KB, align_bytes=ALIGN)

        picked_bytes = mid.tile([P, 9 * KB], U8, name="picked", offset=7 * KB)
        picked = picked_bytes[:, 0:S]
        nc.vector.tensor_copy(picked, tsc[:].bitcast(U8).indirect(idx[:]))
        nc.vector.tensor_copy(rows[:, S: S + H].bitcast(U16).rearrange("p (t g) -> p t g", t=4),
                              wgs_raw[:].bitcast(U16).rearrange("p (g t) -> p t g", t=4))
        nc.vector.tensor_copy(rows[:, 0:S].bitcast(I32), picked.bitcast(I32))
        for q in (0, 2, 1, 3):
            nc.sync.dma_start(planes[32 * q: 32 * q + 4].bitcast(I32), rows[DENSE + 8 * q: DENSE + 8 * q + 8].bitcast(I32))

        wf_first = mid.tile([P, 4, H], F32, name="wf_first", offset=0)
        nc.sync.dma_start(wf_first[:], wf[0:512, :].rearrange("(p j) c -> p j c", j=4))
        wf_last = [mid.tile([P, 4, H // 2], F32, name="wf_last%d" % u, offset=(8 + 4 * u) * KB) for u in range(2)]
        for u in range(2):
            nc.sync.dma_start(wf_last[u][:], wf[512:1024, 256 * u: 256 * (u + 1)].rearrange("(p j) c -> p j c", j=4))
        wo_raw = late.tile([P, 4, N], F32, name="wo_raw", offset=0)
        for t in range(4):
            nc.sync.dma_start(wo_raw[:, t, :], wo.rearrange("(g t i) c -> t g i c", t=4, i=2)[t])
        wr_codes = late.tile([P, PASSES, N], I32, name="wr_codes", offset=8 * KB + ALIGN, align_bytes=ALIGN)
        nc.sync.dma_start(wr_codes[:], wr_words.rearrange("a p c i -> a p (c i)").bitcast(I32).rearrange("a p c -> p a c"))

        v0 = keep.tile([P, S], U32, name="v0", align_bytes=ALIGN)
        nc.vector.tensor_copy(v0[:], tab0[:].bitcast(U32).indirect(idx[:]))
        wg_codes = keep.tile([P, PASSES, 2 * H], U8, name="wg_codes", align_bytes=ALIGN)
        nc.vector.tensor_copy(wg_codes[:].bitcast(I32).rearrange("p a (t g) -> p a t g", t=4),
                              wg_raw[:].rearrange("p a (g t) -> p a t g", t=4))
        window = [keep.tile([P, T], F32, name="window0", align_bytes=ALIGN),
                  mid.tile([P, T], F32, name="window1", offset=36 * KB, align_bytes=ALIGN)]
        nc.vector.memset(window[1][:].bitcast(I32), 0)
        v1 = [keep.tile([P, HALF], U32, name="v1_%d" % half, align_bytes=ALIGN) for half in range(2)]
        for half in range(2):
            nc.vector.tensor_copy(v1[half][:], tab1[:].bitcast(U32).indirect(idx[:, 32 * half: 32 * (half + 1)]))
        wr_sc = mid.tile([P, PASSES, N], U8, name="wr_sc", offset=24 * KB, align_bytes=ALIGN)
        for q in range(4):
            nc.sync.dma_start(wr_sc[32 * q: 32 * q + 4].bitcast(I32), wr_scales.bitcast(I32)[:, 4 * q: 4 * q + 4, :].rearrange("a r c -> r a c"))

        def frames(a, j0, width):
            if a == 0:
                return v0[:, j0: j0 + width].bitcast(FP8X4)
            return v1[j0 // HALF][:, j0 % HALF: j0 % HALF + width].bitcast(FP8X4)

        wf_codes = keep.tile([P, PASSES, H], U32, name="wf_codes", align_bytes=ALIGN)
        wf_sc = keep.tile([P, PASSES, H], U8, name="wf_sc", align_bytes=ALIGN)
        h_codes = keep.tile([P, S], U32, name="h_codes", align_bytes=ALIGN)
        h_sc = keep.tile([P, S], U8, name="h_sc", align_bytes=ALIGN)
        sig = keep.tile([P, 4, S], F32, name="sig")
        wo_sc = keep.tile([P, N], U8, name="wo_sc", align_bytes=ALIGN)
        wo_codes = []

        def gate(half):
            cols = slice(HALF * half, HALF * (half + 1))
            for t in range(4):
                b_ps = bank[4 * half + t]
                for a in range(PASSES):
                    nc.tensor.matmul_mx(b_ps[:], wg_codes[:, a, 256 * t: 256 * (t + 1)].bitcast(FP4X4),
                                        planes[:, a, S + P * t: S + P * (t + 1)], frames(a, HALF * half, HALF),
                                        planes[:, a, cols], start=(a == 0), stop=(a == PASSES - 1))
                nc.scalar.activation(sig[:, t, cols], b_ps[:], ACT.Sigmoid)

        def quantise_wf_first():
            wf_bf = [keep.tile([P, 2 * H], BF16, name="wf_bf0_%d" % w, align_bytes=ALIGN) for w in range(2)]
            for w in range(2):
                nc.vector.tensor_copy(wf_bf[w][:].rearrange("p (t g i j) -> p g j t i", t=2, i=2, j=4),
                                      wf_first[:].rearrange("p j (g t i) -> p g j t i", t=4, i=2)[:, :, :, 2 * w: 2 * w + 2])
            for w in range(2):
                cols = slice(2 * P * w, 2 * P * (w + 1))
                nc.vector.quantize_mx(wf_codes[:, 0, cols].bitcast(FP8X4), wf_sc[:, 0, cols], wf_bf[w][:])

        def quantise_wf_last():
            wf_bf = [keep.tile([P, 2, 2, H // 2], BF16, name="wf_bf1_%d" % w, align_bytes=ALIGN) for w in range(2)]
            for u in range(2):
                for w in range(2):
                    nc.vector.tensor_copy(wf_bf[w][:, :, u, :].rearrange("p t (g i j) -> p g j t i", i=2, j=4),
                                          wf_last[u][:].rearrange("p j (g t i) -> p g j t i", t=4, i=2)[:, :, :, 2 * w: 2 * w + 2])
            for w in range(2):
                cols = slice(2 * P * w, 2 * P * (w + 1))
                nc.vector.quantize_mx(wf_codes[:, 1, cols].bitcast(FP8X4), wf_sc[:, 1, cols], wf_bf[w][:].rearrange("p t u c -> p (t u c)"))

        def cast_wo(n, dst):
            src = wo_raw[:, :, P * n: P * (n + 1)]
            nc.scalar.copy(dst.rearrange("p (c i j) -> p c j i", i=4, j=4), src.rearrange("p j (c i) -> p c j i", i=4))

        def hidden(chunk):
            j0 = CHUNK * chunk
            cols = slice(j0, j0 + CHUNK)
            order = (0, 1) if chunk < EARLY_CHUNKS else (1, 0)
            a_ps = bank[chunk]
            for a in order:
                for t in range(4):
                    nc.tensor.matmul_mx(a_ps[:, CHUNK * t: CHUNK * (t + 1)], wf_codes[:, a, P * t: P * (t + 1)].bitcast(FP8X4),
                                        wf_sc[:, a, P * t: P * (t + 1)], frames(a, j0, CHUNK),
                                        planes[:, a, cols], start=(a == order[0] and t == 0), stop=(a == order[-1] and t == 3))
            th = stage.tile([P, 4 * CHUNK], F32, name="th%d" % chunk, tag="th%d" % chunk, align_bytes=ALIGN)
            nc.scalar.activation(th[:], a_ps[:], ACT.Tanh)
            nc.vector.tensor_tensor(h_bf[:, chunk, :].rearrange("p (c i t) -> p c t i", i=4, t=4),
                                    th[:].rearrange("p (t c i) -> p c t i", t=4, i=4),
                                    gated[chunk // CHUNKS][:, :, j0 % HALF: j0 % HALF + CHUNK].rearrange("p t (c i) -> p c t i", i=4), MULT)

        def quantise_h(chunk):
            cols = slice(CHUNK * chunk, CHUNK * (chunk + 2))
            nc.vector.quantize_mx(h_codes[:, cols].bitcast(FP8X4), h_sc[:, cols], h_bf[:, chunk: chunk + 2, :].rearrange("p c w -> p (c w)"))

        def project(n, half, y):
            cols = slice(HALF * half, HALF * (half + 1))
            out_rows = slice(P * n, P * (n + 1))
            y_ps = bank[2 * n + half]
            for a in range(PASSES):
                nc.tensor.matmul_mx(y_ps[:], wr_codes[:, a, out_rows].bitcast(FP8X4), wr_sc[:, a, out_rows],
                                    frames(a, HALF * half, HALF), planes[:, a, cols], start=(a == 0), stop=False)
            nc.tensor.matmul_mx(y_ps[:], wo_codes[n].bitcast(FP8X4), wo_sc[:, out_rows],
                                h_codes[:, cols].bitcast(FP8X4), h_sc[:, cols], start=False, stop=True)
            nc.scalar.copy(y, y_ps[:])

        def place(n, half, halves, y):
            nc.vector.tensor_tensor(window[n % 2][:].indirect(idx2[:, 32 * half: 32 * (half + halves)]),
                                    y, wgo_sb[:, HALF * half: HALF * (half + halves)], MULT)
            if half + halves == 2:
                nc.sync.dma_start(out[P * n: P * (n + 1), :], window[n % 2][:])

        h_bf = keep.tile([P, 2 * CHUNKS, 4 * CHUNK], BF16, name="h_bf", align_bytes=ALIGN)
        for c0 in range(0, T, CLEAR):
            nc.vector.memset(window[0][:, c0: c0 + CLEAR].bitcast(I32), 0)
        for moving in [frames(0, 0, HALF)] * WARM_EARLY + [tab1[:, 0:HALF].bitcast(FP8X4)] * WARM_LATE:
            nc.tensor.matmul_mx(bank[7][:], wg_codes[:, 0, 0:256].bitcast(FP4X4), rows[:, S: S + P], moving, rows[:, 0:HALF],
                                start=True, stop=True)
        gate(0)
        gate(1)
        quantise_wf_first()
        wgo_sb = mid.tile([P, S], F32, name="wgo_sb", offset=0)
        nc.sync.dma_start(wgo_sb[:], wgo)
        idx2 = lists.tile([P, S // 16], U16, name="idx2")
        nc.sync.dma_start(idx2[:], offs2)
        quantise_wf_last()

        gated = [mid.tile([P, 4, HALF], F32, name="gated%d" % half, offset=(12 - 8 * half) * KB) for half in range(2)]
        for tile_no in range(8):
            half, t = divmod(tile_no, 4)
            src = sig[:, t, HALF * half: HALF * (half + 1)]
            if tile_no < VECTOR_GAINS:
                nc.vector.tensor_scalar(gated[half][:, t, :], src, gain_sb[:, 2 * t: 2 * t + 1], None, MULT)
            else:
                nc.scalar.activation(gated[half][:, t, :], src, ACT.Copy, scale=gain_sb[:, 2 * t: 2 * t + 1])

        hidden(0)
        hidden(1)
        hidden(2)
        quantise_h(0)
        hidden(3)
        hidden(4)
        quantise_h(2)
        hidden(5)
        wo_bf0 = stage.tile([P, 4 * P], BF16, name="wo_bf0", tag="th1", align_bytes=ALIGN)
        cast_wo(0, wo_bf0[:])
        wo_first = keep.tile([P, P], U32, name="wo_first", align_bytes=ALIGN)
        wo_codes.append(wo_first[:])
        nc.vector.quantize_mx(wo_codes[0].bitcast(FP8X4), wo_sc[:, 0:P], wo_bf0[:])
        hidden(6)
        hidden(7)
        quantise_h(4)
        quantise_h(6)

        y00 = stage.tile([P, HALF], F32, name="y00", tag="y00", align_bytes=ALIGN)
        project(0, 0, y00[:])
        place(0, 0, 1, y00[:])
        y01 = keep.tile([P, HALF], F32, name="y01")
        project(0, 1, y01[:])
        wo_bf = stage.tile([P, 3 * 4 * P], BF16, name="wo_bf", tag="th7", align_bytes=ALIGN)
        wo_rest = keep.tile([P, 3 * P], U32, name="wo_rest", align_bytes=ALIGN)
        for n in range(1, 4):
            cast_wo(n, wo_bf[:, 4 * P * (n - 1): 4 * P * n])
            wo_codes.append(wo_rest[:, P * (n - 1): P * n])
        nc.vector.quantize_mx(wo_rest[:, 0:P].bitcast(FP8X4), wo_sc[:, P: 2 * P], wo_bf[:, 0: 4 * P])
        nc.vector.quantize_mx(wo_rest[:, P:].bitcast(FP8X4), wo_sc[:, 2 * P:], wo_bf[:, 4 * P:])
        place(0, 1, 1, y01[:])
        for n in range(1, 4):
            y = keep.tile([P, S], F32, name="y%d" % n)
            for half in range(2):
                project(n, half, y[:, HALF * half: HALF * (half + 1)])
            place(n, 0, 2, y[:])
